import numpy as np
import ml_dtypes


def mxq(x, axis, fmt="e4m3"):
    dtype, down = {"e4m3": (ml_dtypes.float8_e4m3fn, 7), "e5m2": (ml_dtypes.float8_e5m2, 14)}[fmt]
    v = np.moveaxis(np.asarray(x, np.float32).astype(ml_dtypes.bfloat16).astype(np.float64), axis, -1)
    blocks = v.reshape(v.shape[:-1] + (-1, 32))
    amax = np.abs(blocks).max(-1, keepdims=True)
    byte = np.maximum(np.where(amax > 0, np.frexp(amax)[1] - 1 + 127, 0) - down, 1)
    scale = np.exp2(byte - 127.0)
    codes = (blocks / scale).astype(np.float32).astype(dtype).astype(np.float64)
    return np.moveaxis((codes * scale).reshape(v.shape), -1, axis)


WIDE = False


def mx_kscale(k):
    if not WIDE:
        return np.ones(k)
    levels = np.array([10, -10, 5, -5, 0])
    if k % 512:
        return np.exp2(np.random.permutation(np.resize(levels, k // 32))).repeat(32)
    a = np.empty((k // 512, 16))
    for p in range(k // 512):
        a[p, :8] = np.random.permutation(np.resize(levels, 8))
        for g in range(8):
            far = levels[np.abs(levels - a[p, g]) >= 10]
            a[p, g + 8] = far[np.random.randint(len(far))]
    return np.exp2(a.ravel()).repeat(32)


def f64(x):
    return np.asarray(x).astype(np.float64)


def striped(idx):
    return np.tile(idx.reshape(-1, 16).T, (8, 1)).astype(np.uint16)


def unstriped(offs):
    return offs[:16].T.reshape(-1).astype(np.int64)


E2M1 = np.array([0.0, 0.5, 1.0, 1.5, 2.0, 3.0, 4.0, 6.0, -0.0, -0.5, -1.0, -1.5, -2.0, -3.0, -4.0, -6.0])


def pack_weight(w, fmt):
    k, n = w.shape
    w = f64(np.asarray(w, np.float32).astype(ml_dtypes.bfloat16)).reshape(k // 32, 32, n)
    amax = np.abs(w).max(1)
    if fmt == "e4m3":
        byte = np.frexp(amax)[1] - 1 + 127 - 7
    else:
        mant, ex = np.frexp(amax / 6.0)
        byte = np.where(mant > 0.5, ex, ex - 1) + 127
    byte = np.clip(np.where(amax > 0, byte, 1), 1, 254)
    scaled = (w * np.exp2(127.0 - byte)[:, None, :]).reshape(k, n).astype(np.float32)
    by_word = np.ascontiguousarray(scaled.reshape(k // 512, 128, 4, n).transpose(0, 1, 3, 2))
    if fmt == "e4m3":
        words = by_word.astype(ml_dtypes.float8_e4m3fn).view(np.uint8)
    else:
        c = by_word.astype(ml_dtypes.float4_e2m1fn).view(np.uint8) & 0xF
        words = (c[..., 0::2] | (c[..., 1::2] << 4)).reshape(k // 512, 128, 2 * n)
    return np.ascontiguousarray(words), np.ascontiguousarray(byte.astype(np.uint8).reshape(k // 512, 16, n))


def unpack_weight(words, scales, fmt):
    g, _, n = scales.shape
    words = np.ascontiguousarray(words).reshape(g, 128, n, -1)
    if fmt == "e4m3":
        vals = words.view(ml_dtypes.float8_e4m3fn).astype(np.float64)
    else:
        nib = np.empty((g, 128, n, 4), np.uint8)
        nib[..., 0::2] = words & 0xF
        nib[..., 1::2] = words >> 4
        vals = E2M1[nib]
    vals = vals * np.repeat(np.exp2(scales.astype(np.float64) - 127.0), 8, axis=1)[..., None]
    return vals.transpose(0, 1, 3, 2).reshape(g * 512, n)


def gelu(v):
    return 0.5 * v * (1.0 + np.tanh(np.sqrt(2.0 / np.pi) * (v + 0.044715 * v**3)))


K, H, N, T, S, T2, P = 1024, 1024, 512, 4096, 1024, 2048, 1024

def setup_inputs():
    n = np.random.standard_normal
    s = mx_kscale(K)[:, None]
    u = mx_kscale(H)[:, None]
    tab_words, tab_scales = pack_weight(n((K, T)) * s, "e4m3")
    w4_words, w4_scales = pack_weight(n((H, N)) / np.sqrt(H) / u, "e2m1")
    return {
        "tab_words": tab_words, "tab_scales": tab_scales,
        "offs": striped(np.random.permutation(T)[:S]),
        "w1": (n((K, H)) / np.sqrt(K) / s * u.T).astype(np.float32),
        "lo": (-np.exp(0.3 * n(H)) * u[:, 0]).astype(np.float32),
        "hi": (np.exp(0.3 * n(H)) * u[:, 0]).astype(np.float32),
        "offs2": striped(np.random.permutation(T2)[:S]),
        "wgs": np.exp(0.3 * n((128, S))).astype(np.float32),
        "stored": (n((H, T2)) * u).astype(np.float32),
        "w4_words": w4_words, "w4_scales": w4_scales,
        "offs3": striped(np.random.permutation(T2)[:P]),
        "gain": np.exp(0.3 * n(N)).astype(np.float32),
        "duty": n((N, P)).astype(np.float32),
        "offs4": striped(np.random.permutation(T2)[:P]),
        "wgo": np.exp(0.3 * n((128, P))).astype(np.float32),
    }

def reference(tab_words, tab_scales, offs, w1, lo, hi, offs2, wgs, stored, w4_words, w4_scales, offs3, gain, duty, offs4, wgo):
    v = unpack_weight(tab_words, tab_scales, "e4m3")[:, unstriped(offs)]
    d = mxq(f64(w1), 0, "e4m3").T @ v
    h = np.minimum(np.maximum(d, f64(lo)[:, None]), f64(hi)[:, None])
    page = np.zeros((H, T2))
    page[:, unstriped(offs2)] = np.tile(f64(wgs), (H // 128, 1)) * h
    z = page + f64(stored)
    w4 = unpack_weight(w4_words, w4_scales, "e2m1")
    y = w4.T @ mxq(z, 0, "e4m3")
    x = y[:, unstriped(offs3)]
    x = x * f64(gain)[:, None] + f64(duty)
    out = np.zeros((N, T2))
    out[:, unstriped(offs4)] = np.tile(f64(wgo), (N // 128, 1)) * x
    return out

@@ -1,0 +1,328 @@
+from contextlib import ExitStack
+
+import concourse.mybir as mybir
+from concourse.masks import make_identity
+
+K, H, N, T, S, T2, PICK = 1024, 1024, 512, 4096, 1024, 2048, 1024
+FLOPS = 2 * K * H * S + 2 * H * N * T2
+
+F32 = mybir.dt.float32
+BF16 = mybir.dt.bfloat16
+I32 = mybir.dt.int32
+U32 = mybir.dt.uint32
+U16 = mybir.dt.uint16
+U8 = mybir.dt.uint8
+FP8X4 = mybir.dt.float8_e4m3fn_x4
+FP4X4 = mybir.dt.float4_e2m1fn_x4
+ALU = mybir.AluOpType
+COPY = mybir.ActivationFunctionType.Copy
+
+P = 128
+PASSES = 2
+BANK = 512
+R_TILES = H // P
+N_TILES = N // P
+QUARTERS = T2 // BANK
+W1_CHUNKS = [(0,), (1, 2), (3, 4), (5, 6), (7,)]
+PAGES = 3
+OUTS = 2
+
+
+def tile_list_eclipse_shed_planner_kernel(
+    tc, tab_words, tab_scales, offs, w1, lo, hi, offs2, wgs, stored, w4_words, w4_scales, offs3, gain, duty, offs4, wgo, out
+):
+    nc = tc.nc
+    with ExitStack() as ctx:
+        keep = ctx.enter_context(tc.tile_pool(name="keep", bufs=1))
+        ring = ctx.enter_context(tc.tile_pool(name="ring", bufs=2))
+        psum = ctx.enter_context(tc.psum_pool(name="psum", bufs=2))
+
+        tab_plane = keep.tile([P, T], U8, name="tab_plane", tag="plane", align_bytes=64)
+        nc.vector.memset(tab_plane[:].bitcast(I32), 0)
+        rows = keep.tile([P, P], F32, name="rows")
+        nc.gpsimd.memset(rows[:], 0.0)
+        ident = keep.tile([P, P], F32, name="ident")
+        make_identity(nc, ident[:])
+        w4_plane = keep.tile([P, PASSES, N], U8, name="w4_plane", align_bytes=64)
+        nc.vector.memset(w4_plane[:].bitcast(I32), 0)
+        pages = [keep.tile([P, T2], F32, name=f"page{b}") for b in range(PAGES - 1)]
+        for page in pages:
+            nc.vector.memset(page[:], 0.0)
+
+        def load_list(src, name):
+            tile = keep.tile([P, S // 16], U16, name=name)
+            nc.sync.dma_start(tile[:], src)
+            return tile
+
+        def load_table(a):
+            tile = keep.tile([P, T], I32, name=f"words{a}", tag=f"wide{a}", align_bytes=64)
+            nc.sync.dma_start(tile[:], tab_words[a].rearrange("p t i -> p (t i)").bitcast(I32))
+            return tile
+
+        w1_codes = {}
+        w1_scales = {}
+        w1_raw = {}
+
+        def load_w1(chunk):
+            tiles = W1_CHUNKS[chunk]
+            c0, width = P * tiles[0], P * len(tiles)
+            if len(tiles) == 1:
+                both = ring.tile([P, PASSES, 4, P], F32, name=f"w1raw{chunk}", tag="raw", bufs=8)
+            for a in range(PASSES):
+                if len(tiles) == 1:
+                    raw = both[:, a, :, :]
+                else:
+                    wide = ring.tile([P, 4, width], F32, name=f"w1raw{chunk}_{a}", tag="raw", bufs=8)
+                    raw = wide[:]
+                nc.sync.dma_start(raw, w1[512 * a : 512 * (a + 1), c0 : c0 + width].rearrange("(p i) c -> p i c", i=4))
+                for place, j in enumerate(tiles):
+                    w1_raw[j, a] = raw[:, :, P * place : P * (place + 1)]
+
+        w1_grouped = {}
+
+        def round_w1(j):
+            grouped = ring.tile([P, PASSES * P * 4], BF16, name=f"w1g{j}", tag="w1g", bufs=3, align_bytes=64)
+            w1_grouped[j] = grouped
+            for a in range(PASSES):
+                nc.scalar.copy(
+                    grouped[:, 4 * P * a : 4 * P * (a + 1)].rearrange("p (c i) -> p c i", i=4), w1_raw[j, a].rearrange("p i c -> p c i")
+                )
+
+        def quantise_w1(tiles, tag):
+            codes = keep.tile([P, len(tiles) * PASSES * P], U32, name=f"w1c{tiles[0]}", tag=tag, align_bytes=64)
+            for place, j in enumerate(tiles):
+                scales = keep.tile([P, PASSES * P], U8, name=f"w1s{j}", align_bytes=64)
+                mine = codes[:, PASSES * P * place : PASSES * P * (place + 1)]
+                nc.vector.quantize_mx(out=mine.bitcast(FP8X4), scales=scales[:], in_=w1_grouped[j][:])
+                for a in range(PASSES):
+                    w1_codes[j, a] = mine[:, P * a : P * (a + 1)]
+                    w1_scales[j, a] = scales[:, P * a : P * (a + 1)]
+
+        idx = load_list(offs, "idx")
+        scale_rows = ring.tile([P, T // 4], I32, name="scale_rows", tag="h", bufs=6)
+        for quad in range(4):
+            nc.sync.dma_start(scale_rows[32 * quad : 32 * quad + 8, :], tab_scales[:, 4 * quad : 4 * quad + 4, :].bitcast(I32))
+        for quad in range(4):
+            nc.vector.tensor_copy(tab_plane[32 * quad : 32 * quad + 8, :].bitcast(I32), scale_rows[32 * quad : 32 * quad + 8, :])
+        words0 = load_table(0)
+        load_w1(0)
+        vectors = keep.tile([20, P], F32, name="vectors")
+        nc.sync.dma_start(vectors[0:8, :], lo.rearrange("(j p) -> j p", p=P))
+        nc.sync.dma_start(vectors[8:16, :], hi.rearrange("(j p) -> j p", p=P))
+        nc.sync.dma_start(vectors[16:20, :], gain.rearrange("(j p) -> j p", p=P))
+        nc.scalar.copy(rows[0:20, :], vectors[:])
+        words1 = load_table(1)
+        idx2 = load_list(offs2, "idx2")
+        wgs_sb = keep.tile([P, S], F32, name="wgs_sb")
+        nc.sync.dma_start(wgs_sb[:], wgs)
+
+        stored_sb = {}
+
+        def load_stored(j):
+            tile = ring.tile([P, T2], F32, name=f"stored{j}", tag="stored", bufs=2)
+            nc.sync.dma_start(tile[:], stored[P * j : P * (j + 1), :])
+            stored_sb[j] = tile
+
+        turned = psum.tile([P, P], F32, name="turned", tag="back", bufs=2)
+        nc.tensor.transpose(turned[:], rows[:], ident[:])
+        cols = keep.tile([P, 20], F32, name="cols")
+        nc.scalar.copy(cols[:], turned[:, 0:20])
+
+        round_w1(0)
+        quantise_w1((0,), "w1c0")
+
+        v_codes = [keep.tile([P, S], U32, name=f"v_codes{a}", align_bytes=64) for a in range(PASSES)]
+        v_plane = keep.tile([P, S], U8, name="v_plane", align_bytes=64)
+        nc.vector.tensor_copy(v_plane[:], tab_plane[:].indirect(idx[:]))
+        nc.vector.tensor_copy(v_codes[0][:], words0[:].bitcast(U32).indirect(idx[:]))
+        pages.append(keep.tile([P, T2], F32, name="page_late", tag="wide0", align_bytes=64))
+        nc.gpsimd.memset(pages[-1][:], 0.0)
+        for half in range(2):
+            span = slice(BANK * half, BANK * (half + 1))
+            listed = idx[:, 32 * half : 32 * (half + 1)]
+            nc.vector.tensor_copy(v_codes[1][:, span], words1[:].bitcast(U32).indirect(listed))
+
+        h_sb = {}
+
+        def first_product(j):
+            if j == 0:
+                h = [keep.tile([P, BANK], F32, name=f"h0_{half}", tag=f"first{half}", align_bytes=64) for half in range(2)]
+            elif j == 1:
+                h = keep.tile([P, S], F32, name="h1", tag="second", align_bytes=64)
+            else:
+                h = ring.tile([P, S], F32, name=f"h{j}", tag="h", bufs=6)
+            h_sb[j] = h
+            lo_col, hi_col = cols[:, j : j + 1], cols[:, 8 + j : 9 + j]
+            for half in range(2):
+                span = slice(BANK * half, BANK * (half + 1))
+                acc = psum.tile([P, BANK], F32, name=f"dacc{j}_{half}", tag="acc", bufs=2)
+                for a in range(PASSES):
+                    nc.tensor.matmul_mx(
+                        out=acc[:],
+                        lhsT=w1_codes[j, a].bitcast(FP8X4),
+                        lhsT_scale=w1_scales[j, a],
+                        rhs=v_codes[a][:, span].bitcast(FP8X4),
+                        rhs_scale=v_plane[4 * a : P, span],
+                        start=(a == 0),
+                        stop=(a == PASSES - 1),
+                    )
+                if j == 0:
+                    nc.vector.tensor_scalar(h[half][:], acc[:], lo_col, hi_col, ALU.max, ALU.min)
+                else:
+                    nc.scalar.copy(h[:, span], acc[:])
+            if j > 0:
+                nc.vector.tensor_scalar(h[:], h[:], lo_col, hi_col, ALU.max, ALU.min)
+
+        def scatter_page(j):
+            page = pages[j % PAGES]
+            if j == 0:
+                for half in range(2):
+                    span = slice(BANK * half, BANK * (half + 1))
+                    nc.vector.tensor_tensor(
+                        page[:].indirect(idx2[:, 32 * half : 32 * (half + 1)]), h_sb[j][half][:], wgs_sb[:, span], ALU.mult
+                    )
+            else:
+                nc.vector.tensor_tensor(page[:].indirect(idx2[:]), h_sb[j][:], wgs_sb[:], ALU.mult)
+
+        sums = {}
+        z_turned = {}
+
+        def turn_stored(j):
+            for q in range(QUARTERS):
+                bank = psum.tile([P, 4, P], F32, name=f"sum{j}_{q}", tag="sum", bufs=4)
+                sums[j, q] = bank
+                for tt in range(4):
+                    t0 = BANK * q + P * tt
+                    nc.tensor.matmul(bank[:, tt, :], stored_sb[j][:, t0 : t0 + P], ident[:], start=(tt == 0), stop=False, is_transpose=True)
+
+        def add_page(j, q):
+            a, jj = divmod(j, 4)
+            bank = sums[j, q]
+            for tt in range(4):
+                t0 = BANK * q + P * tt
+                nc.tensor.matmul(bank[:, tt, :], pages[j % PAGES][:, t0 : t0 + P], ident[:], start=False, stop=(tt == 3), is_transpose=True)
+            if jj == 0:
+                z_turned[a, q] = ring.tile([P, 4, 2, P, 2], BF16, name=f"zt{a}_{q}", tag="zt", bufs=6)
+            dst = z_turned[a, q][:, :, :, 32 * jj : 32 * (jj + 1), :]
+            src = bank[:].rearrange("t s (p u e) -> t s u p e", u=2, e=2)
+            if j == R_TILES - 1:
+                nc.vector.tensor_copy(dst, src)
+            else:
+                nc.scalar.copy(dst, src)
+
+        z_codes = {}
+        z_scales = {}
+
+        def quantise_z(a, q):
+            codes = keep.tile([P, BANK], U32, name=f"zc{a}_{q}", align_bytes=64)
+            scales = keep.tile([P, BANK], U8, name=f"zs{a}_{q}", align_bytes=64)
+            z_codes[a, q], z_scales[a, q] = codes, scales
+            pairs = z_turned[a, q][:].rearrange("t s u p e -> t (s u p e)").bitcast(F32).rearrange("t (s u p) -> t s u p", s=4, u=2)
+            for half in range(2):
+                bank = psum.tile([P, 2, 256], F32, name=f"back{a}_{q}_{half}", tag="back", bufs=2)
+                for s in range(2):
+                    for u in range(2):
+                        nc.tensor.transpose(bank[:, u, P * s : P * (s + 1)], pairs[:, 2 * half + s, u, :], ident[:])
+                grouped = ring.tile([P, 1024], BF16, name=f"zg{a}_{q}_{half}", tag="grouped", bufs=8, align_bytes=64)
+                nc.scalar.copy(grouped[:].bitcast(F32).rearrange("p (t u) -> p t u", u=2), bank[:].rearrange("p u t -> p t u"))
+                span = slice(256 * half, 256 * (half + 1))
+                nc.vector.quantize_mx(out=codes[:, span].bitcast(FP8X4), scales=scales[:, span], in_=grouped[:])
+
+        y_sb = {}
+
+        def second_product(n, q):
+            if q == 0:
+                y_sb[n] = keep.tile([P, T2], F32, name=f"y{n}", tag=f"wide{n % 2}", align_bytes=64)
+            acc = psum.tile([P, BANK], F32, name=f"yacc{n}_{q}", tag="acc", bufs=2)
+            for a in range(PASSES):
+                nc.tensor.matmul_mx(
+                    out=acc[:],
+                    lhsT=w4_sb[:, a, 2 * P * n : 2 * P * (n + 1)].bitcast(FP4X4),
+                    lhsT_scale=w4_plane[:, a, P * n : P * (n + 1)],
+                    rhs=z_codes[a, q][:].bitcast(FP8X4),
+                    rhs_scale=z_scales[a, q][:],
+                    start=(a == 0),
+                    stop=(a == PASSES - 1),
+                )
+            dst = y_sb[n][:, BANK * q : BANK * (q + 1)]
+            gain_col = cols[:, 16 + n : 17 + n]
+            if n == 0 and q % 2 == 1:
+                nc.vector.tensor_scalar(dst, acc[:], gain_col, None, ALU.mult)
+            else:
+                nc.scalar.activation(dst, acc[:], COPY, scale=gain_col)
+
+        load_w1(1)
+        load_w1(2)
+        load_stored(0)
+        load_w1(3)
+        load_w1(4)
+        load_stored(1)
+        first_product(0)
+        scatter_page(0)
+        round_w1(1)
+        quantise_w1((1,), "wide1")
+        first_product(1)
+        round_w1(2)
+        round_w1(3)
+        quantise_w1((2, 3), "first0")
+        round_w1(4)
+        quantise_w1((4,), "first1")
+        for j in range(2, 5):
+            first_product(j)
+        for j in range(5, R_TILES):
+            round_w1(j)
+
+        w4_sb = keep.tile([P, PASSES, 2 * N], U8, name="w4_sb", align_bytes=64)
+        nc.sync.dma_start(w4_sb[:].bitcast(I32), w4_words.rearrange("a p c -> p a c").bitcast(I32))
+        for quad in range(4):
+            nc.sync.dma_start(
+                w4_plane[32 * quad : 32 * quad + 4, :, :].bitcast(I32),
+                w4_scales[:, 4 * quad : 4 * quad + 4, :].rearrange("a r c -> r a c").bitcast(I32),
+            )
+        idx3 = load_list(offs3, "idx3")
+        idx4 = load_list(offs4, "idx4")
+        wgo_sb = keep.tile([P, PICK], F32, name="wgo_sb", tag="plane", align_bytes=64)
+        nc.sync.dma_start(wgo_sb[:], wgo)
+
+        duty_sb = {}
+        for j in range(R_TILES):
+            turn_stored(j)
+            if j > 0:
+                scatter_page(j)
+            if j == 1:
+                quantise_w1((5, 6, 7), "second")
+                for m in range(5, R_TILES):
+                    first_product(m)
+            if j + 2 < R_TILES:
+                load_stored(j + 2)
+            if j >= 4:
+                duty_sb[j - 4] = ring.tile([P, PICK], F32, name=f"duty{j - 4}", tag="raw", bufs=8)
+                nc.sync.dma_start(duty_sb[j - 4][:], duty[P * (j - 4) : P * (j - 3), :])
+            if j < R_TILES - 1:
+                for q in range(QUARTERS):
+                    add_page(j, q)
+            if j == 3:
+                for q in range(QUARTERS):
+                    quantise_z(0, q)
+
+        outs = [ring.tile([P, T2], F32, name=f"outpage{b}", tag="stored", bufs=2) for b in range(OUTS)]
+        for page in outs:
+            nc.gpsimd.memset(page[:], 0.0)
+        last = R_TILES - 1
+        for step in range(QUARTERS + 2):
+            if step < QUARTERS:
+                add_page(last, step)
+            if 1 <= step <= QUARTERS:
+                quantise_z(1, step - 1)
+            if step >= 2:
+                second_product(0, step - 2)
+
+        for n in range(N_TILES):
+            if n + 1 < N_TILES:
+                for q in range(QUARTERS):
+                    second_product(n + 1, q)
+            x = ring.tile([P, PICK], F32, name=f"x{n}", tag="h", bufs=6)
+            nc.vector.tensor_tensor(x[:], y_sb[n][:].indirect(idx3[:]), duty_sb[n][:], ALU.add)
+            page = outs[n % OUTS]
+            nc.vector.tensor_tensor(page[:].indirect(idx4[:]), x[:], wgo_sb[:], ALU.mult)
+            nc.sync.dma_start(out[P * n : P * (n + 1), :], page[:])

@@ -24,6 +24,7 @@ R_TILES = H // P
 N_TILES = N // P
 QUARTERS = T2 // BANK
 W1_CHUNKS = [(0,), (1, 2), (3, 4), (5, 6), (7,)]
+LAST_SPLIT = 768
 PAGES = 3
 OUTS = 2
 
@@ -99,7 +100,7 @@ def tile_list_eclipse_shed_planner_kernel(
                     w1_scales[j, a] = scales[:, P * a : P * (a + 1)]
 
         idx = load_list(offs, "idx")
-        scale_rows = ring.tile([P, T // 4], I32, name="scale_rows", tag="h", bufs=6)
+        scale_rows = ring.tile([P, T // 4], I32, name="scale_rows", tag="h", bufs=5)
         for quad in range(4):
             nc.sync.dma_start(scale_rows[32 * quad : 32 * quad + 8, :], tab_scales[:, 4 * quad : 4 * quad + 4, :].bitcast(I32))
         for quad in range(4):
@@ -142,17 +143,24 @@ def tile_list_eclipse_shed_planner_kernel(
             listed = idx[:, 32 * half : 32 * (half + 1)]
             nc.vector.tensor_copy(v_codes[1][:, span], words1[:].bitcast(U32).indirect(listed))
 
+        last = R_TILES - 1
         h_sb = {}
 
-        def first_product(j):
+        def pieces(j):
             if j == 0:
-                h = [keep.tile([P, BANK], F32, name=f"h0_{half}", tag=f"first{half}", align_bytes=64) for half in range(2)]
-            elif j == 1:
-                h = keep.tile([P, S], F32, name="h1", tag="second", align_bytes=64)
-            else:
-                h = ring.tile([P, S], F32, name=f"h{j}", tag="h", bufs=6)
-            h_sb[j] = h
+                return [(0, BANK, "first0"), (BANK, S, "first1")]
+            if j == last:
+                return [(0, LAST_SPLIT, "last0"), (LAST_SPLIT, S, "unclamped")]
+            return [(0, S, "second" if j == 1 else "h")]
+
+        def first_product(j):
             lo_col, hi_col = cols[:, j : j + 1], cols[:, 8 + j : 9 + j]
+            h_sb[j] = []
+            for c0, c1, tag in pieces(j):
+                if tag == "h":
+                    h_sb[j].append(ring.tile([P, c1 - c0], F32, name=f"h{j}", tag="h", bufs=5))
+                else:
+                    h_sb[j].append(keep.tile([P, c1 - c0], F32, name=f"h{j}_{c0}", tag=tag, align_bytes=64))
             for half in range(2):
                 span = slice(BANK * half, BANK * (half + 1))
                 acc = psum.tile([P, BANK], F32, name=f"dacc{j}_{half}", tag="acc", bufs=2)
@@ -167,22 +175,24 @@ def tile_list_eclipse_shed_planner_kernel(
                         stop=(a == PASSES - 1),
                     )
                 if j == 0:
-                    nc.vector.tensor_scalar(h[half][:], acc[:], lo_col, hi_col, ALU.max, ALU.min)
+                    nc.vector.tensor_scalar(h_sb[j][half][:], acc[:], lo_col, hi_col, ALU.max, ALU.min)
                 else:
-                    nc.scalar.copy(h[:, span], acc[:])
+                    for h, (c0, c1, tag) in zip(h_sb[j], pieces(j)):
+                        begin, end = max(c0, span.start), min(c1, span.stop)
+                        if begin < end:
+                            nc.scalar.copy(h[:, begin - c0 : end - c0], acc[:, begin - span.start : end - span.start])
             if j > 0:
-                nc.vector.tensor_scalar(h[:], h[:], lo_col, hi_col, ALU.max, ALU.min)
+                nc.vector.tensor_scalar(h_sb[j][0][:], h_sb[j][0][:], lo_col, hi_col, ALU.max, ALU.min)
 
-        def scatter_page(j):
-            page = pages[j % PAGES]
-            if j == 0:
-                for half in range(2):
-                    span = slice(BANK * half, BANK * (half + 1))
-                    nc.vector.tensor_tensor(
-                        page[:].indirect(idx2[:, 32 * half : 32 * (half + 1)]), h_sb[j][half][:], wgs_sb[:, span], ALU.mult
-                    )
-            else:
-                nc.vector.tensor_tensor(page[:].indirect(idx2[:]), h_sb[j][:], wgs_sb[:], ALU.mult)
+        def clamp_last_piece():
+            h = keep.tile([P, S - LAST_SPLIT], F32, name="h_end", tag="hold", align_bytes=64)
+            nc.vector.tensor_scalar(h[:], h_sb[last][1][:], cols[:, last : last + 1], cols[:, 8 + last : 9 + last], ALU.max, ALU.min)
+            h_sb[last][1] = h
+
+        def scatter_page(j, piece):
+            c0, c1, tag = pieces(j)[piece]
+            window = pages[j % PAGES][:].indirect(idx2[:, c0 // 16 : c1 // 16])
+            nc.vector.tensor_tensor(window, h_sb[j][piece][:], wgs_sb[:, c0:c1], ALU.mult)
 
         sums = {}
         z_turned = {}
@@ -205,7 +215,7 @@ def tile_list_eclipse_shed_planner_kernel(
                 z_turned[a, q] = ring.tile([P, 4, 2, P, 2], BF16, name=f"zt{a}_{q}", tag="zt", bufs=6)
             dst = z_turned[a, q][:, :, :, 32 * jj : 32 * (jj + 1), :]
             src = bank[:].rearrange("t s (p u e) -> t s u p e", u=2, e=2)
-            if j == R_TILES - 1:
+            if j == last and q >= 2:
                 nc.vector.tensor_copy(dst, src)
             else:
                 nc.scalar.copy(dst, src)
@@ -213,43 +223,61 @@ def tile_list_eclipse_shed_planner_kernel(
         z_codes = {}
         z_scales = {}
 
-        def quantise_z(a, q):
-            codes = keep.tile([P, BANK], U32, name=f"zc{a}_{q}", align_bytes=64)
-            scales = keep.tile([P, BANK], U8, name=f"zs{a}_{q}", align_bytes=64)
-            z_codes[a, q], z_scales[a, q] = codes, scales
+        z_grouped = {}
+
+        def turn_back(a, q):
             pairs = z_turned[a, q][:].rearrange("t s u p e -> t (s u p e)").bitcast(F32).rearrange("t (s u p) -> t s u p", s=4, u=2)
             for half in range(2):
                 bank = psum.tile([P, 2, 256], F32, name=f"back{a}_{q}_{half}", tag="back", bufs=2)
                 for s in range(2):
                     for u in range(2):
                         nc.tensor.transpose(bank[:, u, P * s : P * (s + 1)], pairs[:, 2 * half + s, u, :], ident[:])
-                grouped = ring.tile([P, 1024], BF16, name=f"zg{a}_{q}_{half}", tag="grouped", bufs=8, align_bytes=64)
+                if (a, q, half) == (0, 1, 1):
+                    grouped = keep.tile([P, 1024], BF16, name="zg_hold", tag="hold", align_bytes=64)
+                else:
+                    grouped = ring.tile([P, 1024], BF16, name=f"zg{a}_{q}_{half}", tag="grouped", bufs=11, align_bytes=64)
                 nc.scalar.copy(grouped[:].bitcast(F32).rearrange("p (t u) -> p t u", u=2), bank[:].rearrange("p u t -> p t u"))
-                span = slice(256 * half, 256 * (half + 1))
-                nc.vector.quantize_mx(out=codes[:, span].bitcast(FP8X4), scales=scales[:, span], in_=grouped[:])
+                z_grouped[a, q, half] = grouped
+
+        def quantise_z(a, quarters, tag):
+            codes = keep.tile([P, BANK * len(quarters)], U32, name=f"zc{a}_{quarters[0]}", tag=tag, align_bytes=64)
+            for place, q in enumerate(quarters):
+                scales = keep.tile([P, BANK], U8, name=f"zs{a}_{q}", align_bytes=64)
+                z_codes[a, q], z_scales[a, q] = codes[:, BANK * place : BANK * (place + 1)], scales
+                for half in range(2):
+                    span = slice(256 * half, 256 * (half + 1))
+                    nc.vector.quantize_mx(
+                        out=z_codes[a, q][:, span].bitcast(FP8X4), scales=scales[:, span], in_=z_grouped[a, q, half][:]
+                    )
 
         y_sb = {}
+        y_acc = {}
 
-        def second_product(n, q):
+        def second_pass(n, q, a):
+            if a == 0:
+                if (QUARTERS * n + q) % 6 < 2:
+                    y_acc[n, q] = psum.tile([P, BANK], F32, name=f"yacc{n}_{q}", tag="acc", bufs=2)
+                else:
+                    y_acc[n, q] = psum.tile([P, BANK], F32, name=f"yacc{n}_{q}", tag="sum", bufs=4)
+            nc.tensor.matmul_mx(
+                out=y_acc[n, q][:],
+                lhsT=w4_sb[:, a, 2 * P * n : 2 * P * (n + 1)].bitcast(FP4X4),
+                lhsT_scale=w4_plane[:, a, P * n : P * (n + 1)],
+                rhs=z_codes[a, q].bitcast(FP8X4),
+                rhs_scale=z_scales[a, q][:],
+                start=(a == 0),
+                stop=(a == PASSES - 1),
+            )
+
+        def fetch_scores(n, q):
             if q == 0:
                 y_sb[n] = keep.tile([P, T2], F32, name=f"y{n}", tag=f"wide{n % 2}", align_bytes=64)
-            acc = psum.tile([P, BANK], F32, name=f"yacc{n}_{q}", tag="acc", bufs=2)
-            for a in range(PASSES):
-                nc.tensor.matmul_mx(
-                    out=acc[:],
-                    lhsT=w4_sb[:, a, 2 * P * n : 2 * P * (n + 1)].bitcast(FP4X4),
-                    lhsT_scale=w4_plane[:, a, P * n : P * (n + 1)],
-                    rhs=z_codes[a, q][:].bitcast(FP8X4),
-                    rhs_scale=z_scales[a, q][:],
-                    start=(a == 0),
-                    stop=(a == PASSES - 1),
-                )
             dst = y_sb[n][:, BANK * q : BANK * (q + 1)]
             gain_col = cols[:, 16 + n : 17 + n]
             if n == 0 and q % 2 == 1:
-                nc.vector.tensor_scalar(dst, acc[:], gain_col, None, ALU.mult)
+                nc.vector.tensor_scalar(dst, y_acc[n, q][:], gain_col, None, ALU.mult)
             else:
-                nc.scalar.activation(dst, acc[:], COPY, scale=gain_col)
+                nc.scalar.activation(dst, y_acc[n, q][:], COPY, scale=gain_col)
 
         load_w1(1)
         load_w1(2)
@@ -258,7 +286,8 @@ def tile_list_eclipse_shed_planner_kernel(
         load_w1(4)
         load_stored(1)
         first_product(0)
-        scatter_page(0)
+        scatter_page(0, 0)
+        scatter_page(0, 1)
         round_w1(1)
         quantise_w1((1,), "wide1")
         first_product(1)
@@ -288,7 +317,7 @@ def tile_list_eclipse_shed_planner_kernel(
         for j in range(R_TILES):
             turn_stored(j)
             if j > 0:
-                scatter_page(j)
+                scatter_page(j, 0)
             if j == 1:
                 quantise_w1((5, 6, 7), "second")
                 for m in range(5, R_TILES):
@@ -303,25 +332,39 @@ def tile_list_eclipse_shed_planner_kernel(
                     add_page(j, q)
             if j == 3:
                 for q in range(QUARTERS):
-                    quantise_z(0, q)
+                    turn_back(0, q)
 
         outs = [ring.tile([P, T2], F32, name=f"outpage{b}", tag="stored", bufs=2) for b in range(OUTS)]
         for page in outs:
             nc.gpsimd.memset(page[:], 0.0)
-        last = R_TILES - 1
+        quantise_z(0, (0, 1), "last0")
+        second_pass(0, 0, 0)
+        second_pass(0, 1, 0)
+        clamp_last_piece()
+        scatter_page(last, 1)
+        quantise_z(0, (2, 3), "hold")
         for step in range(QUARTERS + 2):
             if step < QUARTERS:
                 add_page(last, step)
+            if step in (1, 2):
+                second_pass(0, step + 1, 0)
             if 1 <= step <= QUARTERS:
-                quantise_z(1, step - 1)
+                turn_back(1, step - 1)
+                quantise_z(1, (step - 1,), f"z1_{step - 1}")
+            if step in (3, 4):
+                second_pass(1, step - 3, 0)
             if step >= 2:
-                second_product(0, step - 2)
+                second_pass(0, step - 2, 1)
+                fetch_scores(0, step - 2)
 
         for n in range(N_TILES):
             if n + 1 < N_TILES:
                 for q in range(QUARTERS):
-                    second_product(n + 1, q)
-            x = ring.tile([P, PICK], F32, name=f"x{n}", tag="h", bufs=6)
+                    if (n + 1, q) not in y_acc:
+                        second_pass(n + 1, q, 0)
+                    second_pass(n + 1, q, 1)
+                    fetch_scores(n + 1, q)
+            x = ring.tile([P, PICK], F32, name=f"x{n}", tag="h", bufs=5)
             nc.vector.tensor_tensor(x[:], y_sb[n][:].indirect(idx3[:]), duty_sb[n][:], ALU.add)
             page = outs[n % OUTS]
             nc.vector.tensor_tensor(page[:].indirect(idx4[:]), x[:], wgo_sb[:], ALU.mult)

@@ -23,7 +23,7 @@ BANK = 512
 R_TILES = H // P
 N_TILES = N // P
 QUARTERS = T2 // BANK
-W1_CHUNKS = [(0,), (1, 2), (3, 4), (5, 6), (7,)]
+W1_CHUNKS = [(0,), (1,), (2, 3), (4, 5), (6, 7)]
 LAST_SPLIT = 768
 PAGES = 3
 OUTS = 2
@@ -81,8 +81,8 @@ def tile_list_eclipse_shed_planner_kernel(
 
         w1_grouped = {}
 
-        def round_w1(j):
-            grouped = ring.tile([P, PASSES * P * 4], BF16, name=f"w1g{j}", tag="w1g", bufs=3, align_bytes=64)
+        def round_w1(j, tag):
+            grouped = keep.tile([P, PASSES * P * 4], BF16, name=f"w1g{j}", tag=tag, align_bytes=64)
             w1_grouped[j] = grouped
             for a in range(PASSES):
                 nc.scalar.copy(
@@ -100,7 +100,7 @@ def tile_list_eclipse_shed_planner_kernel(
                     w1_scales[j, a] = scales[:, P * a : P * (a + 1)]
 
         idx = load_list(offs, "idx")
-        scale_rows = ring.tile([P, T // 4], I32, name="scale_rows", tag="h", bufs=5)
+        scale_rows = ring.tile([P, T // 4], I32, name="scale_rows", tag="h", bufs=3)
         for quad in range(4):
             nc.sync.dma_start(scale_rows[32 * quad : 32 * quad + 8, :], tab_scales[:, 4 * quad : 4 * quad + 4, :].bitcast(I32))
         for quad in range(4):
@@ -129,41 +129,28 @@ def tile_list_eclipse_shed_planner_kernel(
         cols = keep.tile([P, 20], F32, name="cols")
         nc.scalar.copy(cols[:], turned[:, 0:20])
 
-        round_w1(0)
+        round_w1(0, "slot_a")
         quantise_w1((0,), "w1c0")
 
         v_codes = [keep.tile([P, S], U32, name=f"v_codes{a}", align_bytes=64) for a in range(PASSES)]
         v_plane = keep.tile([P, S], U8, name="v_plane", align_bytes=64)
         nc.vector.tensor_copy(v_plane[:], tab_plane[:].indirect(idx[:]))
-        nc.vector.tensor_copy(v_codes[0][:], words0[:].bitcast(U32).indirect(idx[:]))
-        pages.append(keep.tile([P, T2], F32, name="page_late", tag="wide0", align_bytes=64))
+        pages.append(keep.tile([P, T2], F32, name="page_late", tag="plane", align_bytes=64))
         nc.gpsimd.memset(pages[-1][:], 0.0)
+        nc.vector.tensor_copy(v_codes[0][:], words0[:].bitcast(U32).indirect(idx[:]))
         for half in range(2):
             span = slice(BANK * half, BANK * (half + 1))
             listed = idx[:, 32 * half : 32 * (half + 1)]
             nc.vector.tensor_copy(v_codes[1][:, span], words1[:].bitcast(U32).indirect(listed))
 
         last = R_TILES - 1
-        h_sb = {}
+        d_acc = {}
 
-        def pieces(j):
-            if j == 0:
-                return [(0, BANK, "first0"), (BANK, S, "first1")]
-            if j == last:
-                return [(0, LAST_SPLIT, "last0"), (LAST_SPLIT, S, "unclamped")]
-            return [(0, S, "second" if j == 1 else "h")]
-
-        def first_product(j):
-            lo_col, hi_col = cols[:, j : j + 1], cols[:, 8 + j : 9 + j]
-            h_sb[j] = []
-            for c0, c1, tag in pieces(j):
-                if tag == "h":
-                    h_sb[j].append(ring.tile([P, c1 - c0], F32, name=f"h{j}", tag="h", bufs=5))
-                else:
-                    h_sb[j].append(keep.tile([P, c1 - c0], F32, name=f"h{j}_{c0}", tag=tag, align_bytes=64))
+        def first_product(j, banks):
             for half in range(2):
                 span = slice(BANK * half, BANK * (half + 1))
-                acc = psum.tile([P, BANK], F32, name=f"dacc{j}_{half}", tag="acc", bufs=2)
+                acc = psum.tile([P, BANK], F32, name=f"dacc{j}_{half}", tag=f"bank{banks[half]}", bufs=1)
+                d_acc[j, half] = acc
                 for a in range(PASSES):
                     nc.tensor.matmul_mx(
                         out=acc[:],
@@ -174,32 +161,37 @@ def tile_list_eclipse_shed_planner_kernel(
                         start=(a == 0),
                         stop=(a == PASSES - 1),
                     )
-                if j == 0:
-                    nc.vector.tensor_scalar(h_sb[j][half][:], acc[:], lo_col, hi_col, ALU.max, ALU.min)
-                else:
-                    for h, (c0, c1, tag) in zip(h_sb[j], pieces(j)):
-                        begin, end = max(c0, span.start), min(c1, span.stop)
-                        if begin < end:
-                            nc.scalar.copy(h[:, begin - c0 : end - c0], acc[:, begin - span.start : end - span.start])
-            if j > 0:
-                nc.vector.tensor_scalar(h_sb[j][0][:], h_sb[j][0][:], lo_col, hi_col, ALU.max, ALU.min)
 
-        def clamp_last_piece():
-            h = keep.tile([P, S - LAST_SPLIT], F32, name="h_end", tag="hold", align_bytes=64)
-            nc.vector.tensor_scalar(h[:], h_sb[last][1][:], cols[:, last : last + 1], cols[:, 8 + last : 9 + last], ALU.max, ALU.min)
-            h_sb[last][1] = h
+        def values(name, width, tag):
+            if tag == "h":
+                return ring.tile([P, width], F32, name=name, tag="h", bufs=3)
+            return keep.tile([P, width], F32, name=name, tag=tag, align_bytes=64)
 
-        def scatter_page(j, piece):
-            c0, c1, tag = pieces(j)[piece]
+        def fetch_product(j, c0, c1, tag):
+            d = values(f"d{j}_{c0}", c1 - c0, tag)
+            for half in range(2):
+                begin, end = max(c0, BANK * half), min(c1, BANK * (half + 1))
+                if begin < end:
+                    nc.scalar.copy(d[:, begin - c0 : end - c0], d_acc[j, half][:, begin - BANK * half : end - BANK * half])
+            return d
+
+        def clamp(j, dst, src):
+            nc.vector.tensor_scalar(dst[:], src[:], cols[:, j : j + 1], cols[:, 8 + j : 9 + j], ALU.max, ALU.min)
+            return dst
+
+        def scatter_page(j, h, c0, c1):
             window = pages[j % PAGES][:].indirect(idx2[:, c0 // 16 : c1 // 16])
-            nc.vector.tensor_tensor(window, h_sb[j][piece][:], wgs_sb[:, c0:c1], ALU.mult)
+            nc.vector.tensor_tensor(window, h[:], wgs_sb[:, c0:c1], ALU.mult)
+
+        def sum_banks(j):
+            return (0, 1, 2, 3) if j % 2 == 0 else (4, 5, 2, 3)
 
         sums = {}
         z_turned = {}
 
         def turn_stored(j):
             for q in range(QUARTERS):
-                bank = psum.tile([P, 4, P], F32, name=f"sum{j}_{q}", tag="sum", bufs=4)
+                bank = psum.tile([P, 4, P], F32, name=f"sum{j}_{q}", tag=f"bank{sum_banks(j)[q]}", bufs=1)
                 sums[j, q] = bank
                 for tt in range(4):
                     t0 = BANK * q + P * tt
@@ -212,7 +204,7 @@ def tile_list_eclipse_shed_planner_kernel(
                 t0 = BANK * q + P * tt
                 nc.tensor.matmul(bank[:, tt, :], pages[j % PAGES][:, t0 : t0 + P], ident[:], start=False, stop=(tt == 3), is_transpose=True)
             if jj == 0:
-                z_turned[a, q] = ring.tile([P, 4, 2, P, 2], BF16, name=f"zt{a}_{q}", tag="zt", bufs=6)
+                z_turned[a, q] = ring.tile([P, 4, 2, P, 2], BF16, name=f"zt{a}_{q}", tag="zt", bufs=5)
             dst = z_turned[a, q][:, :, :, 32 * jj : 32 * (jj + 1), :]
             src = bank[:].rearrange("t s (p u e) -> t s u p e", u=2, e=2)
             if j == last and q >= 2:
@@ -235,7 +227,7 @@ def tile_list_eclipse_shed_planner_kernel(
                 if (a, q, half) == (0, 1, 1):
                     grouped = keep.tile([P, 1024], BF16, name="zg_hold", tag="hold", align_bytes=64)
                 else:
-                    grouped = ring.tile([P, 1024], BF16, name=f"zg{a}_{q}_{half}", tag="grouped", bufs=11, align_bytes=64)
+                    grouped = ring.tile([P, 1024], BF16, name=f"zg{a}_{q}_{half}", tag="grouped", bufs=9, align_bytes=64)
                 nc.scalar.copy(grouped[:].bitcast(F32).rearrange("p (t u) -> p t u", u=2), bank[:].rearrange("p u t -> p t u"))
                 z_grouped[a, q, half] = grouped
 
@@ -255,10 +247,8 @@ def tile_list_eclipse_shed_planner_kernel(
 
         def second_pass(n, q, a):
             if a == 0:
-                if (QUARTERS * n + q) % 6 < 2:
-                    y_acc[n, q] = psum.tile([P, BANK], F32, name=f"yacc{n}_{q}", tag="acc", bufs=2)
-                else:
-                    y_acc[n, q] = psum.tile([P, BANK], F32, name=f"yacc{n}_{q}", tag="sum", bufs=4)
+                bank = (0, 1, 4, 5, 2, 3)[(QUARTERS * n + q) % 6]
+                y_acc[n, q] = psum.tile([P, BANK], F32, name=f"yacc{n}_{q}", tag=f"bank{bank}", bufs=1)
             nc.tensor.matmul_mx(
                 out=y_acc[n, q][:],
                 lhsT=w4_sb[:, a, 2 * P * n : 2 * P * (n + 1)].bitcast(FP4X4),
@@ -285,21 +275,24 @@ def tile_list_eclipse_shed_planner_kernel(
         load_w1(3)
         load_w1(4)
         load_stored(1)
-        first_product(0)
-        scatter_page(0, 0)
-        scatter_page(0, 1)
-        round_w1(1)
-        quantise_w1((1,), "wide1")
-        first_product(1)
-        round_w1(2)
-        round_w1(3)
-        quantise_w1((2, 3), "first0")
-        round_w1(4)
-        quantise_w1((4,), "first1")
-        for j in range(2, 5):
-            first_product(j)
-        for j in range(5, R_TILES):
-            round_w1(j)
+        h_sb = {}
+        first_product(0, (4, 5))
+        scatter_page(0, clamp(0, values("h0a", BANK, "slot_b"), d_acc[0, 0]), 0, BANK)
+        round_w1(1, "slot_c")
+        round_w1(2, "slot_d")
+        round_w1(3, "slot_a")
+        quantise_w1((1,), "slot_b")
+        scatter_page(0, clamp(0, values("h0b", BANK, "slot_c"), d_acc[0, 1]), BANK, S)
+        first_product(1, (4, 5))
+        unclamped = fetch_product(1, 0, S, "slot_e")
+        quantise_w1((2, 3), "slot_c")
+        h_sb[1] = clamp(1, values("h1", S, "slot_d"), unclamped)
+        first_product(2, (4, 5))
+        h_sb[2] = fetch_product(2, 0, S, "slot_f")
+        clamp(2, h_sb[2], h_sb[2])
+        round_w1(4, "slot_b")
+        round_w1(5, "slot_a")
+        round_w1(6, "slot_e")
 
         w4_sb = keep.tile([P, PASSES, 2 * N], U8, name="w4_sb", align_bytes=64)
         nc.sync.dma_start(w4_sb[:].bitcast(I32), w4_words.rearrange("a p c -> p a c").bitcast(I32))
@@ -310,38 +303,52 @@ def tile_list_eclipse_shed_planner_kernel(
             )
         idx3 = load_list(offs3, "idx3")
         idx4 = load_list(offs4, "idx4")
-        wgo_sb = keep.tile([P, PICK], F32, name="wgo_sb", tag="plane", align_bytes=64)
-        nc.sync.dma_start(wgo_sb[:], wgo)
 
         duty_sb = {}
+        outs = []
         for j in range(R_TILES):
             turn_stored(j)
             if j > 0:
-                scatter_page(j, 0)
+                scatter_page(j, h_sb[j], 0, LAST_SPLIT if j == last else S)
             if j == 1:
-                quantise_w1((5, 6, 7), "second")
-                for m in range(5, R_TILES):
-                    first_product(m)
+                quantise_w1((4, 5, 6), "slot_d")
+                round_w1(7, "slot_b")
+            if j == 2:
+                quantise_w1((7,), "slot_f")
             if j + 2 < R_TILES:
                 load_stored(j + 2)
             if j >= 4:
                 duty_sb[j - 4] = ring.tile([P, PICK], F32, name=f"duty{j - 4}", tag="raw", bufs=8)
                 nc.sync.dma_start(duty_sb[j - 4][:], duty[P * (j - 4) : P * (j - 3), :])
-            if j < R_TILES - 1:
+            if j < last:
                 for q in range(QUARTERS):
                     add_page(j, q)
+            ahead = j + PAGES
+            if ahead < R_TILES:
+                first_product(ahead, sum_banks(j)[:2])
+                if ahead in (4, 5):
+                    tag = f"out{ahead - 4}"
+                    h_sb[ahead] = clamp(ahead, values(f"h{ahead}", S, "h"), fetch_product(ahead, 0, S, tag))
+                    outs.append(values(tag, T2, tag))
+                    nc.gpsimd.memset(outs[-1][:], 0.0)
+                elif ahead < last:
+                    h_sb[ahead] = fetch_product(ahead, 0, S, "h")
+                    clamp(ahead, h_sb[ahead], h_sb[ahead])
+                else:
+                    h_sb[last] = fetch_product(last, 0, LAST_SPLIT, "last0")
+                    unclamped = fetch_product(last, LAST_SPLIT, S, "slot_e")
+                    clamp(last, h_sb[last], h_sb[last])
             if j == 3:
                 for q in range(QUARTERS):
                     turn_back(0, q)
+            if j == 5:
+                wgo_sb = keep.tile([P, PICK], F32, name="wgo_sb", tag="plane", align_bytes=64)
+                nc.sync.dma_start(wgo_sb[:], wgo)
 
-        outs = [ring.tile([P, T2], F32, name=f"outpage{b}", tag="stored", bufs=2) for b in range(OUTS)]
-        for page in outs:
-            nc.gpsimd.memset(page[:], 0.0)
         quantise_z(0, (0, 1), "last0")
         second_pass(0, 0, 0)
         second_pass(0, 1, 0)
-        clamp_last_piece()
-        scatter_page(last, 1)
+        scatter_page(last, clamp(last, values("h_end", S - LAST_SPLIT, "hold"), unclamped), LAST_SPLIT, S)
         quantise_z(0, (2, 3), "hold")
         for step in range(QUARTERS + 2):
             if step < QUARTERS:
@@ -364,7 +371,7 @@ def tile_list_eclipse_shed_planner_kernel(
                         second_pass(n + 1, q, 0)
                     second_pass(n + 1, q, 1)
                     fetch_scores(n + 1, q)
-            x = ring.tile([P, PICK], F32, name=f"x{n}", tag="h", bufs=5)
+            x = ring.tile([P, PICK], F32, name=f"x{n}", tag="h", bufs=3)
             nc.vector.tensor_tensor(x[:], y_sb[n][:].indirect(idx3[:]), duty_sb[n][:], ALU.add)
             page = outs[n % OUTS]
             nc.vector.tensor_tensor(page[:].indirect(idx4[:]), x[:], wgo_sb[:], ALU.mult)

@@ -25,6 +25,7 @@ N_TILES = N // P
 QUARTERS = T2 // BANK
 W1_CHUNKS = [(0,), (1,), (2, 3), (4, 5), (6, 7)]
 LAST_SPLIT = 768
+WARM_UP = 4
 PAGES = 3
 OUTS = 2
 
@@ -348,6 +349,17 @@ def tile_list_eclipse_shed_planner_kernel(
         quantise_z(0, (0, 1), "last0")
         second_pass(0, 0, 0)
         second_pass(0, 1, 0)
+        for turn in range(WARM_UP):
+            spare = psum.tile([P, BANK], F32, name=f"warm{turn}", tag="back", bufs=2)
+            nc.tensor.matmul_mx(
+                out=spare[:],
+                lhsT=w4_sb[:, 0, 0 : 2 * P].bitcast(FP4X4),
+                lhsT_scale=w4_plane[:, 0, 0:P],
+                rhs=z_codes[0, 1].bitcast(FP8X4),
+                rhs_scale=z_scales[0, 1][:],
+                start=True,
+                stop=True,
+            )
         scatter_page(last, clamp(last, values("h_end", S - LAST_SPLIT, "hold"), unclamped), LAST_SPLIT, S)
         quantise_z(0, (2, 3), "hold")
         for step in range(QUARTERS + 2):
@@ -362,6 +374,9 @@ def tile_list_eclipse_shed_planner_kernel(
                 second_pass(1, step - 3, 0)
             if step >= 2:
                 second_pass(0, step - 2, 1)
+            if step in (3, 4):
+                second_pass(1, step - 3, 1)
+            if step >= 2:
                 fetch_scores(0, step - 2)
 
         for n in range(N_TILES):
@@ -369,7 +384,7 @@ def tile_list_eclipse_shed_planner_kernel(
                 for q in range(QUARTERS):
                     if (n + 1, q) not in y_acc:
                         second_pass(n + 1, q, 0)
-                    second_pass(n + 1, q, 1)
+                        second_pass(n + 1, q, 1)
                     fetch_scores(n + 1, q)
             x = ring.tile([P, PICK], F32, name=f"x{n}", tag="h", bufs=3)
             nc.vector.tensor_tensor(x[:], y_sb[n][:].indirect(idx3[:]), duty_sb[n][:], ALU.add)

@@ -18,16 +18,18 @@ ALU = mybir.AluOpType
 COPY = mybir.ActivationFunctionType.Copy
 
 P = 128
+QUAD = 32
 PASSES = 2
 BANK = 512
 R_TILES = H // P
 N_TILES = N // P
 QUARTERS = T2 // BANK
-W1_CHUNKS = [(0,), (1,), (2, 3), (4, 5), (6, 7)]
-LAST_SPLIT = 768
-WARM_UP = 4
-PAGES = 3
-OUTS = 2
+LAST = R_TILES - 1
+PAGES = 2
+STORED_BUFS = 3
+SUM_BANKS = ("sum0", "sum1", "sum2", "sum3")
+BACK_BANKS = ("back0", "back1")
+PROD_BANKS = ("prod0", "prod1")
 
 
 def tile_list_eclipse_shed_planner_kernel(
@@ -36,20 +38,21 @@ def tile_list_eclipse_shed_planner_kernel(
     nc = tc.nc
     with ExitStack() as ctx:
         keep = ctx.enter_context(tc.tile_pool(name="keep", bufs=1))
-        ring = ctx.enter_context(tc.tile_pool(name="ring", bufs=2))
-        psum = ctx.enter_context(tc.psum_pool(name="psum", bufs=2))
+        psum = ctx.enter_context(tc.psum_pool(name="psum", bufs=1))
 
-        tab_plane = keep.tile([P, T], U8, name="tab_plane", tag="plane", align_bytes=64)
-        nc.vector.memset(tab_plane[:].bitcast(I32), 0)
+        def sb(name, shape, dtype, tag=None):
+            return keep.tile(shape, dtype, name=name, tag=tag or name, align_bytes=64)
+
+        def bank_tile(name, shape, tag):
+            return psum.tile(shape, F32, name=name, tag=tag)
+
         rows = keep.tile([P, P], F32, name="rows")
         nc.gpsimd.memset(rows[:], 0.0)
         ident = keep.tile([P, P], F32, name="ident")
         make_identity(nc, ident[:])
-        w4_plane = keep.tile([P, PASSES, N], U8, name="w4_plane", align_bytes=64)
-        nc.vector.memset(w4_plane[:].bitcast(I32), 0)
-        pages = [keep.tile([P, T2], F32, name=f"page{b}") for b in range(PAGES - 1)]
-        for page in pages:
-            nc.vector.memset(page[:], 0.0)
+
+        tab_plane = sb("tab_plane", [P, T], U8)
+        nc.gpsimd.memset(tab_plane[:].bitcast(I32), 0)
 
         def load_list(src, name):
             tile = keep.tile([P, S // 16], U16, name=name)
@@ -57,212 +60,216 @@ def tile_list_eclipse_shed_planner_kernel(
             return tile
 
         def load_table(a):
-            tile = keep.tile([P, T], I32, name=f"words{a}", tag=f"wide{a}", align_bytes=64)
+            tile = sb(f"words{a}", [P, T], I32, f"wide{a}")
             nc.sync.dma_start(tile[:], tab_words[a].rearrange("p t i -> p (t i)").bitcast(I32))
             return tile
 
-        w1_codes = {}
-        w1_scales = {}
         w1_raw = {}
 
-        def load_w1(chunk):
-            tiles = W1_CHUNKS[chunk]
+        def load_w1(tiles, tags):
             c0, width = P * tiles[0], P * len(tiles)
             if len(tiles) == 1:
-                both = ring.tile([P, PASSES, 4, P], F32, name=f"w1raw{chunk}", tag="raw", bufs=8)
+                both = sb(f"w1raw{tiles[0]}", [P, PASSES, 4, P], F32, tags[0])
             for a in range(PASSES):
                 if len(tiles) == 1:
                     raw = both[:, a, :, :]
                 else:
-                    wide = ring.tile([P, 4, width], F32, name=f"w1raw{chunk}_{a}", tag="raw", bufs=8)
-                    raw = wide[:]
+                    raw = sb(f"w1raw{tiles[0]}_{a}", [P, 4, width], F32, tags[a])[:]
                 nc.sync.dma_start(raw, w1[512 * a : 512 * (a + 1), c0 : c0 + width].rearrange("(p i) c -> p i c", i=4))
                 for place, j in enumerate(tiles):
                     w1_raw[j, a] = raw[:, :, P * place : P * (place + 1)]
 
-        w1_grouped = {}
+        stored_sb = {}
 
-        def round_w1(j, tag):
-            grouped = keep.tile([P, PASSES * P * 4], BF16, name=f"w1g{j}", tag=tag, align_bytes=64)
+        def load_stored(j):
+            stored_sb[j] = sb(f"stored{j}", [P, T2], F32, f"rows{j % STORED_BUFS}")
+            nc.sync.dma_start(stored_sb[j][:], stored[P * j : P * (j + 1), :])
+
+        idx = load_list(offs, "idx")
+        scale_rows = sb("scale_rows", [P, T // 4], I32, "h2")
+        for quad in range(4):
+            live = slice(QUAD * quad, QUAD * quad + 8)
+            nc.sync.dma_start(scale_rows[live, :], tab_scales[:, 4 * quad : 4 * quad + 4, :].bitcast(I32))
+            nc.vector.tensor_copy(tab_plane[live, :].bitcast(I32), scale_rows[live, :])
+        words0 = load_table(0)
+        load_w1((0,), ("rawA",))
+        vectors = keep.tile([20, P], F32, name="vectors")
+        nc.sync.dma_start(vectors[0:8, :], lo.rearrange("(j p) -> j p", p=P))
+        nc.sync.dma_start(vectors[8:16, :], hi.rearrange("(j p) -> j p", p=P))
+        nc.sync.dma_start(vectors[16:20, :], gain.rearrange("(j p) -> j p", p=P))
+        words1 = load_table(1)
+        idx2 = load_list(offs2, "idx2")
+        wgs_sb = sb("wgs_sb", [P, S], F32)
+        nc.sync.dma_start(wgs_sb[:], wgs)
+        load_w1((1,), ("rawB",))
+        load_w1((2, 3), ("rawC", "rawD"))
+        load_stored(0)
+
+        pages = [sb(f"page{b}", [P, T2], F32) for b in range(PAGES)]
+        for page in pages:
+            nc.gpsimd.memset(page[:], 0.0)
+        w4_plane = sb("w4_plane", [P, PASSES, N], U8)
+        nc.gpsimd.memset(w4_plane[:].bitcast(I32), 0)
+        w4_fold = sb("w4_fold", [P, 5, 2 * P], U8)
+        nc.gpsimd.memset(w4_fold[:].bitcast(I32), 0)
+        w4_fold_plane = sb("w4_fold_plane", [P, 5, P], U8)
+        nc.gpsimd.memset(w4_fold_plane[:].bitcast(I32), 0)
+        z_turned = [sb(f"zt{q}", [P, 4, 2, LAST * QUAD, 2], BF16) for q in range(QUARTERS)]
+        zb_codes = sb("zb_codes", [P, QUARTERS, BANK], U32)
+        zb_scales = sb("zb_scales", [P, QUARTERS, BANK], U8)
+
+        nc.scalar.copy(rows[0:20, :], vectors[:])
+        turned = bank_tile("turned", [P, P], BACK_BANKS[0])
+        nc.tensor.transpose(turned[:], rows[:], ident[:])
+        cols = keep.tile([P, 20], F32, name="cols")
+        nc.scalar.copy(cols[:], turned[:, 0:20])
+
+        w1_grouped = {}
+        w1_codes = {}
+        w1_scales = {}
+
+        def round_w1(j):
+            grouped = sb(f"w1g{j}", [P, PASSES * P * 4], BF16, f"w1g{j % 2}")
             w1_grouped[j] = grouped
             for a in range(PASSES):
                 nc.scalar.copy(
                     grouped[:, 4 * P * a : 4 * P * (a + 1)].rearrange("p (c i) -> p c i", i=4), w1_raw[j, a].rearrange("p i c -> p c i")
                 )
 
-        def quantise_w1(tiles, tag):
-            codes = keep.tile([P, len(tiles) * PASSES * P], U32, name=f"w1c{tiles[0]}", tag=tag, align_bytes=64)
-            for place, j in enumerate(tiles):
-                scales = keep.tile([P, PASSES * P], U8, name=f"w1s{j}", align_bytes=64)
-                mine = codes[:, PASSES * P * place : PASSES * P * (place + 1)]
-                nc.vector.quantize_mx(out=mine.bitcast(FP8X4), scales=scales[:], in_=w1_grouped[j][:])
-                for a in range(PASSES):
-                    w1_codes[j, a] = mine[:, P * a : P * (a + 1)]
-                    w1_scales[j, a] = scales[:, P * a : P * (a + 1)]
+        def quantise_w1(j):
+            slot = j % 2 if j < 3 else 1
+            w1_codes[j] = sb(f"w1c{j}", [P, PASSES * P], U32, f"w1c{slot}")
+            w1_scales[j] = sb(f"w1s{j}", [P, PASSES * P], U8, f"w1s{slot}")
+            nc.vector.quantize_mx(out=w1_codes[j][:].bitcast(FP8X4), scales=w1_scales[j][:], in_=w1_grouped[j][:])
 
-        idx = load_list(offs, "idx")
-        scale_rows = ring.tile([P, T // 4], I32, name="scale_rows", tag="h", bufs=3)
-        for quad in range(4):
-            nc.sync.dma_start(scale_rows[32 * quad : 32 * quad + 8, :], tab_scales[:, 4 * quad : 4 * quad + 4, :].bitcast(I32))
-        for quad in range(4):
-            nc.vector.tensor_copy(tab_plane[32 * quad : 32 * quad + 8, :].bitcast(I32), scale_rows[32 * quad : 32 * quad + 8, :])
-        words0 = load_table(0)
-        load_w1(0)
-        vectors = keep.tile([20, P], F32, name="vectors")
-        nc.sync.dma_start(vectors[0:8, :], lo.rearrange("(j p) -> j p", p=P))
-        nc.sync.dma_start(vectors[8:16, :], hi.rearrange("(j p) -> j p", p=P))
-        nc.sync.dma_start(vectors[16:20, :], gain.rearrange("(j p) -> j p", p=P))
-        nc.scalar.copy(rows[0:20, :], vectors[:])
-        words1 = load_table(1)
-        idx2 = load_list(offs2, "idx2")
-        wgs_sb = keep.tile([P, S], F32, name="wgs_sb")
-        nc.sync.dma_start(wgs_sb[:], wgs)
-
-        stored_sb = {}
-
-        def load_stored(j):
-            tile = ring.tile([P, T2], F32, name=f"stored{j}", tag="stored", bufs=2)
-            nc.sync.dma_start(tile[:], stored[P * j : P * (j + 1), :])
-            stored_sb[j] = tile
-
-        turned = psum.tile([P, P], F32, name="turned", tag="back", bufs=2)
-        nc.tensor.transpose(turned[:], rows[:], ident[:])
-        cols = keep.tile([P, 20], F32, name="cols")
-        nc.scalar.copy(cols[:], turned[:, 0:20])
-
-        round_w1(0, "slot_a")
-        quantise_w1((0,), "w1c0")
-
-        v_codes = [keep.tile([P, S], U32, name=f"v_codes{a}", align_bytes=64) for a in range(PASSES)]
-        v_plane = keep.tile([P, S], U8, name="v_plane", align_bytes=64)
-        nc.vector.tensor_copy(v_plane[:], tab_plane[:].indirect(idx[:]))
-        pages.append(keep.tile([P, T2], F32, name="page_late", tag="plane", align_bytes=64))
-        nc.gpsimd.memset(pages[-1][:], 0.0)
-        nc.vector.tensor_copy(v_codes[0][:], words0[:].bitcast(U32).indirect(idx[:]))
-        for half in range(2):
-            span = slice(BANK * half, BANK * (half + 1))
-            listed = idx[:, 32 * half : 32 * (half + 1)]
-            nc.vector.tensor_copy(v_codes[1][:, span], words1[:].bitcast(U32).indirect(listed))
-
-        last = R_TILES - 1
+        v_codes = [sb(f"v_codes{a}", [P, S], U32) for a in range(PASSES)]
+        v_plane = sb("v_plane", [P, S], U8)
         d_acc = {}
 
-        def first_product(j, banks):
+        def first_product(j):
             for half in range(2):
+                d_acc[j, half] = bank_tile(f"dacc{j}_{half}", [P, BANK], PROD_BANKS[half])
+            order = [(half, a) for a in range(PASSES) for half in range(2)] if j == 0 else [(half, a) for half in range(2) for a in range(PASSES)]
+            for half, a in order:
                 span = slice(BANK * half, BANK * (half + 1))
-                acc = psum.tile([P, BANK], F32, name=f"dacc{j}_{half}", tag=f"bank{banks[half]}", bufs=1)
-                d_acc[j, half] = acc
-                for a in range(PASSES):
-                    nc.tensor.matmul_mx(
-                        out=acc[:],
-                        lhsT=w1_codes[j, a].bitcast(FP8X4),
-                        lhsT_scale=w1_scales[j, a],
-                        rhs=v_codes[a][:, span].bitcast(FP8X4),
-                        rhs_scale=v_plane[4 * a : P, span],
-                        start=(a == 0),
-                        stop=(a == PASSES - 1),
-                    )
+                nc.tensor.matmul_mx(
+                    out=d_acc[j, half][:],
+                    lhsT=w1_codes[j][:, P * a : P * (a + 1)].bitcast(FP8X4),
+                    lhsT_scale=w1_scales[j][:, P * a : P * (a + 1)],
+                    rhs=v_codes[a][:, span].bitcast(FP8X4),
+                    rhs_scale=v_plane[4 * a : P, span],
+                    start=(a == 0),
+                    stop=(a == PASSES - 1),
+                )
 
-        def values(name, width, tag):
-            if tag == "h":
-                return ring.tile([P, width], F32, name=name, tag="h", bufs=3)
-            return keep.tile([P, width], F32, name=name, tag=tag, align_bytes=64)
+        h_sb = {}
 
-        def fetch_product(j, c0, c1, tag):
-            d = values(f"d{j}_{c0}", c1 - c0, tag)
+        def fetch_product(j, tag):
+            h_sb[j] = sb(f"h{j}", [P, S], F32, tag)
             for half in range(2):
-                begin, end = max(c0, BANK * half), min(c1, BANK * (half + 1))
-                if begin < end:
-                    nc.scalar.copy(d[:, begin - c0 : end - c0], d_acc[j, half][:, begin - BANK * half : end - BANK * half])
-            return d
+                nc.scalar.copy(h_sb[j][:, BANK * half : BANK * (half + 1)], d_acc[j, half][:])
 
         def clamp(j, dst, src):
-            nc.vector.tensor_scalar(dst[:], src[:], cols[:, j : j + 1], cols[:, 8 + j : 9 + j], ALU.max, ALU.min)
-            return dst
+            nc.vector.tensor_scalar(dst, src, cols[:, j : j + 1], cols[:, 8 + j : 9 + j], ALU.max, ALU.min)
 
         def scatter_page(j, h, c0, c1):
             window = pages[j % PAGES][:].indirect(idx2[:, c0 // 16 : c1 // 16])
-            nc.vector.tensor_tensor(window, h[:], wgs_sb[:, c0:c1], ALU.mult)
-
-        def sum_banks(j):
-            return (0, 1, 2, 3) if j % 2 == 0 else (4, 5, 2, 3)
+            nc.vector.tensor_tensor(window, h, wgs_sb[:, c0:c1], ALU.mult)
 
         sums = {}
-        z_turned = {}
 
-        def turn_stored(j):
-            for q in range(QUARTERS):
-                bank = psum.tile([P, 4, P], F32, name=f"sum{j}_{q}", tag=f"bank{sum_banks(j)[q]}", bufs=1)
-                sums[j, q] = bank
-                for tt in range(4):
-                    t0 = BANK * q + P * tt
-                    nc.tensor.matmul(bank[:, tt, :], stored_sb[j][:, t0 : t0 + P], ident[:], start=(tt == 0), stop=False, is_transpose=True)
+        def turn_stored(j, q):
+            sums[j, q] = bank_tile(f"sum{j}_{q}", [P, 4, P], SUM_BANKS[q])
+            for tt in range(4):
+                t0 = BANK * q + P * tt
+                nc.tensor.matmul(sums[j, q][:, tt, :], stored_sb[j][:, t0 : t0 + P], ident[:], start=(tt == 0), stop=False, is_transpose=True)
+
+        z_fold = {}
 
         def add_page(j, q):
-            a, jj = divmod(j, 4)
             bank = sums[j, q]
             for tt in range(4):
                 t0 = BANK * q + P * tt
                 nc.tensor.matmul(bank[:, tt, :], pages[j % PAGES][:, t0 : t0 + P], ident[:], start=False, stop=(tt == 3), is_transpose=True)
-            if jj == 0:
-                z_turned[a, q] = ring.tile([P, 4, 2, P, 2], BF16, name=f"zt{a}_{q}", tag="zt", bufs=5)
-            dst = z_turned[a, q][:, :, :, 32 * jj : 32 * (jj + 1), :]
-            src = bank[:].rearrange("t s (p u e) -> t s u p e", u=2, e=2)
-            if j == last and q >= 2:
-                nc.vector.tensor_copy(dst, src)
+            if j < LAST:
+                dst = z_turned[q][:, :, :, QUAD * j : QUAD * (j + 1), :]
+                nc.scalar.copy(dst, bank[:].rearrange("t s (p u e) -> t s u p e", u=2, e=2))
             else:
-                nc.scalar.copy(dst, src)
+                z_fold[q] = sb(f"zfold{q}", [P, 2, 4, QUAD, 2], BF16)
+                nc.scalar.copy(z_fold[q][:], bank[:].rearrange("t s (p u e) -> t u s p e", u=2, e=2))
+
+        z_grouped = {}
+
+        def turn_back(a, q, banks):
+            first = 3 * QUAD * a
+            pairs = z_turned[q][:].rearrange("t s u p e -> t (s u p e)").bitcast(F32).rearrange("t (s u p) -> t s u p", s=4, u=2)
+            grouped = sb(f"zg{a}_{q}", [P, 4 * BANK], BF16, f"zg{q}")
+            z_grouped[a, q] = grouped
+            for half in range(2):
+                bank = bank_tile(f"back{a}_{q}_{half}", [P, 2, 256], banks[half])
+                for s in range(2):
+                    for u in range(2):
+                        nc.tensor.transpose(bank[:, u, P * s : P * (s + 1)], pairs[:, 2 * half + s, u, first : first + P], ident[:])
+                words = grouped[:, 1024 * half : 1024 * (half + 1)].bitcast(F32)
+                nc.scalar.copy(words.rearrange("p (t u) -> p t u", u=2), bank[:].rearrange("p u t -> p t u"))
 
         z_codes = {}
         z_scales = {}
 
-        z_grouped = {}
+        def quantise_z(a, q):
+            if a == 0:
+                z_codes[a, q], z_scales[a, q] = sb(f"za_codes{q}", [P, BANK], U32)[:], sb(f"za_scales{q}", [P, BANK], U8)[:]
+            else:
+                z_codes[a, q], z_scales[a, q] = zb_codes[:, q, :], zb_scales[:, q, :]
+            nc.vector.quantize_mx(out=z_codes[a, q].bitcast(FP8X4), scales=z_scales[a, q], in_=z_grouped[a, q][:])
 
-        def turn_back(a, q):
-            pairs = z_turned[a, q][:].rearrange("t s u p e -> t (s u p e)").bitcast(F32).rearrange("t (s u p) -> t s u p", s=4, u=2)
-            for half in range(2):
-                bank = psum.tile([P, 2, 256], F32, name=f"back{a}_{q}_{half}", tag="back", bufs=2)
-                for s in range(2):
-                    for u in range(2):
-                        nc.tensor.transpose(bank[:, u, P * s : P * (s + 1)], pairs[:, 2 * half + s, u, :], ident[:])
-                if (a, q, half) == (0, 1, 1):
-                    grouped = keep.tile([P, 1024], BF16, name="zg_hold", tag="hold", align_bytes=64)
-                else:
-                    grouped = ring.tile([P, 1024], BF16, name=f"zg{a}_{q}_{half}", tag="grouped", bufs=9, align_bytes=64)
-                nc.scalar.copy(grouped[:].bitcast(F32).rearrange("p (t u) -> p t u", u=2), bank[:].rearrange("p u t -> p t u"))
-                z_grouped[a, q, half] = grouped
+        fold_codes = sb("fold_codes", [P, QUARTERS, P], U32)
+        fold_scales = sb("fold_scales", [P, QUARTERS, P], U8)
 
-        def quantise_z(a, quarters, tag):
-            codes = keep.tile([P, BANK * len(quarters)], U32, name=f"zc{a}_{quarters[0]}", tag=tag, align_bytes=64)
-            for place, q in enumerate(quarters):
-                scales = keep.tile([P, BANK], U8, name=f"zs{a}_{q}", align_bytes=64)
-                z_codes[a, q], z_scales[a, q] = codes[:, BANK * place : BANK * (place + 1)], scales
-                for half in range(2):
-                    span = slice(256 * half, 256 * (half + 1))
-                    nc.vector.quantize_mx(
-                        out=z_codes[a, q][:, span].bitcast(FP8X4), scales=scales[:, span], in_=z_grouped[a, q, half][:]
-                    )
+        def turn_back_fold(q):
+            pairs = z_fold[q][:].rearrange("t u s p e -> t (u s p e)").bitcast(F32).rearrange("t (u c) -> t u c", u=2)
+            bank = bank_tile(f"backfold{q}", [P, 2, P], SUM_BANKS[q])
+            for u in range(2):
+                nc.tensor.transpose(bank[:, u, :], pairs[:, u, :], ident[:])
+            grouped = sb(f"zgfold{q}", [P, 4 * P], BF16)
+            nc.scalar.copy(grouped[:].bitcast(F32).rearrange("p (t u) -> p t u", u=2), bank[:].rearrange("p u t -> p t u"))
+            nc.vector.quantize_mx(out=fold_codes[:, q, :].bitcast(FP8X4), scales=fold_scales[:, q, :], in_=grouped[:])
 
         y_sb = {}
         y_acc = {}
 
-        def second_pass(n, q, a):
-            if a == 0:
-                bank = (0, 1, 4, 5, 2, 3)[(QUARTERS * n + q) % 6]
-                y_acc[n, q] = psum.tile([P, BANK], F32, name=f"yacc{n}_{q}", tag=f"bank{bank}", bufs=1)
+        def second_pass(n, q, a, bank=None, stop=False):
+            if bank:
+                y_acc[n, q] = bank_tile(f"yacc{n}_{q}", [P, BANK], bank)
+            if (n, a) == (0, 1):
+                weight, plane = w4_fold[:, 4, :], w4_fold_plane[:, 4, :]
+            else:
+                weight, plane = w4_sb[:, a, 2 * P * n : 2 * P * (n + 1)], w4_plane[:, a, P * n : P * (n + 1)]
             nc.tensor.matmul_mx(
                 out=y_acc[n, q][:],
-                lhsT=w4_sb[:, a, 2 * P * n : 2 * P * (n + 1)].bitcast(FP4X4),
-                lhsT_scale=w4_plane[:, a, P * n : P * (n + 1)],
+                lhsT=weight.bitcast(FP4X4),
+                lhsT_scale=plane,
                 rhs=z_codes[a, q].bitcast(FP8X4),
-                rhs_scale=z_scales[a, q][:],
-                start=(a == 0),
-                stop=(a == PASSES - 1),
+                rhs_scale=z_scales[a, q],
+                start=bool(bank),
+                stop=stop,
             )
+
+        def fold_passes(q):
+            for s in range(4):
+                nc.tensor.matmul_mx(
+                    out=y_acc[0, q][:, P * s : P * (s + 1)],
+                    lhsT=w4_fold[:, s, :].bitcast(FP4X4),
+                    lhsT_scale=w4_fold_plane[:, s, :],
+                    rhs=fold_codes[:, q, :].bitcast(FP8X4),
+                    rhs_scale=fold_scales[:, q, :],
+                    start=False,
+                    stop=(s == 3),
+                )
 
         def fetch_scores(n, q):
             if q == 0:
-                y_sb[n] = keep.tile([P, T2], F32, name=f"y{n}", tag=f"wide{n % 2}", align_bytes=64)
+                y_sb[n] = sb(f"y{n}", [P, T2], F32, f"rows{(R_TILES + n) % STORED_BUFS}")
             dst = y_sb[n][:, BANK * q : BANK * (q + 1)]
             gain_col = cols[:, 16 + n : 17 + n]
             if n == 0 and q % 2 == 1:
@@ -270,124 +277,134 @@ def tile_list_eclipse_shed_planner_kernel(
             else:
                 nc.scalar.activation(dst, y_acc[n, q][:], COPY, scale=gain_col)
 
-        load_w1(1)
-        load_w1(2)
-        load_stored(0)
-        load_w1(3)
-        load_w1(4)
-        load_stored(1)
-        h_sb = {}
-        first_product(0, (4, 5))
-        scatter_page(0, clamp(0, values("h0a", BANK, "slot_b"), d_acc[0, 0]), 0, BANK)
-        round_w1(1, "slot_c")
-        round_w1(2, "slot_d")
-        round_w1(3, "slot_a")
-        quantise_w1((1,), "slot_b")
-        scatter_page(0, clamp(0, values("h0b", BANK, "slot_c"), d_acc[0, 1]), BANK, S)
-        first_product(1, (4, 5))
-        unclamped = fetch_product(1, 0, S, "slot_e")
-        quantise_w1((2, 3), "slot_c")
-        h_sb[1] = clamp(1, values("h1", S, "slot_d"), unclamped)
-        first_product(2, (4, 5))
-        h_sb[2] = fetch_product(2, 0, S, "slot_f")
-        clamp(2, h_sb[2], h_sb[2])
-        round_w1(4, "slot_b")
-        round_w1(5, "slot_a")
-        round_w1(6, "slot_e")
+        nc.vector.tensor_copy(v_codes[0][:], words0[:].bitcast(U32).indirect(idx[:]))
+        round_w1(0)
+        quantise_w1(0)
+        nc.vector.tensor_copy(v_plane[:], tab_plane[:].indirect(idx[:]))
+        for half in range(2):
+            listed = idx[:, 32 * half : 32 * (half + 1)]
+            nc.vector.tensor_copy(v_codes[1][:, BANK * half : BANK * (half + 1)], words1[:].bitcast(U32).indirect(listed))
+        outs = [None, sb("out1", [P, T2], F32, "wide1")]
+        nc.gpsimd.memset(outs[1][:], 0.0)
 
-        w4_sb = keep.tile([P, PASSES, 2 * N], U8, name="w4_sb", align_bytes=64)
-        nc.sync.dma_start(w4_sb[:].bitcast(I32), w4_words.rearrange("a p c -> p a c").bitcast(I32))
+        first_product(0)
+        h_first = sb("h0a", [P, BANK], F32, "h0")
+        clamp(0, h_first[:], d_acc[0, 0][:])
+        scatter_page(0, h_first[:], 0, BANK)
+        round_w1(1)
+        quantise_w1(1)
+        h_second = sb("h0b", [P, BANK], F32, "rawB")
+        nc.scalar.copy(h_second[:], d_acc[0, 1][:])
+        clamp(0, h_second[:], h_second[:])
+        scatter_page(0, h_second[:], BANK, S)
+
+        load_stored(1)
+        load_w1((4, 5), ("rawA", "rawB"))
+        w4_sb = sb("w4_sb", [P, PASSES, 2 * N], U8)
+        nc.sync.dma_start(w4_sb[:, 0, :].bitcast(I32), w4_words[0].bitcast(I32))
         for quad in range(4):
-            nc.sync.dma_start(
-                w4_plane[32 * quad : 32 * quad + 4, :, :].bitcast(I32),
-                w4_scales[:, 4 * quad : 4 * quad + 4, :].rearrange("a r c -> r a c").bitcast(I32),
-            )
+            lanes = slice(QUAD * quad, QUAD * (quad + 1))
+            live = slice(QUAD * quad, QUAD * quad + 4)
+            src = (quad + 3) % 4
+            src_lanes = slice(QUAD * src, QUAD * (src + 1))
+            src_live = slice(4 * src, 4 * src + 4)
+            nc.sync.dma_start(w4_plane[live, 0, :].bitcast(I32), w4_scales[0, 4 * quad : 4 * quad + 4, :].bitcast(I32))
+            nc.sync.dma_start(w4_plane[live, 1, :].bitcast(I32), w4_scales[1, src_live, :].bitcast(I32))
+            nc.sync.dma_start(w4_sb[lanes, 1, :].bitcast(I32), w4_words[1, src_lanes, :].bitcast(I32))
+            if quad > 0:
+                nc.sync.dma_start(w4_fold[lanes, 4, :].bitcast(I32), w4_words[1, src_lanes, 0 : 2 * P].bitcast(I32))
+                nc.sync.dma_start(w4_fold_plane[live, 4, :].bitcast(I32), w4_scales[1, src_live, 0:P].bitcast(I32))
+            nc.sync.dma_start(w4_fold[lanes, quad, :].bitcast(I32), w4_words[1, 3 * QUAD : P, 0 : 2 * P].bitcast(I32))
+            nc.sync.dma_start(w4_fold_plane[live, quad, :].bitcast(I32), w4_scales[1, 12:16, 0:P].bitcast(I32))
+        load_stored(2)
         idx3 = load_list(offs3, "idx3")
         idx4 = load_list(offs4, "idx4")
 
-        duty_sb = {}
-        outs = []
-        for j in range(R_TILES):
-            turn_stored(j)
-            if j > 0:
-                scatter_page(j, h_sb[j], 0, LAST_SPLIT if j == last else S)
-            if j == 1:
-                quantise_w1((4, 5, 6), "slot_d")
-                round_w1(7, "slot_b")
-            if j == 2:
-                quantise_w1((7,), "slot_f")
-            if j + 2 < R_TILES:
-                load_stored(j + 2)
-            if j >= 4:
-                duty_sb[j - 4] = ring.tile([P, PICK], F32, name=f"duty{j - 4}", tag="raw", bufs=8)
-                nc.sync.dma_start(duty_sb[j - 4][:], duty[P * (j - 4) : P * (j - 3), :])
-            if j < last:
-                for q in range(QUARTERS):
-                    add_page(j, q)
-            ahead = j + PAGES
-            if ahead < R_TILES:
-                first_product(ahead, sum_banks(j)[:2])
-                if ahead in (4, 5):
-                    tag = f"out{ahead - 4}"
-                    h_sb[ahead] = clamp(ahead, values(f"h{ahead}", S, "h"), fetch_product(ahead, 0, S, tag))
-                    outs.append(values(tag, T2, tag))
-                    nc.gpsimd.memset(outs[-1][:], 0.0)
-                elif ahead < last:
-                    h_sb[ahead] = fetch_product(ahead, 0, S, "h")
-                    clamp(ahead, h_sb[ahead], h_sb[ahead])
-                else:
-                    h_sb[last] = fetch_product(last, 0, LAST_SPLIT, "last0")
-                    unclamped = fetch_product(last, LAST_SPLIT, S, "slot_e")
-                    clamp(last, h_sb[last], h_sb[last])
-            if j == 3:
-                for q in range(QUARTERS):
-                    turn_back(0, q)
-            if j == 5:
-                wgo_sb = keep.tile([P, PICK], F32, name="wgo_sb", tag="plane", align_bytes=64)
-                nc.sync.dma_start(wgo_sb[:], wgo)
+        first_product(1)
+        round_w1(2)
+        round_w1(3)
+        quantise_w1(2)
+        quantise_w1(3)
+        fetch_product(1, "rawC")
+        clamp(1, h_sb[1][:], h_sb[1][:])
+        for q in range(QUARTERS):
+            turn_stored(0, q)
+        first_product(2)
+        fetch_product(2, "h2")
+        load_w1((6, 7), ("rawC", "rawD"))
+        duty_sb = sb("duty_sb", [P, N_TILES, PICK], F32, "wide0")
+        nc.sync.dma_start(duty_sb[:], duty.rearrange("(n p) m -> p n m", p=P))
+        wgo_sb = sb("wgo_sb", [P, PICK], F32)
+        nc.sync.dma_start(wgo_sb[:], wgo)
 
-        quantise_z(0, (0, 1), "last0")
-        second_pass(0, 0, 0)
-        second_pass(0, 1, 0)
-        for turn in range(WARM_UP):
-            spare = psum.tile([P, BANK], F32, name=f"warm{turn}", tag="back", bufs=2)
-            nc.tensor.matmul_mx(
-                out=spare[:],
-                lhsT=w4_sb[:, 0, 0 : 2 * P].bitcast(FP4X4),
-                lhsT_scale=w4_plane[:, 0, 0:P],
-                rhs=z_codes[0, 1].bitcast(FP8X4),
-                rhs_scale=z_scales[0, 1][:],
-                start=True,
-                stop=True,
+        for j in range(1, LAST):
+            scatter_page(j, h_sb[j][:], 0, S)
+            if j == 1:
+                clamp(2, h_sb[2][:], h_sb[2][:])
+            ahead = j + 2
+            if ahead <= LAST:
+                first_product(ahead)
+                fetch_product(ahead, f"h{ahead % 3}")
+                clamp(ahead, h_sb[ahead][:], h_sb[ahead][:])
+                if ahead < LAST:
+                    round_w1(ahead + 1)
+                    quantise_w1(ahead + 1)
+            if j == 6:
+                turn_back(0, 3, PROD_BANKS)
+                quantise_z(0, 3)
+            for q in range(QUARTERS):
+                add_page(j - 1, q)
+            for q in range(QUARTERS):
+                turn_stored(j, q)
+            if j + 2 <= LAST:
+                load_stored(j + 2)
+            for q in {4: (2,), 5: (0, 1)}.get(j, ()):
+                turn_back(0, q, BACK_BANKS)
+                quantise_z(0, q)
+
+        scatter_page(LAST, h_sb[LAST][:], 0, S)
+        add_page(6, 0)
+        add_page(6, 1)
+        second_pass(0, 0, 0, PROD_BANKS[0])
+        second_pass(0, 1, 0, PROD_BANKS[1])
+        add_page(6, 2)
+        add_page(6, 3)
+        outs[0] = sb("out0", [P, T2], F32, "page0")
+        nc.gpsimd.memset(outs[0][:], 0.0)
+        for q in range(QUARTERS):
+            turn_back(1, q, BACK_BANKS)
+            quantise_z(1, q)
+            turn_stored(LAST, q)
+        second_pass(0, 2, 0, BACK_BANKS[0])
+        second_pass(0, 3, 0, BACK_BANKS[1])
+
+        for q in range(QUARTERS):
+            add_page(LAST, q)
+        second_pass(0, 0, 1)
+        for q in range(QUARTERS):
+            turn_back_fold(q)
+        for q in range(1, QUARTERS):
+            second_pass(0, q, 1)
+        for q in range(QUARTERS):
+            fold_passes(q)
+            fetch_scores(0, q)
+        for s in range(4):
+            nc.sync.dma_start(
+                zb_codes[0:QUAD, :, P * s : P * (s + 1)].bitcast(I32), fold_codes[QUAD * s : QUAD * (s + 1), :, :].bitcast(I32)
             )
-        scatter_page(last, clamp(last, values("h_end", S - LAST_SPLIT, "hold"), unclamped), LAST_SPLIT, S)
-        quantise_z(0, (2, 3), "hold")
-        for step in range(QUARTERS + 2):
-            if step < QUARTERS:
-                add_page(last, step)
-            if step in (1, 2):
-                second_pass(0, step + 1, 0)
-            if 1 <= step <= QUARTERS:
-                turn_back(1, step - 1)
-                quantise_z(1, (step - 1,), f"z1_{step - 1}")
-            if step in (3, 4):
-                second_pass(1, step - 3, 0)
-            if step >= 2:
-                second_pass(0, step - 2, 1)
-            if step in (3, 4):
-                second_pass(1, step - 3, 1)
-            if step >= 2:
-                fetch_scores(0, step - 2)
+            nc.sync.dma_start(
+                zb_scales[0:4, :, P * s : P * (s + 1)].bitcast(I32), fold_scales[QUAD * s : QUAD * s + 4, :, :].bitcast(I32)
+            )
 
         for n in range(N_TILES):
             if n + 1 < N_TILES:
+                banks = SUM_BANKS if n % 2 == 0 else PROD_BANKS + BACK_BANKS
                 for q in range(QUARTERS):
-                    if (n + 1, q) not in y_acc:
-                        second_pass(n + 1, q, 0)
-                        second_pass(n + 1, q, 1)
+                    second_pass(n + 1, q, 1, banks[q])
+                    second_pass(n + 1, q, 0, stop=True)
                     fetch_scores(n + 1, q)
-            x = ring.tile([P, PICK], F32, name=f"x{n}", tag="h", bufs=3)
-            nc.vector.tensor_tensor(x[:], y_sb[n][:].indirect(idx3[:]), duty_sb[n][:], ALU.add)
-            page = outs[n % OUTS]
+            x = sb(f"x{n}", [P, PICK], F32, f"h{n % 3}")
+            nc.vector.tensor_tensor(x[:], y_sb[n][:].indirect(idx3[:]), duty_sb[:, n, :], ALU.add)
+            page = outs[n % 2]
             nc.vector.tensor_tensor(page[:].indirect(idx4[:]), x[:], wgo_sb[:], ALU.mult)
             nc.sync.dma_start(out[P * n : P * (n + 1), :], page[:])

@@ -27,9 +27,11 @@ QUARTERS = T2 // BANK
 LAST = R_TILES - 1
 PAGES = 2
 STORED_BUFS = 3
-SUM_BANKS = ("sum0", "sum1", "sum2", "sum3")
+H_AT = (0, 3584)
+CODES_AT = {1: 0, 2: 2048, 3: 6656, 4: 0, 5: 6656, 6: 0, 7: 6656}
+PAIRS = (("work0", "work1"), ("work2", "work3"))
 BACK_BANKS = ("back0", "back1")
-PROD_BANKS = ("prod0", "prod1")
+SPARE_BANKS = ("spare0", "spare1")
 
 
 def tile_list_eclipse_shed_planner_kernel(
@@ -38,6 +40,7 @@ def tile_list_eclipse_shed_planner_kernel(
     nc = tc.nc
     with ExitStack() as ctx:
         keep = ctx.enter_context(tc.tile_pool(name="keep", bufs=1))
+        chain = ctx.enter_context(tc.tile_pool(name="chain", bufs=1))
         psum = ctx.enter_context(tc.psum_pool(name="psum", bufs=1))
 
         def sb(name, shape, dtype, tag=None):
@@ -105,18 +108,14 @@ def tile_list_eclipse_shed_planner_kernel(
         load_w1((2, 3), ("rawC", "rawD"))
         load_stored(0)
 
-        pages = [sb(f"page{b}", [P, T2], F32) for b in range(PAGES)]
-        for page in pages:
-            nc.gpsimd.memset(page[:], 0.0)
+        pages = [sb("page0", [P, T2], F32)]
+        nc.gpsimd.memset(pages[0][:], 0.0)
         w4_plane = sb("w4_plane", [P, PASSES, N], U8)
         nc.gpsimd.memset(w4_plane[:].bitcast(I32), 0)
-        w4_fold = sb("w4_fold", [P, 5, 2 * P], U8)
+        w4_fold = sb("w4_fold", [P, 4, 2 * P], U8)
         nc.gpsimd.memset(w4_fold[:].bitcast(I32), 0)
-        w4_fold_plane = sb("w4_fold_plane", [P, 5, P], U8)
+        w4_fold_plane = sb("w4_fold_plane", [P, 4, P], U8)
         nc.gpsimd.memset(w4_fold_plane[:].bitcast(I32), 0)
-        z_turned = [sb(f"zt{q}", [P, 4, 2, LAST * QUAD, 2], BF16) for q in range(QUARTERS)]
-        zb_codes = sb("zb_codes", [P, QUARTERS, BANK], U32)
-        zb_scales = sb("zb_scales", [P, QUARTERS, BANK], U8)
 
         nc.scalar.copy(rows[0:20, :], vectors[:])
         turned = bank_tile("turned", [P, P], BACK_BANKS[0])
@@ -136,10 +135,15 @@ def tile_list_eclipse_shed_planner_kernel(
                     grouped[:, 4 * P * a : 4 * P * (a + 1)].rearrange("p (c i) -> p c i", i=4), w1_raw[j, a].rearrange("p i c -> p c i")
                 )
 
+        def link(name, shape, dtype, offset):
+            return chain.tile(shape, dtype, name=name, align_bytes=64, offset=offset)
+
         def quantise_w1(j):
-            slot = j % 2 if j < 3 else 1
-            w1_codes[j] = sb(f"w1c{j}", [P, PASSES * P], U32, f"w1c{slot}")
-            w1_scales[j] = sb(f"w1s{j}", [P, PASSES * P], U8, f"w1s{slot}")
+            if j == 0:
+                w1_codes[j] = sb("w1c0", [P, PASSES * P], U32)
+            else:
+                w1_codes[j] = link(f"w1c{j}", [P, PASSES * P], U32, CODES_AT[j])
+            w1_scales[j] = sb(f"w1s{j}", [P, PASSES * P], U8, {2: "w1s_first", 5: "w1s5", 6: "w1s6", LAST: "w1s_last"}.get(j, f"w1s{j % 2}"))
             nc.vector.quantize_mx(out=w1_codes[j][:].bitcast(FP8X4), scales=w1_scales[j][:], in_=w1_grouped[j][:])
 
         v_codes = [sb(f"v_codes{a}", [P, S], U32) for a in range(PASSES)]
@@ -148,7 +152,7 @@ def tile_list_eclipse_shed_planner_kernel(
 
         def first_product(j):
             for half in range(2):
-                d_acc[j, half] = bank_tile(f"dacc{j}_{half}", [P, BANK], PROD_BANKS[half])
+                d_acc[j, half] = bank_tile(f"dacc{j}_{half}", [P, BANK], PAIRS[j % 2][half])
             order = [(half, a) for a in range(PASSES) for half in range(2)] if j == 0 else [(half, a) for half in range(2) for a in range(PASSES)]
             for half, a in order:
                 span = slice(BANK * half, BANK * (half + 1))
@@ -165,9 +169,11 @@ def tile_list_eclipse_shed_planner_kernel(
         h_sb = {}
 
         def fetch_product(j, tag):
-            h_sb[j] = sb(f"h{j}", [P, S], F32, tag)
+            d_sb = sb(f"d{j}", [P, S], F32, tag)
             for half in range(2):
-                nc.scalar.copy(h_sb[j][:, BANK * half : BANK * (half + 1)], d_acc[j, half][:])
+                nc.scalar.copy(d_sb[:, BANK * half : BANK * (half + 1)], d_acc[j, half][:])
+            h_sb[j] = link(f"h{j}", [P, S], F32, H_AT[j % 2])
+            clamp(j, h_sb[j][:], d_sb[:])
 
         def clamp(j, dst, src):
             nc.vector.tensor_scalar(dst, src, cols[:, j : j + 1], cols[:, 8 + j : 9 + j], ALU.max, ALU.min)
@@ -178,62 +184,67 @@ def tile_list_eclipse_shed_planner_kernel(
 
         sums = {}
 
+        def sum_bank(j, q):
+            return PAIRS[(j + q // 2) % 2][q % 2]
+
         def turn_stored(j, q):
-            sums[j, q] = bank_tile(f"sum{j}_{q}", [P, 4, P], SUM_BANKS[q])
+            sums[j, q] = bank_tile(f"sum{j}_{q}", [P, 4, P], sum_bank(j, q))
             for tt in range(4):
                 t0 = BANK * q + P * tt
                 nc.tensor.matmul(sums[j, q][:, tt, :], stored_sb[j][:, t0 : t0 + P], ident[:], start=(tt == 0), stop=False, is_transpose=True)
 
-        z_fold = {}
+        z_turned = {}
 
         def add_page(j, q):
             bank = sums[j, q]
             for tt in range(4):
                 t0 = BANK * q + P * tt
                 nc.tensor.matmul(bank[:, tt, :], pages[j % PAGES][:, t0 : t0 + P], ident[:], start=False, stop=(tt == 3), is_transpose=True)
-            if j < LAST:
-                dst = z_turned[q][:, :, :, QUAD * j : QUAD * (j + 1), :]
-                nc.scalar.copy(dst, bank[:].rearrange("t s (p u e) -> t s u p e", u=2, e=2))
-            else:
-                z_fold[q] = sb(f"zfold{q}", [P, 2, 4, QUAD, 2], BF16)
-                nc.scalar.copy(z_fold[q][:], bank[:].rearrange("t s (p u e) -> t u s p e", u=2, e=2))
+            z_turned[j, q] = sb(f"zt{j}_{q}", [P, 2, 4, QUAD, 2], BF16, f"zt{j % 2}_{q}")
+            nc.scalar.copy(z_turned[j, q][:], bank[:].rearrange("t s (p u e) -> t u s p e", u=2, e=2))
 
         z_grouped = {}
+        fold_codes = {}
+        fold_scales = {}
 
-        def turn_back(a, q, banks):
-            first = 3 * QUAD * a
-            pairs = z_turned[q][:].rearrange("t s u p e -> t (s u p e)").bitcast(F32).rearrange("t (s u p) -> t s u p", s=4, u=2)
-            grouped = sb(f"zg{a}_{q}", [P, 4 * BANK], BF16, f"zg{q}")
-            z_grouped[a, q] = grouped
+        def turn_back(j, quarters, tag):
+            if quarters[0] == 0:
+                z_grouped[j] = sb(f"zg{j}", [P, T2], BF16, f"zg{j % 3}")
+            bank = bank_tile(f"back{j}_{quarters[0]}", [P, len(quarters), 2, P], tag)
+            for place, q in enumerate(quarters):
+                pairs = z_turned[j, q][:].rearrange("t u s p e -> t (u s p e)").bitcast(F32).rearrange("t (u c) -> t u c", u=2)
+                for u in range(2):
+                    nc.tensor.transpose(bank[:, place, u, :], pairs[:, u, :], ident[:])
+            words = z_grouped[j][:, BANK * quarters[0] : BANK * (quarters[-1] + 1)].bitcast(F32)
+            nc.scalar.copy(words.rearrange("p (q t u) -> p q t u", t=P, u=2), bank[:].rearrange("p q u t -> p q t u"))
+
+        def quantise_z(j, q0, q1):
+            if q0 == 0:
+                fold_codes[j] = sb(f"fold_codes{j}", [P, QUARTERS * P], U32, f"fold_codes{j % 3}")
+                fold_scales[j] = sb(f"fold_scales{j}", [P, QUARTERS * P], U8, f"fold_scales{j % 3}")
+            nc.vector.quantize_mx(
+                out=fold_codes[j][:, P * q0 : P * q1].bitcast(FP8X4),
+                scales=fold_scales[j][:, P * q0 : P * q1],
+                in_=z_grouped[j][:, BANK * q0 : BANK * q1],
+            )
+
+        def unfold(j):
+            a, quad = divmod(j, 4)
+            for s in range(4):
+                nc.sync.dma_start(
+                    z_codes[a][QUAD * quad : QUAD * (quad + 1), :, P * s : P * (s + 1)].bitcast(I32),
+                    fold_codes[j][QUAD * s : QUAD * (s + 1), :].bitcast(I32).rearrange("p (q c) -> p q c", q=QUARTERS),
+                )
+                nc.sync.dma_start(
+                    z_scales[a][QUAD * quad : QUAD * quad + 4, :, P * s : P * (s + 1)].bitcast(I32),
+                    fold_scales[j][QUAD * s : QUAD * s + 4, :].bitcast(I32).rearrange("p (q c) -> p q c", q=QUARTERS),
+                )
+
+        def finish_z(j):
             for half in range(2):
-                bank = bank_tile(f"back{a}_{q}_{half}", [P, 2, 256], banks[half])
-                for s in range(2):
-                    for u in range(2):
-                        nc.tensor.transpose(bank[:, u, P * s : P * (s + 1)], pairs[:, 2 * half + s, u, first : first + P], ident[:])
-                words = grouped[:, 1024 * half : 1024 * (half + 1)].bitcast(F32)
-                nc.scalar.copy(words.rearrange("p (t u) -> p t u", u=2), bank[:].rearrange("p u t -> p t u"))
-
-        z_codes = {}
-        z_scales = {}
-
-        def quantise_z(a, q):
-            if a == 0:
-                z_codes[a, q], z_scales[a, q] = sb(f"za_codes{q}", [P, BANK], U32)[:], sb(f"za_scales{q}", [P, BANK], U8)[:]
-            else:
-                z_codes[a, q], z_scales[a, q] = zb_codes[:, q, :], zb_scales[:, q, :]
-            nc.vector.quantize_mx(out=z_codes[a, q].bitcast(FP8X4), scales=z_scales[a, q], in_=z_grouped[a, q][:])
-
-        fold_codes = sb("fold_codes", [P, QUARTERS, P], U32)
-        fold_scales = sb("fold_scales", [P, QUARTERS, P], U8)
-
-        def turn_back_fold(q):
-            pairs = z_fold[q][:].rearrange("t u s p e -> t (u s p e)").bitcast(F32).rearrange("t (u c) -> t u c", u=2)
-            bank = bank_tile(f"backfold{q}", [P, 2, P], SUM_BANKS[q])
-            for u in range(2):
-                nc.tensor.transpose(bank[:, u, :], pairs[:, u, :], ident[:])
-            grouped = sb(f"zgfold{q}", [P, 4 * P], BF16)
-            nc.scalar.copy(grouped[:].bitcast(F32).rearrange("p (t u) -> p t u", u=2), bank[:].rearrange("p u t -> p t u"))
-            nc.vector.quantize_mx(out=fold_codes[:, q, :].bitcast(FP8X4), scales=fold_scales[:, q, :], in_=grouped[:])
+                turn_back(j, (2 * half, 2 * half + 1), BACK_BANKS[half])
+            quantise_z(j, 0, QUARTERS)
+            unfold(j)
 
         y_sb = {}
         y_acc = {}
@@ -241,16 +252,12 @@ def tile_list_eclipse_shed_planner_kernel(
         def second_pass(n, q, a, bank=None, stop=False):
             if bank:
                 y_acc[n, q] = bank_tile(f"yacc{n}_{q}", [P, BANK], bank)
-            if (n, a) == (0, 1):
-                weight, plane = w4_fold[:, 4, :], w4_fold_plane[:, 4, :]
-            else:
-                weight, plane = w4_sb[:, a, 2 * P * n : 2 * P * (n + 1)], w4_plane[:, a, P * n : P * (n + 1)]
             nc.tensor.matmul_mx(
                 out=y_acc[n, q][:],
-                lhsT=weight.bitcast(FP4X4),
-                lhsT_scale=plane,
-                rhs=z_codes[a, q].bitcast(FP8X4),
-                rhs_scale=z_scales[a, q],
+                lhsT=w4_sb[:, a, 2 * P * n : 2 * P * (n + 1)].bitcast(FP4X4),
+                lhsT_scale=w4_plane[:, a, P * n : P * (n + 1)],
+                rhs=z_codes[a][:, q, :].bitcast(FP8X4),
+                rhs_scale=z_scales[a][:, q, :],
                 start=bool(bank),
                 stop=stop,
             )
@@ -261,8 +268,8 @@ def tile_list_eclipse_shed_planner_kernel(
                     out=y_acc[0, q][:, P * s : P * (s + 1)],
                     lhsT=w4_fold[:, s, :].bitcast(FP4X4),
                     lhsT_scale=w4_fold_plane[:, s, :],
-                    rhs=fold_codes[:, q, :].bitcast(FP8X4),
-                    rhs_scale=fold_scales[:, q, :],
+                    rhs=fold_codes[LAST][:, P * q : P * (q + 1)].bitcast(FP8X4),
+                    rhs_scale=fold_scales[LAST][:, P * q : P * (q + 1)],
                     start=False,
                     stop=(s == 3),
                 )
@@ -284,36 +291,31 @@ def tile_list_eclipse_shed_planner_kernel(
         for half in range(2):
             listed = idx[:, 32 * half : 32 * (half + 1)]
             nc.vector.tensor_copy(v_codes[1][:, BANK * half : BANK * (half + 1)], words1[:].bitcast(U32).indirect(listed))
-        outs = [None, sb("out1", [P, T2], F32, "wide1")]
-        nc.gpsimd.memset(outs[1][:], 0.0)
+        pages.append(sb("page1", [P, T2], F32, "wide1"))
+        nc.gpsimd.memset(pages[1][:], 0.0)
 
         first_product(0)
-        h_first = sb("h0a", [P, BANK], F32, "h0")
+        h_first = link("h0a", [P, BANK], F32, 0)
         clamp(0, h_first[:], d_acc[0, 0][:])
         scatter_page(0, h_first[:], 0, BANK)
         round_w1(1)
         quantise_w1(1)
-        h_second = sb("h0b", [P, BANK], F32, "rawB")
-        nc.scalar.copy(h_second[:], d_acc[0, 1][:])
-        clamp(0, h_second[:], h_second[:])
+        d_second = sb("d0b", [P, BANK], F32, "rawB")
+        nc.scalar.copy(d_second[:], d_acc[0, 1][:])
+        h_second = link("h0b", [P, BANK], F32, 2048)
+        clamp(0, h_second[:], d_second[:])
         scatter_page(0, h_second[:], BANK, S)
 
         load_stored(1)
         load_w1((4, 5), ("rawA", "rawB"))
         w4_sb = sb("w4_sb", [P, PASSES, 2 * N], U8)
-        nc.sync.dma_start(w4_sb[:, 0, :].bitcast(I32), w4_words[0].bitcast(I32))
+        nc.sync.dma_start(w4_sb[:].bitcast(I32), w4_words.rearrange("a p c -> p a c").bitcast(I32))
         for quad in range(4):
             lanes = slice(QUAD * quad, QUAD * (quad + 1))
             live = slice(QUAD * quad, QUAD * quad + 4)
-            src = (quad + 3) % 4
-            src_lanes = slice(QUAD * src, QUAD * (src + 1))
-            src_live = slice(4 * src, 4 * src + 4)
-            nc.sync.dma_start(w4_plane[live, 0, :].bitcast(I32), w4_scales[0, 4 * quad : 4 * quad + 4, :].bitcast(I32))
-            nc.sync.dma_start(w4_plane[live, 1, :].bitcast(I32), w4_scales[1, src_live, :].bitcast(I32))
-            nc.sync.dma_start(w4_sb[lanes, 1, :].bitcast(I32), w4_words[1, src_lanes, :].bitcast(I32))
-            if quad > 0:
-                nc.sync.dma_start(w4_fold[lanes, 4, :].bitcast(I32), w4_words[1, src_lanes, 0 : 2 * P].bitcast(I32))
-                nc.sync.dma_start(w4_fold_plane[live, 4, :].bitcast(I32), w4_scales[1, src_live, 0:P].bitcast(I32))
+            nc.sync.dma_start(
+                w4_plane[live, :, :].bitcast(I32), w4_scales[:, 4 * quad : 4 * quad + 4, :].rearrange("a r c -> r a c").bitcast(I32)
+            )
             nc.sync.dma_start(w4_fold[lanes, quad, :].bitcast(I32), w4_words[1, 3 * QUAD : P, 0 : 2 * P].bitcast(I32))
             nc.sync.dma_start(w4_fold_plane[live, quad, :].bitcast(I32), w4_scales[1, 12:16, 0:P].bitcast(I32))
         load_stored(2)
@@ -324,86 +326,83 @@ def tile_list_eclipse_shed_planner_kernel(
         round_w1(2)
         round_w1(3)
         quantise_w1(2)
-        quantise_w1(3)
         fetch_product(1, "rawC")
-        clamp(1, h_sb[1][:], h_sb[1][:])
-        for q in range(QUARTERS):
-            turn_stored(0, q)
-        first_product(2)
-        fetch_product(2, "h2")
         load_w1((6, 7), ("rawC", "rawD"))
         duty_sb = sb("duty_sb", [P, N_TILES, PICK], F32, "wide0")
         nc.sync.dma_start(duty_sb[:], duty.rearrange("(n p) m -> p n m", p=P))
         wgo_sb = sb("wgo_sb", [P, PICK], F32)
         nc.sync.dma_start(wgo_sb[:], wgo)
 
+        outs = {}
+        z_scales = []
+        z_codes = [sb("za_codes", [P, QUARTERS, BANK], U32)]
         for j in range(1, LAST):
             scatter_page(j, h_sb[j][:], 0, S)
+            if 4 <= j + 2 <= LAST:
+                round_w1(j + 2)
+            first_product(j + 1)
             if j == 1:
-                clamp(2, h_sb[2][:], h_sb[2][:])
-            ahead = j + 2
-            if ahead <= LAST:
-                first_product(ahead)
-                fetch_product(ahead, f"h{ahead % 3}")
-                clamp(ahead, h_sb[ahead][:], h_sb[ahead][:])
-                if ahead < LAST:
-                    round_w1(ahead + 1)
-                    quantise_w1(ahead + 1)
-            if j == 6:
-                turn_back(0, 3, PROD_BANKS)
-                quantise_z(0, 3)
+                z_scales.append(sb("za_scales", [P, QUARTERS, BANK], U8, "w1s_first"))
+                nc.gpsimd.memset(z_scales[0][:].bitcast(I32), 0)
+                z_codes.append(None)
+            if j == 2:
+                z_scales.append(sb("zb_scales", [P, QUARTERS, BANK], U8, "w1s1"))
+                nc.gpsimd.memset(z_scales[1][:].bitcast(I32), 0)
+            if j == 3:
+                z_codes[1] = sb("zb_codes", [P, QUARTERS, BANK], U32, "w1s0")
+                nc.gpsimd.memset(z_codes[1][3 * QUAD : P, :, :].bitcast(I32), 0)
+            if j + 1 == LAST:
+                outs[1] = sb("out1", [P, T2], F32, "w1s_last")
+                nc.gpsimd.memset(outs[1][:], 0.0)
+            fetch_product(j + 1, "h2")
+            if j + 2 <= LAST:
+                quantise_w1(j + 2)
+            if j >= 2:
+                finish_z(j - 2)
             for q in range(QUARTERS):
+                turn_stored(j - 1, q)
                 add_page(j - 1, q)
-            for q in range(QUARTERS):
-                turn_stored(j, q)
             if j + 2 <= LAST:
                 load_stored(j + 2)
-            for q in {4: (2,), 5: (0, 1)}.get(j, ()):
-                turn_back(0, q, BACK_BANKS)
-                quantise_z(0, q)
+        finish_z(5)
+        for q in range(QUARTERS):
+            second_pass(0, q, 0, (SPARE_BANKS + BACK_BANKS)[q])
 
         scatter_page(LAST, h_sb[LAST][:], 0, S)
-        add_page(6, 0)
-        add_page(6, 1)
-        second_pass(0, 0, 0, PROD_BANKS[0])
-        second_pass(0, 1, 0, PROD_BANKS[1])
-        add_page(6, 2)
-        add_page(6, 3)
+        for q in range(QUARTERS):
+            turn_stored(6, q)
+            add_page(6, q)
         outs[0] = sb("out0", [P, T2], F32, "page0")
         nc.gpsimd.memset(outs[0][:], 0.0)
-        for q in range(QUARTERS):
-            turn_back(1, q, BACK_BANKS)
-            quantise_z(1, q)
-            turn_stored(LAST, q)
-        second_pass(0, 2, 0, BACK_BANKS[0])
-        second_pass(0, 3, 0, BACK_BANKS[1])
+        turn_stored(LAST, 3)
+        turn_back(6, (0, 1), sum_bank(6, 0))
+        turn_stored(LAST, 1)
+        turn_back(6, (2, 3), sum_bank(6, 2))
+        quantise_z(6, 0, QUARTERS)
+        unfold(6)
+        turn_stored(LAST, 2)
+        turn_stored(LAST, 0)
 
         for q in range(QUARTERS):
             add_page(LAST, q)
-        second_pass(0, 0, 1)
         for q in range(QUARTERS):
-            turn_back_fold(q)
-        for q in range(1, QUARTERS):
+            turn_back(LAST, (q,), sum_bank(LAST, q))
+            quantise_z(LAST, q, q + 1)
+        for q in range(QUARTERS):
             second_pass(0, q, 1)
         for q in range(QUARTERS):
             fold_passes(q)
             fetch_scores(0, q)
-        for s in range(4):
-            nc.sync.dma_start(
-                zb_codes[0:QUAD, :, P * s : P * (s + 1)].bitcast(I32), fold_codes[QUAD * s : QUAD * (s + 1), :, :].bitcast(I32)
-            )
-            nc.sync.dma_start(
-                zb_scales[0:4, :, P * s : P * (s + 1)].bitcast(I32), fold_scales[QUAD * s : QUAD * s + 4, :, :].bitcast(I32)
-            )
+        unfold(LAST)
 
         for n in range(N_TILES):
             if n + 1 < N_TILES:
-                banks = SUM_BANKS if n % 2 == 0 else PROD_BANKS + BACK_BANKS
+                banks = PAIRS[0] + PAIRS[1] if n % 2 == 0 else SPARE_BANKS + BACK_BANKS
                 for q in range(QUARTERS):
                     second_pass(n + 1, q, 1, banks[q])
                     second_pass(n + 1, q, 0, stop=True)
                     fetch_scores(n + 1, q)
-            x = sb(f"x{n}", [P, PICK], F32, f"h{n % 3}")
+            x = sb(f"x{n}", [P, PICK], F32, f"x{n % 2}")
             nc.vector.tensor_tensor(x[:], y_sb[n][:].indirect(idx3[:]), duty_sb[:, n, :], ALU.add)
             page = outs[n % 2]
             nc.vector.tensor_tensor(page[:].indirect(idx4[:]), x[:], wgo_sb[:], ALU.mult)

@@ -55,7 +55,7 @@ def tile_list_eclipse_shed_planner_kernel(
         make_identity(nc, ident[:])
 
         tab_plane = sb("tab_plane", [P, T], U8)
-        nc.gpsimd.memset(tab_plane[:].bitcast(I32), 0)
+        nc.vector.memset(tab_plane[:].bitcast(I32), 0)
 
         def load_list(src, name):
             tile = keep.tile([P, S // 16], U16, name=name)
@@ -108,14 +108,17 @@ def tile_list_eclipse_shed_planner_kernel(
         load_w1((2, 3), ("rawC", "rawD"))
         load_stored(0)
 
-        pages = [sb("page0", [P, T2], F32)]
-        nc.gpsimd.memset(pages[0][:], 0.0)
+        pages = [sb(f"page{b}", [P, T2], F32) for b in range(PAGES)]
+        for page in pages:
+            nc.vector.memset(page[:], 0.0)
         w4_plane = sb("w4_plane", [P, PASSES, N], U8)
-        nc.gpsimd.memset(w4_plane[:].bitcast(I32), 0)
-        w4_fold = sb("w4_fold", [P, 4, 2 * P], U8)
-        nc.gpsimd.memset(w4_fold[:].bitcast(I32), 0)
-        w4_fold_plane = sb("w4_fold_plane", [P, 4, P], U8)
-        nc.gpsimd.memset(w4_fold_plane[:].bitcast(I32), 0)
+        nc.vector.memset(w4_plane[:].bitcast(I32), 0)
+        w4_fold = sb("w4_fold", [P, 5, 2 * P], U8)
+        nc.vector.memset(w4_fold[:].bitcast(I32), 0)
+        w4_fold_plane = sb("w4_fold_plane", [P, P], U8)
+        nc.vector.memset(w4_fold_plane[:].bitcast(I32), 0)
+        outs = {1: sb("out1", [P, T2], F32)}
+        nc.vector.memset(outs[1][:], 0.0)
 
         nc.scalar.copy(rows[0:20, :], vectors[:])
         turned = bank_tile("turned", [P, P], BACK_BANKS[0])
@@ -143,7 +146,7 @@ def tile_list_eclipse_shed_planner_kernel(
                 w1_codes[j] = sb("w1c0", [P, PASSES * P], U32)
             else:
                 w1_codes[j] = link(f"w1c{j}", [P, PASSES * P], U32, CODES_AT[j])
-            w1_scales[j] = sb(f"w1s{j}", [P, PASSES * P], U8, {2: "w1s_first", 5: "w1s5", 6: "w1s6", LAST: "w1s_last"}.get(j, f"w1s{j % 2}"))
+            w1_scales[j] = sb(f"w1s{j}", [P, PASSES * P], U8, f"w1s{j % 2}")
             nc.vector.quantize_mx(out=w1_codes[j][:].bitcast(FP8X4), scales=w1_scales[j][:], in_=w1_grouped[j][:])
 
         v_codes = [sb(f"v_codes{a}", [P, S], U32) for a in range(PASSES)]
@@ -193,58 +196,49 @@ def tile_list_eclipse_shed_planner_kernel(
                 t0 = BANK * q + P * tt
                 nc.tensor.matmul(sums[j, q][:, tt, :], stored_sb[j][:, t0 : t0 + P], ident[:], start=(tt == 0), stop=False, is_transpose=True)
 
-        z_turned = {}
+        z_turned = [sb(f"zt{q}", [P, 4, 2, LAST * QUAD, 2], BF16) for q in range(QUARTERS)]
+        z_fold = {}
 
         def add_page(j, q):
             bank = sums[j, q]
             for tt in range(4):
                 t0 = BANK * q + P * tt
                 nc.tensor.matmul(bank[:, tt, :], pages[j % PAGES][:, t0 : t0 + P], ident[:], start=False, stop=(tt == 3), is_transpose=True)
-            z_turned[j, q] = sb(f"zt{j}_{q}", [P, 2, 4, QUAD, 2], BF16, f"zt{j % 2}_{q}")
-            nc.scalar.copy(z_turned[j, q][:], bank[:].rearrange("t s (p u e) -> t u s p e", u=2, e=2))
+            if j < LAST:
+                place = (j + 3) % LAST
+                dst = z_turned[q][:, :, :, QUAD * place : QUAD * (place + 1), :]
+                nc.scalar.copy(dst, bank[:].rearrange("t s (p u e) -> t s u p e", u=2, e=2))
+            else:
+                z_fold[q] = sb(f"zfold{q}", [P, 2, 4, QUAD, 2], BF16)
+                nc.scalar.copy(z_fold[q][:], bank[:].rearrange("t s (p u e) -> t u s p e", u=2, e=2))
 
-        z_grouped = {}
-        fold_codes = {}
-        fold_scales = {}
+        z_codes = [sb(f"z_codes{a}", [P, QUARTERS, BANK], U32) for a in range(PASSES)]
+        z_scales = [sb(f"z_scales{a}", [P, QUARTERS, BANK], U8) for a in range(PASSES)]
 
-        def turn_back(j, quarters, tag):
-            if quarters[0] == 0:
-                z_grouped[j] = sb(f"zg{j}", [P, T2], BF16, f"zg{j % 3}")
-            bank = bank_tile(f"back{j}_{quarters[0]}", [P, len(quarters), 2, P], tag)
-            for place, q in enumerate(quarters):
-                pairs = z_turned[j, q][:].rearrange("t u s p e -> t (u s p e)").bitcast(F32).rearrange("t (u c) -> t u c", u=2)
-                for u in range(2):
-                    nc.tensor.transpose(bank[:, place, u, :], pairs[:, u, :], ident[:])
-            words = z_grouped[j][:, BANK * quarters[0] : BANK * (quarters[-1] + 1)].bitcast(F32)
-            nc.scalar.copy(words.rearrange("p (q t u) -> p q t u", t=P, u=2), bank[:].rearrange("p q u t -> p q t u"))
-
-        def quantise_z(j, q0, q1):
-            if q0 == 0:
-                fold_codes[j] = sb(f"fold_codes{j}", [P, QUARTERS * P], U32, f"fold_codes{j % 3}")
-                fold_scales[j] = sb(f"fold_scales{j}", [P, QUARTERS * P], U8, f"fold_scales{j % 3}")
-            nc.vector.quantize_mx(
-                out=fold_codes[j][:, P * q0 : P * q1].bitcast(FP8X4),
-                scales=fold_scales[j][:, P * q0 : P * q1],
-                in_=z_grouped[j][:, BANK * q0 : BANK * q1],
-            )
-
-        def unfold(j):
-            a, quad = divmod(j, 4)
-            for s in range(4):
-                nc.sync.dma_start(
-                    z_codes[a][QUAD * quad : QUAD * (quad + 1), :, P * s : P * (s + 1)].bitcast(I32),
-                    fold_codes[j][QUAD * s : QUAD * (s + 1), :].bitcast(I32).rearrange("p (q c) -> p q c", q=QUARTERS),
-                )
-                nc.sync.dma_start(
-                    z_scales[a][QUAD * quad : QUAD * quad + 4, :, P * s : P * (s + 1)].bitcast(I32),
-                    fold_scales[j][QUAD * s : QUAD * s + 4, :].bitcast(I32).rearrange("p (q c) -> p q c", q=QUARTERS),
-                )
-
-        def finish_z(j):
+        def finish_z(a, q, banks):
+            first = 3 * QUAD * (1 - a)
+            pairs = z_turned[q][:].rearrange("t s u p e -> t (s u p e)").bitcast(F32).rearrange("t (s u p) -> t s u p", s=4, u=2)
+            grouped = sb(f"zg{a}_{q}", [P, 4 * BANK], BF16, f"zg{q}")
             for half in range(2):
-                turn_back(j, (2 * half, 2 * half + 1), BACK_BANKS[half])
-            quantise_z(j, 0, QUARTERS)
-            unfold(j)
+                bank = bank_tile(f"back{a}_{q}_{half}", [P, 2, 256], banks[half])
+                for s in range(2):
+                    for u in range(2):
+                        nc.tensor.transpose(bank[:, u, P * s : P * (s + 1)], pairs[:, 2 * half + s, u, first : first + P], ident[:])
+                words = grouped[:, 1024 * half : 1024 * (half + 1)].bitcast(F32)
+                nc.scalar.copy(words.rearrange("p (t u) -> p t u", u=2), bank[:].rearrange("p u t -> p t u"))
+            nc.vector.quantize_mx(out=z_codes[a][:, q, :].bitcast(FP8X4), scales=z_scales[a][:, q, :], in_=grouped[:])
+
+        fold_codes = sb("fold_codes", [P, QUARTERS, P], U32)
+        fold_scales = sb("fold_scales", [P, QUARTERS, P], U8)
+
+        def finish_fold(q):
+            pairs = z_fold[q][:].rearrange("t u s p e -> t (u s p e)").bitcast(F32).rearrange("t (u c) -> t u c", u=2)
+            bank = bank_tile(f"backfold{q}", [P, 2, P], sum_bank(LAST, q))
+            for u in range(2):
+                nc.tensor.transpose(bank[:, u, :], pairs[:, u, :], ident[:])
+            grouped = sb(f"zgfold{q}", [P, 4 * P], BF16)
+            nc.scalar.copy(grouped[:].bitcast(F32).rearrange("p (t u) -> p t u", u=2), bank[:].rearrange("p u t -> p t u"))
+            nc.vector.quantize_mx(out=fold_codes[:, q, :].bitcast(FP8X4), scales=fold_scales[:, q, :], in_=grouped[:])
 
         y_sb = {}
         y_acc = {}
@@ -254,7 +248,7 @@ def tile_list_eclipse_shed_planner_kernel(
                 y_acc[n, q] = bank_tile(f"yacc{n}_{q}", [P, BANK], bank)
             nc.tensor.matmul_mx(
                 out=y_acc[n, q][:],
-                lhsT=w4_sb[:, a, 2 * P * n : 2 * P * (n + 1)].bitcast(FP4X4),
+                lhsT=(w4_fold[:, 4, :] if (n, a) == (0, 1) else w4_sb[:, a, 2 * P * n : 2 * P * (n + 1)]).bitcast(FP4X4),
                 lhsT_scale=w4_plane[:, a, P * n : P * (n + 1)],
                 rhs=z_codes[a][:, q, :].bitcast(FP8X4),
                 rhs_scale=z_scales[a][:, q, :],
@@ -267,9 +261,9 @@ def tile_list_eclipse_shed_planner_kernel(
                 nc.tensor.matmul_mx(
                     out=y_acc[0, q][:, P * s : P * (s + 1)],
                     lhsT=w4_fold[:, s, :].bitcast(FP4X4),
-                    lhsT_scale=w4_fold_plane[:, s, :],
-                    rhs=fold_codes[LAST][:, P * q : P * (q + 1)].bitcast(FP8X4),
-                    rhs_scale=fold_scales[LAST][:, P * q : P * (q + 1)],
+                    lhsT_scale=w4_fold_plane[:],
+                    rhs=fold_codes[:, q, :].bitcast(FP8X4),
+                    rhs_scale=fold_scales[:, q, :],
                     start=False,
                     stop=(s == 3),
                 )
@@ -291,8 +285,6 @@ def tile_list_eclipse_shed_planner_kernel(
         for half in range(2):
             listed = idx[:, 32 * half : 32 * (half + 1)]
             nc.vector.tensor_copy(v_codes[1][:, BANK * half : BANK * (half + 1)], words1[:].bitcast(U32).indirect(listed))
-        pages.append(sb("page1", [P, T2], F32, "wide1"))
-        nc.gpsimd.memset(pages[1][:], 0.0)
 
         first_product(0)
         h_first = link("h0a", [P, BANK], F32, 0)
@@ -317,7 +309,8 @@ def tile_list_eclipse_shed_planner_kernel(
                 w4_plane[live, :, :].bitcast(I32), w4_scales[:, 4 * quad : 4 * quad + 4, :].rearrange("a r c -> r a c").bitcast(I32)
             )
             nc.sync.dma_start(w4_fold[lanes, quad, :].bitcast(I32), w4_words[1, 3 * QUAD : P, 0 : 2 * P].bitcast(I32))
-            nc.sync.dma_start(w4_fold_plane[live, quad, :].bitcast(I32), w4_scales[1, 12:16, 0:P].bitcast(I32))
+            nc.sync.dma_start(w4_fold_plane[live, :].bitcast(I32), w4_scales[1, 12:16, 0:P].bitcast(I32))
+        nc.sync.dma_start(w4_fold[0 : 3 * QUAD, 4, :].bitcast(I32), w4_words[1, 0 : 3 * QUAD, 0 : 2 * P].bitcast(I32))
         load_stored(2)
         idx3 = load_list(offs3, "idx3")
         idx4 = load_list(offs4, "idx4")
@@ -333,67 +326,54 @@ def tile_list_eclipse_shed_planner_kernel(
         wgo_sb = sb("wgo_sb", [P, PICK], F32)
         nc.sync.dma_start(wgo_sb[:], wgo)
 
-        outs = {}
-        z_scales = []
-        z_codes = [sb("za_codes", [P, QUARTERS, BANK], U32)]
         for j in range(1, LAST):
             scatter_page(j, h_sb[j][:], 0, S)
             if 4 <= j + 2 <= LAST:
                 round_w1(j + 2)
             first_product(j + 1)
-            if j == 1:
-                z_scales.append(sb("za_scales", [P, QUARTERS, BANK], U8, "w1s_first"))
-                nc.gpsimd.memset(z_scales[0][:].bitcast(I32), 0)
-                z_codes.append(None)
-            if j == 2:
-                z_scales.append(sb("zb_scales", [P, QUARTERS, BANK], U8, "w1s1"))
-                nc.gpsimd.memset(z_scales[1][:].bitcast(I32), 0)
-            if j == 3:
-                z_codes[1] = sb("zb_codes", [P, QUARTERS, BANK], U32, "w1s0")
-                nc.gpsimd.memset(z_codes[1][3 * QUAD : P, :, :].bitcast(I32), 0)
-            if j + 1 == LAST:
-                outs[1] = sb("out1", [P, T2], F32, "w1s_last")
-                nc.gpsimd.memset(outs[1][:], 0.0)
             fetch_product(j + 1, "h2")
             if j + 2 <= LAST:
                 quantise_w1(j + 2)
-            if j >= 2:
-                finish_z(j - 2)
+            if j >= 5:
+                finish_z(0, 2 * (j - 5), BACK_BANKS)
+                finish_z(0, 2 * (j - 5) + 1, SPARE_BANKS)
             for q in range(QUARTERS):
                 turn_stored(j - 1, q)
                 add_page(j - 1, q)
             if j + 2 <= LAST:
                 load_stored(j + 2)
-        finish_z(5)
-        for q in range(QUARTERS):
-            second_pass(0, q, 0, (SPARE_BANKS + BACK_BANKS)[q])
 
         scatter_page(LAST, h_sb[LAST][:], 0, S)
+        second_pass(0, 0, 0, SPARE_BANKS[0])
+        second_pass(0, 1, 0, SPARE_BANKS[1])
         for q in range(QUARTERS):
             turn_stored(6, q)
             add_page(6, q)
         outs[0] = sb("out0", [P, T2], F32, "page0")
-        nc.gpsimd.memset(outs[0][:], 0.0)
-        turn_stored(LAST, 3)
-        turn_back(6, (0, 1), sum_bank(6, 0))
-        turn_stored(LAST, 1)
-        turn_back(6, (2, 3), sum_bank(6, 2))
-        quantise_z(6, 0, QUARTERS)
-        unfold(6)
-        turn_stored(LAST, 2)
-        turn_stored(LAST, 0)
+        nc.vector.memset(outs[0][:], 0.0)
+        for q in range(QUARTERS):
+            finish_z(1, q, BACK_BANKS)
+            turn_stored(LAST, (q + 2) % QUARTERS)
+        second_pass(0, 2, 0, BACK_BANKS[0])
+        second_pass(0, 3, 0, BACK_BANKS[1])
 
         for q in range(QUARTERS):
             add_page(LAST, q)
+        second_pass(0, 0, 1)
         for q in range(QUARTERS):
-            turn_back(LAST, (q,), sum_bank(LAST, q))
-            quantise_z(LAST, q, q + 1)
-        for q in range(QUARTERS):
+            finish_fold(q)
+        for q in range(1, QUARTERS):
             second_pass(0, q, 1)
         for q in range(QUARTERS):
             fold_passes(q)
             fetch_scores(0, q)
-        unfold(LAST)
+        for s in range(4):
+            nc.sync.dma_start(
+                z_codes[1][3 * QUAD : P, :, P * s : P * (s + 1)].bitcast(I32), fold_codes[QUAD * s : QUAD * (s + 1), :, :].bitcast(I32)
+            )
+            nc.sync.dma_start(
+                z_scales[1][3 * QUAD : 3 * QUAD + 4, :, P * s : P * (s + 1)].bitcast(I32), fold_scales[QUAD * s : QUAD * s + 4, :, :].bitcast(I32)
+            )
 
         for n in range(N_TILES):
             if n + 1 < N_TILES:

@@ -27,8 +27,7 @@ QUARTERS = T2 // BANK
 LAST = R_TILES - 1
 PAGES = 2
 STORED_BUFS = 3
-H_AT = (0, 3584)
-CODES_AT = {1: 0, 2: 2048, 3: 6656, 4: 0, 5: 6656, 6: 0, 7: 6656}
+FIRST_HALF_AT, SECOND_HALF_AT, H1_AT, H2_AT = 0, 2048, 4096, 8192
 PAIRS = (("work0", "work1"), ("work2", "work3"))
 BACK_BANKS = ("back0", "back1")
 SPARE_BANKS = ("spare0", "spare1")
@@ -71,10 +70,10 @@ def tile_list_eclipse_shed_planner_kernel(
 
         def load_w1(tiles, tags):
             c0, width = P * tiles[0], P * len(tiles)
-            if len(tiles) == 1:
-                both = sb(f"w1raw{tiles[0]}", [P, PASSES, 4, P], F32, tags[0])
+            if len(tags) == 1:
+                both = sb(f"w1raw{tiles[0]}", [P, PASSES, 4, width], F32, tags[0])
             for a in range(PASSES):
-                if len(tiles) == 1:
+                if len(tags) == 1:
                     raw = both[:, a, :, :]
                 else:
                     raw = sb(f"w1raw{tiles[0]}_{a}", [P, 4, width], F32, tags[a])[:]
@@ -112,13 +111,13 @@ def tile_list_eclipse_shed_planner_kernel(
         for page in pages:
             nc.vector.memset(page[:], 0.0)
         w4_plane = sb("w4_plane", [P, PASSES, N], U8)
-        nc.vector.memset(w4_plane[:].bitcast(I32), 0)
+        nc.gpsimd.memset(w4_plane[:].bitcast(I32), 0)
         w4_fold = sb("w4_fold", [P, 5, 2 * P], U8)
-        nc.vector.memset(w4_fold[:].bitcast(I32), 0)
+        nc.gpsimd.memset(w4_fold[:].bitcast(I32), 0)
         w4_fold_plane = sb("w4_fold_plane", [P, P], U8)
-        nc.vector.memset(w4_fold_plane[:].bitcast(I32), 0)
+        nc.gpsimd.memset(w4_fold_plane[:].bitcast(I32), 0)
         outs = {1: sb("out1", [P, T2], F32)}
-        nc.vector.memset(outs[1][:], 0.0)
+        nc.gpsimd.memset(outs[1][:], 0.0)
 
         nc.scalar.copy(rows[0:20, :], vectors[:])
         turned = bank_tile("turned", [P, P], BACK_BANKS[0])
@@ -131,7 +130,10 @@ def tile_list_eclipse_shed_planner_kernel(
         w1_scales = {}
 
         def round_w1(j):
-            grouped = sb(f"w1g{j}", [P, PASSES * P * 4], BF16, f"w1g{j % 2}")
+            if j == 4:
+                grouped = link("w1g4", [P, PASSES * P * 4], BF16, H2_AT)
+            else:
+                grouped = sb(f"w1g{j}", [P, PASSES * P * 4], BF16, f"w1g{j % 2}")
             w1_grouped[j] = grouped
             for a in range(PASSES):
                 nc.scalar.copy(
@@ -145,7 +147,7 @@ def tile_list_eclipse_shed_planner_kernel(
             if j == 0:
                 w1_codes[j] = sb("w1c0", [P, PASSES * P], U32)
             else:
-                w1_codes[j] = link(f"w1c{j}", [P, PASSES * P], U32, CODES_AT[j])
+                w1_codes[j] = link(f"w1c{j}", [P, PASSES * P], U32, FIRST_HALF_AT if j == 1 else SECOND_HALF_AT + 1024 * (j % 2))
             w1_scales[j] = sb(f"w1s{j}", [P, PASSES * P], U8, f"w1s{j % 2}")
             nc.vector.quantize_mx(out=w1_codes[j][:].bitcast(FP8X4), scales=w1_scales[j][:], in_=w1_grouped[j][:])
 
@@ -175,7 +177,9 @@ def tile_list_eclipse_shed_planner_kernel(
             d_sb = sb(f"d{j}", [P, S], F32, tag)
             for half in range(2):
                 nc.scalar.copy(d_sb[:, BANK * half : BANK * (half + 1)], d_acc[j, half][:])
-            h_sb[j] = link(f"h{j}", [P, S], F32, H_AT[j % 2])
+            if j == 2:
+                quantise_w1(4)
+            h_sb[j] = link(f"h{j}", [P, S], F32, (H1_AT, H2_AT)[j - 1]) if j <= 2 else d_sb
             clamp(j, h_sb[j][:], d_sb[:])
 
         def clamp(j, dst, src):
@@ -188,7 +192,7 @@ def tile_list_eclipse_shed_planner_kernel(
         sums = {}
 
         def sum_bank(j, q):
-            return PAIRS[(j + q // 2) % 2][q % 2]
+            return PAIRS[(j + 1 + q // 2) % 2][q % 2]
 
         def turn_stored(j, q):
             sums[j, q] = bank_tile(f"sum{j}_{q}", [P, 4, P], sum_bank(j, q))
@@ -287,19 +291,19 @@ def tile_list_eclipse_shed_planner_kernel(
             nc.vector.tensor_copy(v_codes[1][:, BANK * half : BANK * (half + 1)], words1[:].bitcast(U32).indirect(listed))
 
         first_product(0)
-        h_first = link("h0a", [P, BANK], F32, 0)
+        h_first = link("h0a", [P, BANK], F32, FIRST_HALF_AT)
         clamp(0, h_first[:], d_acc[0, 0][:])
         scatter_page(0, h_first[:], 0, BANK)
         round_w1(1)
         quantise_w1(1)
         d_second = sb("d0b", [P, BANK], F32, "rawB")
         nc.scalar.copy(d_second[:], d_acc[0, 1][:])
-        h_second = link("h0b", [P, BANK], F32, 2048)
-        clamp(0, h_second[:], d_second[:])
-        scatter_page(0, h_second[:], BANK, S)
+        h_second = link("h0b", [P, BANK + 16], F32, SECOND_HALF_AT)
+        clamp(0, h_second[:, 0:BANK], d_second[:])
+        scatter_page(0, h_second[:, 0:BANK], BANK, S)
 
+        load_w1((4, 5, 6, 7), ("wide1",))
         load_stored(1)
-        load_w1((4, 5), ("rawA", "rawB"))
         w4_sb = sb("w4_sb", [P, PASSES, 2 * N], U8)
         nc.sync.dma_start(w4_sb[:].bitcast(I32), w4_words.rearrange("a p c -> p a c").bitcast(I32))
         for quad in range(4):
@@ -318,9 +322,9 @@ def tile_list_eclipse_shed_planner_kernel(
         first_product(1)
         round_w1(2)
         round_w1(3)
-        quantise_w1(2)
         fetch_product(1, "rawC")
-        load_w1((6, 7), ("rawC", "rawD"))
+        quantise_w1(2)
+        quantise_w1(3)
         duty_sb = sb("duty_sb", [P, N_TILES, PICK], F32, "wide0")
         nc.sync.dma_start(duty_sb[:], duty.rearrange("(n p) m -> p n m", p=P))
         wgo_sb = sb("wgo_sb", [P, PICK], F32)
@@ -328,12 +332,14 @@ def tile_list_eclipse_shed_planner_kernel(
 
         for j in range(1, LAST):
             scatter_page(j, h_sb[j][:], 0, S)
-            if 4 <= j + 2 <= LAST:
-                round_w1(j + 2)
-            first_product(j + 1)
-            fetch_product(j + 1, "h2")
-            if j + 2 <= LAST:
-                quantise_w1(j + 2)
+            if j + 3 <= LAST:
+                round_w1(j + 3)
+            for ahead in (2, 3) if j == 1 else (j + 2,):
+                if ahead <= LAST:
+                    first_product(ahead)
+                    fetch_product(ahead, f"h{ahead % 3}")
+            if 4 < j + 3 <= LAST:
+                quantise_w1(j + 3)
             if j >= 5:
                 finish_z(0, 2 * (j - 5), BACK_BANKS)
                 finish_z(0, 2 * (j - 5) + 1, SPARE_BANKS)
@@ -382,7 +388,7 @@ def tile_list_eclipse_shed_planner_kernel(
                     second_pass(n + 1, q, 1, banks[q])
                     second_pass(n + 1, q, 0, stop=True)
                     fetch_scores(n + 1, q)
-            x = sb(f"x{n}", [P, PICK], F32, f"x{n % 2}")
+            x = sb(f"x{n}", [P, PICK], F32, f"h{n % 3}")
             nc.vector.tensor_tensor(x[:], y_sb[n][:].indirect(idx3[:]), duty_sb[:, n, :], ALU.add)
             page = outs[n % 2]
             nc.vector.tensor_tensor(page[:].indirect(idx4[:]), x[:], wgo_sb[:], ALU.mult)

@@ -28,6 +28,7 @@ LAST = R_TILES - 1
 PAGES = 2
 STORED_BUFS = 3
 FIRST_HALF_AT, SECOND_HALF_AT, H1_AT, H2_AT = 0, 2048, 4096, 8192
+H_AT = {1: H1_AT, 2: H2_AT, LAST: H1_AT}
 PAIRS = (("work0", "work1"), ("work2", "work3"))
 BACK_BANKS = ("back0", "back1")
 SPARE_BANKS = ("spare0", "spare1")
@@ -116,8 +117,9 @@ def tile_list_eclipse_shed_planner_kernel(
         nc.gpsimd.memset(w4_fold[:].bitcast(I32), 0)
         w4_fold_plane = sb("w4_fold_plane", [P, P], U8)
         nc.gpsimd.memset(w4_fold_plane[:].bitcast(I32), 0)
-        outs = {1: sb("out1", [P, T2], F32)}
+        outs = [sb(f"out{b}", [P, T2], F32) for b in range(2)]
         nc.gpsimd.memset(outs[1][:], 0.0)
+        nc.gpsimd.memset(outs[0][:], 0.0)
 
         nc.scalar.copy(rows[0:20, :], vectors[:])
         turned = bank_tile("turned", [P, P], BACK_BANKS[0])
@@ -179,7 +181,7 @@ def tile_list_eclipse_shed_planner_kernel(
                 nc.scalar.copy(d_sb[:, BANK * half : BANK * (half + 1)], d_acc[j, half][:])
             if j == 2:
                 quantise_w1(4)
-            h_sb[j] = link(f"h{j}", [P, S], F32, (H1_AT, H2_AT)[j - 1]) if j <= 2 else d_sb
+            h_sb[j] = link(f"h{j}", [P, S], F32, H_AT[j]) if j in H_AT else d_sb
             clamp(j, h_sb[j][:], d_sb[:])
 
         def clamp(j, dst, src):
@@ -216,13 +218,16 @@ def tile_list_eclipse_shed_planner_kernel(
                 z_fold[q] = sb(f"zfold{q}", [P, 2, 4, QUAD, 2], BF16)
                 nc.scalar.copy(z_fold[q][:], bank[:].rearrange("t s (p u e) -> t u s p e", u=2, e=2))
 
-        z_codes = [sb(f"z_codes{a}", [P, QUARTERS, BANK], U32) for a in range(PASSES)]
+        zb_codes = sb("zb_codes", [P, QUARTERS, BANK], U32)
+        z_codes = {(1, q): zb_codes[:, q, :] for q in range(QUARTERS)}
         z_scales = [sb(f"z_scales{a}", [P, QUARTERS, BANK], U8) for a in range(PASSES)]
 
-        def finish_z(a, q, banks):
+        z_grouped = {}
+
+        def turn_back(a, q, banks):
             first = 3 * QUAD * (1 - a)
             pairs = z_turned[q][:].rearrange("t s u p e -> t (s u p e)").bitcast(F32).rearrange("t (s u p) -> t s u p", s=4, u=2)
-            grouped = sb(f"zg{a}_{q}", [P, 4 * BANK], BF16, f"zg{q}")
+            grouped = sb(f"zg{a}_{q}", [P, 4 * BANK], BF16, ("rawA", "rawB", "rawC", "rawD", "rawA", "rawB", "zg2", "zg3")[4 * a + q])
             for half in range(2):
                 bank = bank_tile(f"back{a}_{q}_{half}", [P, 2, 256], banks[half])
                 for s in range(2):
@@ -230,7 +235,14 @@ def tile_list_eclipse_shed_planner_kernel(
                         nc.tensor.transpose(bank[:, u, P * s : P * (s + 1)], pairs[:, 2 * half + s, u, first : first + P], ident[:])
                 words = grouped[:, 1024 * half : 1024 * (half + 1)].bitcast(F32)
                 nc.scalar.copy(words.rearrange("p (t u) -> p t u", u=2), bank[:].rearrange("p u t -> p t u"))
-            nc.vector.quantize_mx(out=z_codes[a][:, q, :].bitcast(FP8X4), scales=z_scales[a][:, q, :], in_=grouped[:])
+            z_grouped[a, q] = grouped
+
+        def quantise_z(a, q):
+            grouped = z_grouped[a, q]
+            if a == 0:
+                name = f"za_codes{q}"
+                z_codes[a, q] = (link(name, [P, BANK], U32, H1_AT + 2048 * (q - 2)) if q >= 2 else sb(name, [P, BANK], U32))[:]
+            nc.vector.quantize_mx(out=z_codes[a, q].bitcast(FP8X4), scales=z_scales[a][:, q, :], in_=grouped[:])
 
         fold_codes = sb("fold_codes", [P, QUARTERS, P], U32)
         fold_scales = sb("fold_scales", [P, QUARTERS, P], U8)
@@ -254,7 +266,7 @@ def tile_list_eclipse_shed_planner_kernel(
                 out=y_acc[n, q][:],
                 lhsT=(w4_fold[:, 4, :] if (n, a) == (0, 1) else w4_sb[:, a, 2 * P * n : 2 * P * (n + 1)]).bitcast(FP4X4),
                 lhsT_scale=w4_plane[:, a, P * n : P * (n + 1)],
-                rhs=z_codes[a][:, q, :].bitcast(FP8X4),
+                rhs=z_codes[a, q].bitcast(FP8X4),
                 rhs_scale=z_scales[a][:, q, :],
                 start=bool(bank),
                 stop=stop,
@@ -341,30 +353,36 @@ def tile_list_eclipse_shed_planner_kernel(
             if 4 < j + 3 <= LAST:
                 quantise_w1(j + 3)
             if j >= 5:
-                finish_z(0, 2 * (j - 5), BACK_BANKS)
-                finish_z(0, 2 * (j - 5) + 1, SPARE_BANKS)
+                turn_back(0, 2 * (j - 5), BACK_BANKS)
+                turn_back(0, 2 * (j - 5) + 1, SPARE_BANKS)
+            if j == 5:
+                quantise_z(0, 0)
+                quantise_z(0, 1)
             for q in range(QUARTERS):
-                turn_stored(j - 1, q)
+                if (j - 1, q) not in sums:
+                    turn_stored(j - 1, q)
                 add_page(j - 1, q)
             if j + 2 <= LAST:
                 load_stored(j + 2)
+            for q in {4: (2, 3), 5: (2, 3, 0, 1), 6: (2, 3, 0, 1)}.get(j, ()):
+                turn_stored(j, q)
 
         scatter_page(LAST, h_sb[LAST][:], 0, S)
+        quantise_z(0, 2)
+        quantise_z(0, 3)
         second_pass(0, 0, 0, SPARE_BANKS[0])
         second_pass(0, 1, 0, SPARE_BANKS[1])
         for q in range(QUARTERS):
-            turn_stored(6, q)
             add_page(6, q)
-        outs[0] = sb("out0", [P, T2], F32, "page0")
-        nc.vector.memset(outs[0][:], 0.0)
         for q in range(QUARTERS):
-            finish_z(1, q, BACK_BANKS)
+            turn_back(1, q, BACK_BANKS)
+            quantise_z(1, q)
             turn_stored(LAST, (q + 2) % QUARTERS)
-        second_pass(0, 2, 0, BACK_BANKS[0])
-        second_pass(0, 3, 0, BACK_BANKS[1])
 
         for q in range(QUARTERS):
             add_page(LAST, q)
+        second_pass(0, 2, 0, BACK_BANKS[0])
+        second_pass(0, 3, 0, BACK_BANKS[1])
         second_pass(0, 0, 1)
         for q in range(QUARTERS):
             finish_fold(q)
@@ -375,7 +393,7 @@ def tile_list_eclipse_shed_planner_kernel(
             fetch_scores(0, q)
         for s in range(4):
             nc.sync.dma_start(
-                z_codes[1][3 * QUAD : P, :, P * s : P * (s + 1)].bitcast(I32), fold_codes[QUAD * s : QUAD * (s + 1), :, :].bitcast(I32)
+                zb_codes[3 * QUAD : P, :, P * s : P * (s + 1)].bitcast(I32), fold_codes[QUAD * s : QUAD * (s + 1), :, :].bitcast(I32)
             )
             nc.sync.dma_start(
                 z_scales[1][3 * QUAD : 3 * QUAD + 4, :, P * s : P * (s + 1)].bitcast(I32), fold_scales[QUAD * s : QUAD * s + 4, :, :].bitcast(I32)

@@ -88,13 +88,18 @@ def tile_list_eclipse_shed_planner_kernel(
             stored_sb[j] = sb(f"stored{j}", [P, T2], F32, f"rows{j % STORED_BUFS}")
             nc.sync.dma_start(stored_sb[j][:], stored[P * j : P * (j + 1), :])
 
-        idx = load_list(offs, "idx")
         scale_rows = sb("scale_rows", [P, T // 4], I32, "h2")
         for quad in range(4):
             live = slice(QUAD * quad, QUAD * quad + 8)
-            nc.sync.dma_start(scale_rows[live, :], tab_scales[:, 4 * quad : 4 * quad + 4, :].bitcast(I32))
+            if quad < 3:
+                for a in range(PASSES):
+                    first = QUAD * quad + 4 * a
+                    nc.sync.dma_start(scale_rows[first : first + 4, :], tab_scales[a, 4 * quad : 4 * quad + 4, :].bitcast(I32))
+            else:
+                nc.sync.dma_start(scale_rows[live, :], tab_scales[:, 4 * quad : 4 * quad + 4, :].bitcast(I32))
             nc.vector.tensor_copy(tab_plane[live, :].bitcast(I32), scale_rows[live, :])
         words0 = load_table(0)
+        idx = load_list(offs, "idx")
         load_w1((0,), ("rawA",))
         vectors = keep.tile([20, P], F32, name="vectors")
         nc.sync.dma_start(vectors[0:8, :], lo.rearrange("(j p) -> j p", p=P))
@@ -112,14 +117,14 @@ def tile_list_eclipse_shed_planner_kernel(
         for page in pages:
             nc.vector.memset(page[:], 0.0)
         w4_plane = sb("w4_plane", [P, PASSES, N], U8)
-        nc.gpsimd.memset(w4_plane[:].bitcast(I32), 0)
+        nc.vector.memset(w4_plane[:].bitcast(I32), 0)
         w4_fold = sb("w4_fold", [P, 5, 2 * P], U8)
-        nc.gpsimd.memset(w4_fold[:].bitcast(I32), 0)
+        nc.vector.memset(w4_fold[:].bitcast(I32), 0)
         w4_fold_plane = sb("w4_fold_plane", [P, P], U8)
-        nc.gpsimd.memset(w4_fold_plane[:].bitcast(I32), 0)
+        nc.vector.memset(w4_fold_plane[:].bitcast(I32), 0)
         outs = [sb(f"out{b}", [P, T2], F32) for b in range(2)]
-        nc.gpsimd.memset(outs[1][:], 0.0)
-        nc.gpsimd.memset(outs[0][:], 0.0)
+        for page in outs:
+            nc.vector.memset(page[:], 0.0)
 
         nc.scalar.copy(rows[0:20, :], vectors[:])
         turned = bank_tile("turned", [P, P], BACK_BANKS[0])
@@ -303,15 +308,15 @@ def tile_list_eclipse_shed_planner_kernel(
             nc.vector.tensor_copy(v_codes[1][:, BANK * half : BANK * (half + 1)], words1[:].bitcast(U32).indirect(listed))
 
         first_product(0)
-        h_first = link("h0a", [P, BANK], F32, FIRST_HALF_AT)
-        clamp(0, h_first[:], d_acc[0, 0][:])
-        scatter_page(0, h_first[:], 0, BANK)
+        h_first = link("h0a", [P, BANK + 16], F32, FIRST_HALF_AT)
+        clamp(0, h_first[:, 0:BANK], d_acc[0, 0][:])
+        scatter_page(0, h_first[:, 0:BANK], 0, BANK)
         round_w1(1)
-        quantise_w1(1)
         d_second = sb("d0b", [P, BANK], F32, "rawB")
         nc.scalar.copy(d_second[:], d_acc[0, 1][:])
         h_second = link("h0b", [P, BANK + 16], F32, SECOND_HALF_AT)
         clamp(0, h_second[:, 0:BANK], d_second[:])
+        quantise_w1(1)
         scatter_page(0, h_second[:, 0:BANK], BANK, S)
 
         load_w1((4, 5, 6, 7), ("wide1",))

@@ -54,7 +54,7 @@ def tile_list_eclipse_shed_planner_kernel(
         ident = keep.tile([P, P], F32, name="ident")
         make_identity(nc, ident[:])
 
-        tab_plane = sb("tab_plane", [P, T], U8)
+        tab_plane = sb("tab_plane", [P, T], U8, "plane")
         nc.vector.memset(tab_plane[:].bitcast(I32), 0)
 
         def load_list(src, name):
@@ -184,10 +184,11 @@ def tile_list_eclipse_shed_planner_kernel(
             d_sb = sb(f"d{j}", [P, S], F32, tag)
             for half in range(2):
                 nc.scalar.copy(d_sb[:, BANK * half : BANK * (half + 1)], d_acc[j, half][:])
-            if j == 2:
-                quantise_w1(4)
-            h_sb[j] = link(f"h{j}", [P, S], F32, H_AT[j]) if j in H_AT else d_sb
-            clamp(j, h_sb[j][:], d_sb[:])
+            return d_sb
+
+        def clamp_product(j, d_sb):
+            h_sb[j] = link(f"h{j}", [P, S + 32 * (j == LAST)], F32, H_AT[j])[:, 0:S] if j in H_AT else d_sb[:]
+            clamp(j, h_sb[j], d_sb[:])
 
         def clamp(j, dst, src):
             nc.vector.tensor_scalar(dst, src, cols[:, j : j + 1], cols[:, 8 + j : 9 + j], ALU.max, ALU.min)
@@ -232,7 +233,7 @@ def tile_list_eclipse_shed_planner_kernel(
         def turn_back(a, q, banks):
             first = 3 * QUAD * (1 - a)
             pairs = z_turned[q][:].rearrange("t s u p e -> t (s u p e)").bitcast(F32).rearrange("t (s u p) -> t s u p", s=4, u=2)
-            grouped = sb(f"zg{a}_{q}", [P, 4 * BANK], BF16, ("rawA", "rawB", "rawC", "rawD", "rawA", "rawB", "zg2", "zg3")[4 * a + q])
+            grouped = sb(f"zg{a}_{q}", [P, 4 * BANK], BF16, ("rawA", "rawB", "rawC", "rawD", "h0", "plane", "zg2", "zg3")[4 * a + q])
             for half in range(2):
                 bank = bank_tile(f"back{a}_{q}_{half}", [P, 2, 256], banks[half])
                 for s in range(2):
@@ -246,7 +247,7 @@ def tile_list_eclipse_shed_planner_kernel(
             grouped = z_grouped[a, q]
             if a == 0:
                 name = f"za_codes{q}"
-                z_codes[a, q] = (link(name, [P, BANK], U32, H1_AT + 2048 * (q - 2)) if q >= 2 else sb(name, [P, BANK], U32))[:]
+                z_codes[a, q] = (link(name, [P, BANK], U32, H1_AT - 1984 + 2048 * q))[:]
             nc.vector.quantize_mx(out=z_codes[a, q].bitcast(FP8X4), scales=z_scales[a][:, q, :], in_=grouped[:])
 
         fold_codes = sb("fold_codes", [P, QUARTERS, P], U32)
@@ -269,7 +270,7 @@ def tile_list_eclipse_shed_planner_kernel(
                 y_acc[n, q] = bank_tile(f"yacc{n}_{q}", [P, BANK], bank)
             nc.tensor.matmul_mx(
                 out=y_acc[n, q][:],
-                lhsT=(w4_fold[:, 4, :] if (n, a) == (0, 1) else w4_sb[:, a, 2 * P * n : 2 * P * (n + 1)]).bitcast(FP4X4),
+                lhsT=(w4_fold[:, 4, :] if (n, a) == (0, 1) else w4_sb[n][:, a, :]).bitcast(FP4X4),
                 lhsT_scale=w4_plane[:, a, P * n : P * (n + 1)],
                 rhs=z_codes[a, q].bitcast(FP8X4),
                 rhs_scale=z_scales[a][:, q, :],
@@ -321,8 +322,11 @@ def tile_list_eclipse_shed_planner_kernel(
 
         load_w1((4, 5, 6, 7), ("wide1",))
         load_stored(1)
-        w4_sb = sb("w4_sb", [P, PASSES, 2 * N], U8)
-        nc.sync.dma_start(w4_sb[:].bitcast(I32), w4_words.rearrange("a p c -> p a c").bitcast(I32))
+        w4_sb = []
+        for n in range(N_TILES):
+            w4_sb.append(sb(f"w4_sb{n}", [P, PASSES, 2 * P], U8))
+            columns = w4_words[:, :, 2 * P * n : 2 * P * (n + 1)]
+            nc.sync.dma_start(w4_sb[n][:].bitcast(I32), columns.rearrange("a p c -> p a c").bitcast(I32))
         for quad in range(4):
             lanes = slice(QUAD * quad, QUAD * (quad + 1))
             live = slice(QUAD * quad, QUAD * quad + 4)
@@ -339,7 +343,7 @@ def tile_list_eclipse_shed_planner_kernel(
         first_product(1)
         round_w1(2)
         round_w1(3)
-        fetch_product(1, "rawC")
+        clamp_product(1, fetch_product(1, "rawC"))
         quantise_w1(2)
         quantise_w1(3)
         duty_sb = sb("duty_sb", [P, N_TILES, PICK], F32, "wide0")
@@ -348,21 +352,28 @@ def tile_list_eclipse_shed_planner_kernel(
         nc.sync.dma_start(wgo_sb[:], wgo)
 
         for j in range(1, LAST):
-            scatter_page(j, h_sb[j][:], 0, S)
-            if j + 3 <= LAST:
-                round_w1(j + 3)
-            for ahead in (2, 3) if j == 1 else (j + 2,):
-                if ahead <= LAST:
+            scatter_page(j, h_sb[j], 0, S)
+            if j == 1:
+                round_w1(4)
+                round_w1(5)
+                fetched = []
+                for ahead in (2, 3):
                     first_product(ahead)
-                    fetch_product(ahead, f"h{ahead % 3}")
-            if 4 < j + 3 <= LAST:
-                quantise_w1(j + 3)
+                    fetched.append(fetch_product(ahead, f"h{ahead % 3}"))
+                quantise_w1(4)
+                quantise_w1(5)
+                clamp_product(2, fetched[0])
+                clamp_product(3, fetched[1])
+            elif j + 2 <= LAST:
+                if j + 4 <= LAST:
+                    round_w1(j + 4)
+                first_product(j + 2)
+                clamp_product(j + 2, fetch_product(j + 2, f"h{(j + 2) % 3}"))
+                if j + 4 <= LAST:
+                    quantise_w1(j + 4)
             if j >= 5:
                 turn_back(0, 2 * (j - 5), BACK_BANKS)
                 turn_back(0, 2 * (j - 5) + 1, SPARE_BANKS)
-            if j == 5:
-                quantise_z(0, 0)
-                quantise_z(0, 1)
             for q in range(QUARTERS):
                 if (j - 1, q) not in sums:
                     turn_stored(j - 1, q)
@@ -372,22 +383,20 @@ def tile_list_eclipse_shed_planner_kernel(
             for q in {4: (2, 3), 5: (2, 3, 0, 1), 6: (2, 3, 0, 1)}.get(j, ()):
                 turn_stored(j, q)
 
-        scatter_page(LAST, h_sb[LAST][:], 0, S)
-        quantise_z(0, 2)
-        quantise_z(0, 3)
-        second_pass(0, 0, 0, SPARE_BANKS[0])
-        second_pass(0, 1, 0, SPARE_BANKS[1])
+        scatter_page(LAST, h_sb[LAST], 0, S)
+        for q in range(QUARTERS):
+            quantise_z(0, q)
         for q in range(QUARTERS):
             add_page(6, q)
         for q in range(QUARTERS):
-            turn_back(1, q, BACK_BANKS)
+            turn_back(1, q, (BACK_BANKS, SPARE_BANKS)[q % 2])
             quantise_z(1, q)
             turn_stored(LAST, (q + 2) % QUARTERS)
 
         for q in range(QUARTERS):
             add_page(LAST, q)
-        second_pass(0, 2, 0, BACK_BANKS[0])
-        second_pass(0, 3, 0, BACK_BANKS[1])
+        for q in range(QUARTERS):
+            second_pass(0, q, 0, (BACK_BANKS + SPARE_BANKS)[q])
         second_pass(0, 0, 1)
         for q in range(QUARTERS):
             finish_fold(q)
@@ -404,15 +413,28 @@ def tile_list_eclipse_shed_planner_kernel(
                 z_scales[1][3 * QUAD : 3 * QUAD + 4, :, P * s : P * (s + 1)].bitcast(I32), fold_scales[QUAD * s : QUAD * s + 4, :, :].bitcast(I32)
             )
 
+        x_sb = {}
+
+        def pick(n, tag):
+            x_sb[n] = sb(f"x{n}", [P, PICK], F32, tag)
+            nc.vector.tensor_tensor(x_sb[n][:], y_sb[n][:].indirect(idx3[:]), duty_sb[:, n, :], ALU.add)
+
+        def scores(n):
+            banks = PAIRS[0] + PAIRS[1] if n % 2 == 1 else BACK_BANKS + SPARE_BANKS
+            for q in range(QUARTERS):
+                second_pass(n, q, 1, banks[q])
+                second_pass(n, q, 0, stop=True)
+                fetch_scores(n, q)
+
+        pick(0, "h0")
+        scores(1)
+        scores(2)
+        scores(3)
         for n in range(N_TILES):
-            if n + 1 < N_TILES:
-                banks = PAIRS[0] + PAIRS[1] if n % 2 == 0 else SPARE_BANKS + BACK_BANKS
-                for q in range(QUARTERS):
-                    second_pass(n + 1, q, 1, banks[q])
-                    second_pass(n + 1, q, 0, stop=True)
-                    fetch_scores(n + 1, q)
-            x = sb(f"x{n}", [P, PICK], F32, f"h{n % 3}")
-            nc.vector.tensor_tensor(x[:], y_sb[n][:].indirect(idx3[:]), duty_sb[:, n, :], ALU.add)
+            if n == 1:
+                pick(1, "w4_sb2")
+            if 1 <= n < N_TILES - 1:
+                pick(n + 1, f"h{n}")
             page = outs[n % 2]
-            nc.vector.tensor_tensor(page[:].indirect(idx4[:]), x[:], wgo_sb[:], ALU.mult)
+            nc.vector.tensor_tensor(page[:].indirect(idx4[:]), x_sb[n][:], wgo_sb[:], ALU.mult)
             nc.sync.dma_start(out[P * n : P * (n + 1), :], page[:])

@@ -1,7 +1,6 @@
 from contextlib import ExitStack
 
 import concourse.mybir as mybir
-from concourse.masks import make_identity
 
 K, H, N, T, S, T2, PICK = 1024, 1024, 512, 4096, 1024, 2048, 1024
 FLOPS = 2 * K * H * S + 2 * H * N * T2
@@ -19,19 +18,29 @@ COPY = mybir.ActivationFunctionType.Copy
 
 P = 128
 QUAD = 32
+QUADS = P // QUAD
 PASSES = 2
 BANK = 512
 R_TILES = H // P
 N_TILES = N // P
 QUARTERS = T2 // BANK
 LAST = R_TILES - 1
+FINAL = QUARTERS - 1
 PAGES = 2
-STORED_BUFS = 3
+ROW_BUFS = 3
+H_BUFS = 3
+LIMIT_ROWS = 2 * R_TILES + N_TILES
+
 FIRST_HALF_AT, SECOND_HALF_AT, H1_AT, H2_AT = 0, 2048, 4096, 8192
-H_AT = {1: H1_AT, 2: H2_AT, LAST: H1_AT}
+H_AT = {1: H1_AT, 2: H2_AT}
+REACH = 16
+W1_CODES_BYTES = 4 * PASSES * P
+
 PAIRS = (("work0", "work1"), ("work2", "work3"))
 BACK_BANKS = ("back0", "back1")
 SPARE_BANKS = ("spare0", "spare1")
+TURNED_EARLY = {4: (2, 3), 5: (2, 3, 0, 1), 6: (2, 3, 0, 1)}
+WOVEN_TAGS = ("rawA", "rawB", "rawC", "rawD", "h0", "plane", "woven6", "woven7")
 
 
 def tile_list_eclipse_shed_planner_kernel(
@@ -46,13 +55,18 @@ def tile_list_eclipse_shed_planner_kernel(
         def sb(name, shape, dtype, tag=None):
             return keep.tile(shape, dtype, name=name, tag=tag or name, align_bytes=64)
 
+        def link(name, shape, dtype, offset):
+            return chain.tile(shape, dtype, name=name, align_bytes=64, offset=offset)
+
         def bank_tile(name, shape, tag):
             return psum.tile(shape, F32, name=name, tag=tag)
 
-        rows = keep.tile([P, P], F32, name="rows")
-        nc.gpsimd.memset(rows[:], 0.0)
+        limit_rows = keep.tile([P, P], F32, name="limit_rows")
+        nc.vector.memset(limit_rows[:], 0.0)
+        distance = keep.tile([P, P], F32, name="distance")
+        nc.gpsimd.iota(distance[:], [[1, P]], base=0, channel_multiplier=-1, allow_small_or_imprecise_dtypes=True)
         ident = keep.tile([P, P], F32, name="ident")
-        make_identity(nc, ident[:])
+        nc.vector.tensor_scalar(ident[:], distance[:], 0.0, None, ALU.is_equal)
 
         tab_plane = sb("tab_plane", [P, T], U8, "plane")
         nc.vector.memset(tab_plane[:].bitcast(I32), 0)
@@ -85,13 +99,13 @@ def tile_list_eclipse_shed_planner_kernel(
         stored_sb = {}
 
         def load_stored(j):
-            stored_sb[j] = sb(f"stored{j}", [P, T2], F32, f"rows{j % STORED_BUFS}")
+            stored_sb[j] = sb(f"stored{j}", [P, T2], F32, f"rows{j % ROW_BUFS}")
             nc.sync.dma_start(stored_sb[j][:], stored[P * j : P * (j + 1), :])
 
         scale_rows = sb("scale_rows", [P, T // 4], I32, "h2")
-        for quad in range(4):
-            live = slice(QUAD * quad, QUAD * quad + 8)
-            if quad < 3:
+        for quad in range(QUADS):
+            live = slice(QUAD * quad, QUAD * quad + 4 * PASSES)
+            if quad < QUADS - 1:
                 for a in range(PASSES):
                     first = QUAD * quad + 4 * a
                     nc.sync.dma_start(scale_rows[first : first + 4, :], tab_scales[a, 4 * quad : 4 * quad + 4, :].bitcast(I32))
@@ -101,10 +115,10 @@ def tile_list_eclipse_shed_planner_kernel(
         words0 = load_table(0)
         idx = load_list(offs, "idx")
         load_w1((0,), ("rawA",))
-        vectors = keep.tile([20, P], F32, name="vectors")
-        nc.sync.dma_start(vectors[0:8, :], lo.rearrange("(j p) -> j p", p=P))
-        nc.sync.dma_start(vectors[8:16, :], hi.rearrange("(j p) -> j p", p=P))
-        nc.sync.dma_start(vectors[16:20, :], gain.rearrange("(j p) -> j p", p=P))
+        limits = keep.tile([LIMIT_ROWS, P], F32, name="limits")
+        nc.sync.dma_start(limits[0:R_TILES, :], lo.rearrange("(j p) -> j p", p=P))
+        nc.sync.dma_start(limits[R_TILES : 2 * R_TILES, :], hi.rearrange("(j p) -> j p", p=P))
+        nc.sync.dma_start(limits[2 * R_TILES : LIMIT_ROWS, :], gain.rearrange("(j p) -> j p", p=P))
         words1 = load_table(1)
         idx2 = load_list(offs2, "idx2")
         wgs_sb = sb("wgs_sb", [P, S], F32)
@@ -118,45 +132,42 @@ def tile_list_eclipse_shed_planner_kernel(
             nc.vector.memset(page[:], 0.0)
         w4_plane = sb("w4_plane", [P, PASSES, N], U8)
         nc.vector.memset(w4_plane[:].bitcast(I32), 0)
-        w4_fold = sb("w4_fold", [P, 5, 2 * P], U8)
-        nc.vector.memset(w4_fold[:].bitcast(I32), 0)
+        w4_masked = sb("w4_masked", [P, QUADS + 1, 2 * P], U8)
+        nc.vector.memset(w4_masked[:].bitcast(I32), 0)
         w4_fold_plane = sb("w4_fold_plane", [P, P], U8)
         nc.vector.memset(w4_fold_plane[:].bitcast(I32), 0)
-        outs = [sb(f"out{b}", [P, T2], F32) for b in range(2)]
-        for page in outs:
-            nc.vector.memset(page[:], 0.0)
+        outs = [sb("out0", [P, T2], F32)]
+        nc.vector.memset(outs[0][:], 0.0)
 
-        nc.scalar.copy(rows[0:20, :], vectors[:])
+        nc.scalar.copy(limit_rows[0:LIMIT_ROWS, :], limits[:])
         turned = bank_tile("turned", [P, P], BACK_BANKS[0])
-        nc.tensor.transpose(turned[:], rows[:], ident[:])
-        cols = keep.tile([P, 20], F32, name="cols")
-        nc.scalar.copy(cols[:], turned[:, 0:20])
+        nc.tensor.transpose(turned[:], limit_rows[:], ident[:])
+        cols = keep.tile([P, LIMIT_ROWS], F32, name="cols")
+        nc.scalar.copy(cols[:], turned[:, 0:LIMIT_ROWS])
 
-        w1_grouped = {}
+        w1_rounded = {}
         w1_codes = {}
         w1_scales = {}
 
         def round_w1(j):
             if j == 4:
-                grouped = link("w1g4", [P, PASSES * P * 4], BF16, H2_AT)
+                rounded = link("w1r4", [P, PASSES * P * 4], BF16, H2_AT)
             else:
-                grouped = sb(f"w1g{j}", [P, PASSES * P * 4], BF16, f"w1g{j % 2}")
-            w1_grouped[j] = grouped
+                rounded = sb(f"w1r{j}", [P, PASSES * P * 4], BF16, f"w1r{j % 2}")
+            w1_rounded[j] = rounded
             for a in range(PASSES):
                 nc.scalar.copy(
-                    grouped[:, 4 * P * a : 4 * P * (a + 1)].rearrange("p (c i) -> p c i", i=4), w1_raw[j, a].rearrange("p i c -> p c i")
+                    rounded[:, 4 * P * a : 4 * P * (a + 1)].rearrange("p (c i) -> p c i", i=4), w1_raw[j, a].rearrange("p i c -> p c i")
                 )
-
-        def link(name, shape, dtype, offset):
-            return chain.tile(shape, dtype, name=name, align_bytes=64, offset=offset)
 
         def quantise_w1(j):
             if j == 0:
                 w1_codes[j] = sb("w1c0", [P, PASSES * P], U32)
             else:
-                w1_codes[j] = link(f"w1c{j}", [P, PASSES * P], U32, FIRST_HALF_AT if j == 1 else SECOND_HALF_AT + 1024 * (j % 2))
+                at = FIRST_HALF_AT if j == 1 else SECOND_HALF_AT + W1_CODES_BYTES * (j % 2)
+                w1_codes[j] = link(f"w1c{j}", [P, PASSES * P], U32, at)
             w1_scales[j] = sb(f"w1s{j}", [P, PASSES * P], U8, f"w1s{j % 2}")
-            nc.vector.quantize_mx(out=w1_codes[j][:].bitcast(FP8X4), scales=w1_scales[j][:], in_=w1_grouped[j][:])
+            nc.vector.quantize_mx(out=w1_codes[j][:].bitcast(FP8X4), scales=w1_scales[j][:], in_=w1_rounded[j][:])
 
         v_codes = [sb(f"v_codes{a}", [P, S], U32) for a in range(PASSES)]
         v_plane = sb("v_plane", [P, S], U8)
@@ -165,8 +176,8 @@ def tile_list_eclipse_shed_planner_kernel(
         def first_product(j):
             for half in range(2):
                 d_acc[j, half] = bank_tile(f"dacc{j}_{half}", [P, BANK], PAIRS[j % 2][half])
-            order = [(half, a) for a in range(PASSES) for half in range(2)] if j == 0 else [(half, a) for half in range(2) for a in range(PASSES)]
-            for half, a in order:
+            by_half = [(half, a) for half in range(2) for a in range(PASSES)]
+            for half, a in sorted(by_half, key=lambda step: step[1]) if j == 0 else by_half:
                 span = slice(BANK * half, BANK * (half + 1))
                 nc.tensor.matmul_mx(
                     out=d_acc[j, half][:],
@@ -178,20 +189,20 @@ def tile_list_eclipse_shed_planner_kernel(
                     stop=(a == PASSES - 1),
                 )
 
-        h_sb = {}
-
         def fetch_product(j, tag):
             d_sb = sb(f"d{j}", [P, S], F32, tag)
             for half in range(2):
                 nc.scalar.copy(d_sb[:, BANK * half : BANK * (half + 1)], d_acc[j, half][:])
             return d_sb
 
-        def clamp_product(j, d_sb):
-            h_sb[j] = link(f"h{j}", [P, S + 32 * (j == LAST)], F32, H_AT[j])[:, 0:S] if j in H_AT else d_sb[:]
-            clamp(j, h_sb[j], d_sb[:])
-
         def clamp(j, dst, src):
-            nc.vector.tensor_scalar(dst, src, cols[:, j : j + 1], cols[:, 8 + j : 9 + j], ALU.max, ALU.min)
+            nc.vector.tensor_scalar(dst, src, cols[:, j : j + 1], cols[:, R_TILES + j : R_TILES + j + 1], ALU.max, ALU.min)
+
+        h_sb = {}
+
+        def clamp_product(j, d_sb):
+            h_sb[j] = link(f"h{j}", [P, S], F32, H_AT[j])[:] if j in H_AT else d_sb[:]
+            clamp(j, h_sb[j], d_sb[:])
 
         def scatter_page(j, h, c0, c1):
             window = pages[j % PAGES][:].indirect(idx2[:, c0 // 16 : c1 // 16])
@@ -204,64 +215,62 @@ def tile_list_eclipse_shed_planner_kernel(
 
         def turn_stored(j, q):
             sums[j, q] = bank_tile(f"sum{j}_{q}", [P, 4, P], sum_bank(j, q))
-            for tt in range(4):
-                t0 = BANK * q + P * tt
-                nc.tensor.matmul(sums[j, q][:, tt, :], stored_sb[j][:, t0 : t0 + P], ident[:], start=(tt == 0), stop=False, is_transpose=True)
+            for s in range(4):
+                t0 = BANK * q + P * s
+                nc.tensor.matmul(sums[j, q][:, s, :], stored_sb[j][:, t0 : t0 + P], ident[:], start=(s == 0), stop=False, is_transpose=True)
 
         z_turned = [sb(f"zt{q}", [P, 4, 2, LAST * QUAD, 2], BF16) for q in range(QUARTERS)]
-        z_fold = {}
+        z_folded = {}
 
         def add_page(j, q):
             bank = sums[j, q]
-            for tt in range(4):
-                t0 = BANK * q + P * tt
-                nc.tensor.matmul(bank[:, tt, :], pages[j % PAGES][:, t0 : t0 + P], ident[:], start=False, stop=(tt == 3), is_transpose=True)
+            for s in range(4):
+                t0 = BANK * q + P * s
+                nc.tensor.matmul(bank[:, s, :], pages[j % PAGES][:, t0 : t0 + P], ident[:], start=False, stop=(s == 3), is_transpose=True)
             if j < LAST:
                 place = (j + 3) % LAST
                 dst = z_turned[q][:, :, :, QUAD * place : QUAD * (place + 1), :]
                 nc.scalar.copy(dst, bank[:].rearrange("t s (p u e) -> t s u p e", u=2, e=2))
             else:
-                z_fold[q] = sb(f"zfold{q}", [P, 2, 4, QUAD, 2], BF16)
-                nc.scalar.copy(z_fold[q][:], bank[:].rearrange("t s (p u e) -> t u s p e", u=2, e=2))
+                z_folded[q] = sb(f"zfold{q}", [P, 2, 4, QUAD, 2], BF16)
+                nc.scalar.copy(z_folded[q][:], bank[:].rearrange("t s (p u e) -> t u s p e", u=2, e=2))
 
-        zb_codes = sb("zb_codes", [P, QUARTERS, BANK], U32)
-        z_codes = {(1, q): zb_codes[:, q, :] for q in range(QUARTERS)}
+        pass1_codes = sb("pass1_codes", [P, QUARTERS, BANK], U32)
+        z_codes = {(1, q): pass1_codes[:, q, :] for q in range(QUARTERS)}
         z_scales = [sb(f"z_scales{a}", [P, QUARTERS, BANK], U8) for a in range(PASSES)]
-
-        z_grouped = {}
+        z_woven = {}
 
         def turn_back(a, q, banks):
             first = 3 * QUAD * (1 - a)
             pairs = z_turned[q][:].rearrange("t s u p e -> t (s u p e)").bitcast(F32).rearrange("t (s u p) -> t s u p", s=4, u=2)
-            grouped = sb(f"zg{a}_{q}", [P, 4 * BANK], BF16, ("rawA", "rawB", "rawC", "rawD", "h0", "plane", "zg2", "zg3")[4 * a + q])
+            woven = sb(f"zw{a}_{q}", [P, 4 * BANK], BF16, WOVEN_TAGS[QUARTERS * a + q])
             for half in range(2):
-                bank = bank_tile(f"back{a}_{q}_{half}", [P, 2, 256], banks[half])
+                bank = bank_tile(f"back{a}_{q}_{half}", [P, 2, 2 * P], banks[half])
                 for s in range(2):
                     for u in range(2):
                         nc.tensor.transpose(bank[:, u, P * s : P * (s + 1)], pairs[:, 2 * half + s, u, first : first + P], ident[:])
-                words = grouped[:, 1024 * half : 1024 * (half + 1)].bitcast(F32)
+                words = woven[:, 2 * BANK * half : 2 * BANK * (half + 1)].bitcast(F32)
                 nc.scalar.copy(words.rearrange("p (t u) -> p t u", u=2), bank[:].rearrange("p u t -> p t u"))
-            z_grouped[a, q] = grouped
+            z_woven[a, q] = woven
 
         def quantise_z(a, q):
-            grouped = z_grouped[a, q]
-            if a == 0:
-                name = f"za_codes{q}"
-                z_codes[a, q] = (link(name, [P, BANK], U32, H1_AT - 1984 + 2048 * q))[:]
-            nc.vector.quantize_mx(out=z_codes[a, q].bitcast(FP8X4), scales=z_scales[a][:, q, :], in_=grouped[:])
+            if (a, q) == (0, FINAL):
+                z_codes[a, q] = sb("pass0_final", [P, BANK], U32, f"zwfold{q}")[:]
+            nc.vector.quantize_mx(out=z_codes[a, q].bitcast(FP8X4), scales=z_scales[a][:, q, :], in_=z_woven[a, q][:])
 
         fold_codes = sb("fold_codes", [P, QUARTERS, P], U32)
         fold_scales = sb("fold_scales", [P, QUARTERS, P], U8)
 
         def finish_fold(q):
-            pairs = z_fold[q][:].rearrange("t u s p e -> t (u s p e)").bitcast(F32).rearrange("t (u c) -> t u c", u=2)
+            pairs = z_folded[q][:].rearrange("t u s p e -> t (u s p e)").bitcast(F32).rearrange("t (u c) -> t u c", u=2)
             bank = bank_tile(f"backfold{q}", [P, 2, P], sum_bank(LAST, q))
             for u in range(2):
                 nc.tensor.transpose(bank[:, u, :], pairs[:, u, :], ident[:])
-            grouped = sb(f"zgfold{q}", [P, 4 * P], BF16)
-            nc.scalar.copy(grouped[:].bitcast(F32).rearrange("p (t u) -> p t u", u=2), bank[:].rearrange("p u t -> p t u"))
-            nc.vector.quantize_mx(out=fold_codes[:, q, :].bitcast(FP8X4), scales=fold_scales[:, q, :], in_=grouped[:])
+            woven = sb(f"zwfold{q}", [P, 4 * P], BF16)
+            nc.scalar.copy(woven[:].bitcast(F32).rearrange("p (t u) -> p t u", u=2), bank[:].rearrange("p u t -> p t u"))
+            nc.vector.quantize_mx(out=fold_codes[:, q, :].bitcast(FP8X4), scales=fold_scales[:, q, :], in_=woven[:])
 
+        w4_sb = {}
         y_sb = {}
         y_acc = {}
 
@@ -270,7 +279,7 @@ def tile_list_eclipse_shed_planner_kernel(
                 y_acc[n, q] = bank_tile(f"yacc{n}_{q}", [P, BANK], bank)
             nc.tensor.matmul_mx(
                 out=y_acc[n, q][:],
-                lhsT=(w4_fold[:, 4, :] if (n, a) == (0, 1) else w4_sb[n][:, a, :]).bitcast(FP4X4),
+                lhsT=w4_sb[n, a].bitcast(FP4X4),
                 lhsT_scale=w4_plane[:, a, P * n : P * (n + 1)],
                 rhs=z_codes[a, q].bitcast(FP8X4),
                 rhs_scale=z_scales[a][:, q, :],
@@ -279,23 +288,23 @@ def tile_list_eclipse_shed_planner_kernel(
             )
 
         def fold_passes(q):
-            for s in range(4):
+            for s in range(QUADS):
                 nc.tensor.matmul_mx(
                     out=y_acc[0, q][:, P * s : P * (s + 1)],
-                    lhsT=w4_fold[:, s, :].bitcast(FP4X4),
+                    lhsT=w4_masked[:, s, :].bitcast(FP4X4),
                     lhsT_scale=w4_fold_plane[:],
                     rhs=fold_codes[:, q, :].bitcast(FP8X4),
                     rhs_scale=fold_scales[:, q, :],
                     start=False,
-                    stop=(s == 3),
+                    stop=(s == QUADS - 1 and q < FINAL),
                 )
 
         def fetch_scores(n, q):
             if q == 0:
-                y_sb[n] = sb(f"y{n}", [P, T2], F32, f"rows{(R_TILES + n) % STORED_BUFS}")
+                y_sb[n] = sb(f"y{n}", [P, T2], F32, f"rows{(R_TILES + n) % ROW_BUFS}")
             dst = y_sb[n][:, BANK * q : BANK * (q + 1)]
-            gain_col = cols[:, 16 + n : 17 + n]
-            if n == 0 and q % 2 == 1:
+            gain_col = cols[:, 2 * R_TILES + n : 2 * R_TILES + n + 1]
+            if (n, q) == (0, 1):
                 nc.vector.tensor_scalar(dst, y_acc[n, q][:], gain_col, None, ALU.mult)
             else:
                 nc.scalar.activation(dst, y_acc[n, q][:], COPY, scale=gain_col)
@@ -305,37 +314,40 @@ def tile_list_eclipse_shed_planner_kernel(
         quantise_w1(0)
         nc.vector.tensor_copy(v_plane[:], tab_plane[:].indirect(idx[:]))
         for half in range(2):
-            listed = idx[:, 32 * half : 32 * (half + 1)]
+            listed = idx[:, BANK // 16 * half : BANK // 16 * (half + 1)]
             nc.vector.tensor_copy(v_codes[1][:, BANK * half : BANK * (half + 1)], words1[:].bitcast(U32).indirect(listed))
 
         first_product(0)
-        h_first = link("h0a", [P, BANK + 16], F32, FIRST_HALF_AT)
+        h_first = link("h0a", [P, BANK + REACH], F32, FIRST_HALF_AT)
         clamp(0, h_first[:, 0:BANK], d_acc[0, 0][:])
         scatter_page(0, h_first[:, 0:BANK], 0, BANK)
         round_w1(1)
         d_second = sb("d0b", [P, BANK], F32, "rawB")
         nc.scalar.copy(d_second[:], d_acc[0, 1][:])
-        h_second = link("h0b", [P, BANK + 16], F32, SECOND_HALF_AT)
+        h_second = link("h0b", [P, BANK + REACH], F32, SECOND_HALF_AT)
         clamp(0, h_second[:, 0:BANK], d_second[:])
         quantise_w1(1)
         scatter_page(0, h_second[:, 0:BANK], BANK, S)
 
         load_w1((4, 5, 6, 7), ("wide1",))
         load_stored(1)
-        w4_sb = []
         for n in range(N_TILES):
-            w4_sb.append(sb(f"w4_sb{n}", [P, PASSES, 2 * P], U8))
-            columns = w4_words[:, :, 2 * P * n : 2 * P * (n + 1)]
-            nc.sync.dma_start(w4_sb[n][:].bitcast(I32), columns.rearrange("a p c -> p a c").bitcast(I32))
-        for quad in range(4):
+            passes = 1 if n == 0 else PASSES
+            tile = sb(f"w4_sb{n}", [P, passes, 2 * P], U8)
+            columns = w4_words[0:passes, :, 2 * P * n : 2 * P * (n + 1)]
+            nc.sync.dma_start(tile[:].bitcast(I32), columns.rearrange("a p c -> p a c").bitcast(I32))
+            for a in range(passes):
+                w4_sb[n, a] = tile[:, a, :]
+        w4_sb[0, 1] = w4_masked[:, QUADS, :]
+        for quad in range(QUADS):
             lanes = slice(QUAD * quad, QUAD * (quad + 1))
             live = slice(QUAD * quad, QUAD * quad + 4)
             nc.sync.dma_start(
                 w4_plane[live, :, :].bitcast(I32), w4_scales[:, 4 * quad : 4 * quad + 4, :].rearrange("a r c -> r a c").bitcast(I32)
             )
-            nc.sync.dma_start(w4_fold[lanes, quad, :].bitcast(I32), w4_words[1, 3 * QUAD : P, 0 : 2 * P].bitcast(I32))
+            nc.sync.dma_start(w4_masked[lanes, quad, :].bitcast(I32), w4_words[1, 3 * QUAD : P, 0 : 2 * P].bitcast(I32))
             nc.sync.dma_start(w4_fold_plane[live, :].bitcast(I32), w4_scales[1, 12:16, 0:P].bitcast(I32))
-        nc.sync.dma_start(w4_fold[0 : 3 * QUAD, 4, :].bitcast(I32), w4_words[1, 0 : 3 * QUAD, 0 : 2 * P].bitcast(I32))
+        nc.sync.dma_start(w4_masked[0 : 3 * QUAD, QUADS, :].bitcast(I32), w4_words[1, 0 : 3 * QUAD, 0 : 2 * P].bitcast(I32))
         load_stored(2)
         idx3 = load_list(offs3, "idx3")
         idx4 = load_list(offs4, "idx4")
@@ -359,7 +371,7 @@ def tile_list_eclipse_shed_planner_kernel(
                 fetched = []
                 for ahead in (2, 3):
                     first_product(ahead)
-                    fetched.append(fetch_product(ahead, f"h{ahead % 3}"))
+                    fetched.append(fetch_product(ahead, f"h{ahead % H_BUFS}"))
                 quantise_w1(4)
                 quantise_w1(5)
                 clamp_product(2, fetched[0])
@@ -368,7 +380,7 @@ def tile_list_eclipse_shed_planner_kernel(
                 if j + 4 <= LAST:
                     round_w1(j + 4)
                 first_product(j + 2)
-                clamp_product(j + 2, fetch_product(j + 2, f"h{(j + 2) % 3}"))
+                clamp_product(j + 2, fetch_product(j + 2, f"h{(j + 2) % H_BUFS}"))
                 if j + 4 <= LAST:
                     quantise_w1(j + 4)
             if j >= 5:
@@ -380,37 +392,45 @@ def tile_list_eclipse_shed_planner_kernel(
                 add_page(j - 1, q)
             if j + 2 <= LAST:
                 load_stored(j + 2)
-            for q in {4: (2, 3), 5: (2, 3, 0, 1), 6: (2, 3, 0, 1)}.get(j, ()):
+            for q in TURNED_EARLY.get(j, ()):
                 turn_stored(j, q)
 
         scatter_page(LAST, h_sb[LAST], 0, S)
         for q in range(QUARTERS):
+            add_page(LAST - 1, q)
+        pass0_codes = sb("pass0_codes", [P, FINAL, BANK], U32, f"page{(LAST - 1) % PAGES}")
+        for q in range(FINAL):
+            z_codes[0, q] = pass0_codes[:, q, :]
             quantise_z(0, q)
-        for q in range(QUARTERS):
-            add_page(6, q)
         for q in range(QUARTERS):
             turn_back(1, q, (BACK_BANKS, SPARE_BANKS)[q % 2])
             quantise_z(1, q)
             turn_stored(LAST, (q + 2) % QUARTERS)
 
+        even_banks = BACK_BANKS + SPARE_BANKS
         for q in range(QUARTERS):
             add_page(LAST, q)
-        for q in range(QUARTERS):
-            second_pass(0, q, 0, (BACK_BANKS + SPARE_BANKS)[q])
+        for q in range(FINAL):
+            second_pass(0, q, 0, even_banks[q])
         second_pass(0, 0, 1)
         for q in range(QUARTERS):
             finish_fold(q)
-        for q in range(1, QUARTERS):
+        quantise_z(0, FINAL)
+        for q in range(1, FINAL):
             second_pass(0, q, 1)
+        second_pass(0, FINAL, 1, even_banks[FINAL])
         for q in range(QUARTERS):
             fold_passes(q)
+            if q == FINAL:
+                second_pass(0, q, 0, stop=True)
             fetch_scores(0, q)
-        for s in range(4):
+        outs.append(sb("out1", [P, T2], F32, WOVEN_TAGS[FINAL]))
+        nc.vector.memset(outs[1][:], 0.0)
+        for s in range(QUADS):
+            columns = slice(P * s, P * (s + 1))
+            nc.sync.dma_start(pass1_codes[3 * QUAD : P, :, columns].bitcast(I32), fold_codes[QUAD * s : QUAD * (s + 1), :, :].bitcast(I32))
             nc.sync.dma_start(
-                zb_codes[3 * QUAD : P, :, P * s : P * (s + 1)].bitcast(I32), fold_codes[QUAD * s : QUAD * (s + 1), :, :].bitcast(I32)
-            )
-            nc.sync.dma_start(
-                z_scales[1][3 * QUAD : 3 * QUAD + 4, :, P * s : P * (s + 1)].bitcast(I32), fold_scales[QUAD * s : QUAD * s + 4, :, :].bitcast(I32)
+                z_scales[1][3 * QUAD : 3 * QUAD + 4, :, columns].bitcast(I32), fold_scales[QUAD * s : QUAD * s + 4, :, :].bitcast(I32)
             )
 
         x_sb = {}
@@ -419,17 +439,13 @@ def tile_list_eclipse_shed_planner_kernel(
             x_sb[n] = sb(f"x{n}", [P, PICK], F32, tag)
             nc.vector.tensor_tensor(x_sb[n][:], y_sb[n][:].indirect(idx3[:]), duty_sb[:, n, :], ALU.add)
 
-        def scores(n):
-            banks = PAIRS[0] + PAIRS[1] if n % 2 == 1 else BACK_BANKS + SPARE_BANKS
+        pick(0, "h0")
+        for n in range(1, N_TILES):
+            banks = PAIRS[0] + PAIRS[1] if n % 2 == 1 else even_banks
             for q in range(QUARTERS):
                 second_pass(n, q, 1, banks[q])
                 second_pass(n, q, 0, stop=True)
                 fetch_scores(n, q)
-
-        pick(0, "h0")
-        scores(1)
-        scores(2)
-        scores(3)
         for n in range(N_TILES):
             if n == 1:
                 pick(1, "w4_sb2")

@@ -31,6 +31,9 @@ ROW_BUFS = 3
 H_BUFS = 3
 LIMIT_ROWS = 2 * R_TILES + N_TILES
 
+PLANE_ROW = (12, 0)
+ROWS_AT = 12
+
 FIRST_HALF_AT, SECOND_HALF_AT, H1_AT, H2_AT = 0, 2048, 4096, 8192
 H_AT = {1: H1_AT, 2: H2_AT}
 REACH = 16
@@ -61,15 +64,14 @@ def tile_list_eclipse_shed_planner_kernel(
         def bank_tile(name, shape, tag):
             return psum.tile(shape, F32, name=name, tag=tag)
 
-        limit_rows = keep.tile([P, P], F32, name="limit_rows")
-        nc.vector.memset(limit_rows[:], 0.0)
+        tab_rows = sb("tab_rows", [P, T], U8, "plane")
+        nc.vector.memset(tab_rows[:].bitcast(I32), 0)
         distance = keep.tile([P, P], F32, name="distance")
         nc.gpsimd.iota(distance[:], [[1, P]], base=0, channel_multiplier=-1, allow_small_or_imprecise_dtypes=True)
         ident = keep.tile([P, P], F32, name="ident")
         nc.vector.tensor_scalar(ident[:], distance[:], 0.0, None, ALU.is_equal)
-
-        tab_plane = sb("tab_plane", [P, T], U8, "plane")
-        nc.vector.memset(tab_plane[:].bitcast(I32), 0)
+        limit_rows = keep.tile([P, P], F32, name="limit_rows")
+        nc.scalar.copy(limit_rows[:], distance[:])
 
         def load_list(src, name):
             tile = keep.tile([P, S // 16], U16, name=name)
@@ -102,25 +104,28 @@ def tile_list_eclipse_shed_planner_kernel(
             stored_sb[j] = sb(f"stored{j}", [P, T2], F32, f"rows{j % ROW_BUFS}")
             nc.sync.dma_start(stored_sb[j][:], stored[P * j : P * (j + 1), :])
 
-        scale_rows = sb("scale_rows", [P, T // 4], I32, "h2")
-        for quad in range(QUADS):
-            live = slice(QUAD * quad, QUAD * quad + 4 * PASSES)
-            if quad < QUADS - 1:
-                for a in range(PASSES):
-                    first = QUAD * quad + 4 * a
-                    nc.sync.dma_start(scale_rows[first : first + 4, :], tab_scales[a, 4 * quad : 4 * quad + 4, :].bitcast(I32))
-            else:
-                nc.sync.dma_start(scale_rows[live, :], tab_scales[:, 4 * quad : 4 * quad + 4, :].bitcast(I32))
-            nc.vector.tensor_copy(tab_plane[live, :].bitcast(I32), scale_rows[live, :])
-        words0 = load_table(0)
         idx = load_list(offs, "idx")
         load_w1((0,), ("rawA",))
+        rows = slice(ROWS_AT, ROWS_AT + 16 * PASSES)
+        nc.sync.dma_start(tab_rows[rows, :].bitcast(I32), tab_scales.rearrange("a q t -> (a q) t").bitcast(I32))
         limits = keep.tile([LIMIT_ROWS, P], F32, name="limits")
         nc.sync.dma_start(limits[0:R_TILES, :], lo.rearrange("(j p) -> j p", p=P))
         nc.sync.dma_start(limits[R_TILES : 2 * R_TILES, :], hi.rearrange("(j p) -> j p", p=P))
         nc.sync.dma_start(limits[2 * R_TILES : LIMIT_ROWS, :], gain.rearrange("(j p) -> j p", p=P))
+        words0 = load_table(0)
         words1 = load_table(1)
         idx2 = load_list(offs2, "idx2")
+
+        v_rows = sb("v_rows", [P, S], U8)
+        nc.vector.tensor_copy(v_rows[:], tab_rows[:].indirect(idx[:]))
+        v_plane = sb("v_plane", [P, S], U8)
+        nc.vector.tensor_copy(v_plane[:].bitcast(I32), v_rows[:].bitcast(I32))
+        for a in range(PASSES):
+            for quad in range(QUADS):
+                src, dst = ROWS_AT + 16 * a + 4 * quad, QUAD * quad + PLANE_ROW[a]
+                if src != dst:
+                    nc.scalar.dma_start(v_plane[dst : dst + 4, :].bitcast(I32), v_rows[src : src + 4, :].bitcast(I32))
+
         wgs_sb = sb("wgs_sb", [P, S], F32)
         nc.sync.dma_start(wgs_sb[:], wgs)
         load_w1((1,), ("rawB",))
@@ -170,7 +175,6 @@ def tile_list_eclipse_shed_planner_kernel(
             nc.vector.quantize_mx(out=w1_codes[j][:].bitcast(FP8X4), scales=w1_scales[j][:], in_=w1_rounded[j][:])
 
         v_codes = [sb(f"v_codes{a}", [P, S], U32) for a in range(PASSES)]
-        v_plane = sb("v_plane", [P, S], U8)
         d_acc = {}
 
         def first_product(j):
@@ -184,7 +188,7 @@ def tile_list_eclipse_shed_planner_kernel(
                     lhsT=w1_codes[j][:, P * a : P * (a + 1)].bitcast(FP8X4),
                     lhsT_scale=w1_scales[j][:, P * a : P * (a + 1)],
                     rhs=v_codes[a][:, span].bitcast(FP8X4),
-                    rhs_scale=v_plane[4 * a : P, span],
+                    rhs_scale=v_plane[PLANE_ROW[a] : P, span],
                     start=(a == 0),
                     stop=(a == PASSES - 1),
                 )
@@ -312,7 +316,6 @@ def tile_list_eclipse_shed_planner_kernel(
         nc.vector.tensor_copy(v_codes[0][:], words0[:].bitcast(U32).indirect(idx[:]))
         round_w1(0)
         quantise_w1(0)
-        nc.vector.tensor_copy(v_plane[:], tab_plane[:].indirect(idx[:]))
         for half in range(2):
             listed = idx[:, BANK // 16 * half : BANK // 16 * (half + 1)]
             nc.vector.tensor_copy(v_codes[1][:, BANK * half : BANK * (half + 1)], words1[:].bitcast(U32).indirect(listed))

@@ -21,6 +21,7 @@ QUAD = 32
 QUADS = P // QUAD
 PASSES = 2
 BANK = 512
+HALF = BANK // 2
 R_TILES = H // P
 N_TILES = N // P
 QUARTERS = T2 // BANK
@@ -141,8 +142,9 @@ def tile_list_eclipse_shed_planner_kernel(
         nc.vector.memset(w4_masked[:].bitcast(I32), 0)
         w4_fold_plane = sb("w4_fold_plane", [P, P], U8)
         nc.vector.memset(w4_fold_plane[:].bitcast(I32), 0)
-        outs = [sb("out0", [P, T2], F32)]
-        nc.vector.memset(outs[0][:], 0.0)
+        outs = [sb(f"out{b}", [P, T2], F32) for b in range(2)]
+        for page in outs:
+            nc.vector.memset(page[:], 0.0)
 
         nc.scalar.copy(limit_rows[0:LIMIT_ROWS, :], limits[:])
         turned = bank_tile("turned", [P, P], BACK_BANKS[0])
@@ -260,7 +262,13 @@ def tile_list_eclipse_shed_planner_kernel(
         def quantise_z(a, q):
             if (a, q) == (0, FINAL):
                 z_codes[a, q] = sb("pass0_final", [P, BANK], U32, f"zwfold{q}")[:]
-            nc.vector.quantize_mx(out=z_codes[a, q].bitcast(FP8X4), scales=z_scales[a][:, q, :], in_=z_woven[a, q][:])
+            width = HALF if (a, q) == (0, FINAL) else BANK
+            for c0 in range(0, BANK, width):
+                nc.vector.quantize_mx(
+                    out=z_codes[a, q][:, c0 : c0 + width].bitcast(FP8X4),
+                    scales=z_scales[a][:, q, c0 : c0 + width],
+                    in_=z_woven[a, q][:, 4 * c0 : 4 * (c0 + width)],
+                )
 
         fold_codes = sb("fold_codes", [P, QUARTERS, P], U32)
         fold_scales = sb("fold_scales", [P, QUARTERS, P], U8)
@@ -278,40 +286,41 @@ def tile_list_eclipse_shed_planner_kernel(
         y_sb = {}
         y_acc = {}
 
-        def second_pass(n, q, a, bank=None, stop=False):
+        def second_pass(n, q, a, bank=None, stop=False, c0=0, width=BANK):
             if bank:
-                y_acc[n, q] = bank_tile(f"yacc{n}_{q}", [P, BANK], bank)
+                y_acc[n, q, c0] = bank_tile(f"yacc{n}_{q}_{c0}", [P, width], bank)
             nc.tensor.matmul_mx(
-                out=y_acc[n, q][:],
+                out=y_acc[n, q, c0][:],
                 lhsT=w4_sb[n, a].bitcast(FP4X4),
                 lhsT_scale=w4_plane[:, a, P * n : P * (n + 1)],
-                rhs=z_codes[a, q].bitcast(FP8X4),
-                rhs_scale=z_scales[a][:, q, :],
+                rhs=z_codes[a, q][:, c0 : c0 + width].bitcast(FP8X4),
+                rhs_scale=z_scales[a][:, q, c0 : c0 + width],
                 start=bool(bank),
                 stop=stop,
             )
 
-        def fold_passes(q):
-            for s in range(QUADS):
+        def fold_passes(q, c0=0, width=BANK):
+            groups = range(c0 // P, (c0 + width) // P)
+            for s in groups:
                 nc.tensor.matmul_mx(
-                    out=y_acc[0, q][:, P * s : P * (s + 1)],
+                    out=y_acc[0, q, c0][:, P * s - c0 : P * (s + 1) - c0],
                     lhsT=w4_masked[:, s, :].bitcast(FP4X4),
                     lhsT_scale=w4_fold_plane[:],
                     rhs=fold_codes[:, q, :].bitcast(FP8X4),
                     rhs_scale=fold_scales[:, q, :],
                     start=False,
-                    stop=(s == QUADS - 1 and q < FINAL),
+                    stop=(s == groups[-1] and q < FINAL),
                 )
 
-        def fetch_scores(n, q):
+        def fetch_scores(n, q, c0=0, width=BANK):
             if q == 0:
                 y_sb[n] = sb(f"y{n}", [P, T2], F32, f"rows{(R_TILES + n) % ROW_BUFS}")
-            dst = y_sb[n][:, BANK * q : BANK * (q + 1)]
+            dst = y_sb[n][:, BANK * q + c0 : BANK * q + c0 + width]
             gain_col = cols[:, 2 * R_TILES + n : 2 * R_TILES + n + 1]
             if (n, q) == (0, 1):
-                nc.vector.tensor_scalar(dst, y_acc[n, q][:], gain_col, None, ALU.mult)
+                nc.vector.tensor_scalar(dst, y_acc[n, q, c0][:], gain_col, None, ALU.mult)
             else:
-                nc.scalar.activation(dst, y_acc[n, q][:], COPY, scale=gain_col)
+                nc.scalar.activation(dst, y_acc[n, q, c0][:], COPY, scale=gain_col)
 
         nc.vector.tensor_copy(v_codes[0][:], words0[:].bitcast(U32).indirect(idx[:]))
         round_w1(0)
@@ -421,14 +430,17 @@ def tile_list_eclipse_shed_planner_kernel(
         quantise_z(0, FINAL)
         for q in range(1, FINAL):
             second_pass(0, q, 1)
-        second_pass(0, FINAL, 1, even_banks[FINAL])
-        for q in range(QUARTERS):
+        halves = ((0, even_banks[FINAL]), (HALF, sum_bank(LAST, 0)))
+        for c0, bank in halves:
+            second_pass(0, FINAL, 1, bank, c0=c0, width=HALF)
+        for q in range(FINAL):
             fold_passes(q)
-            if q == FINAL:
-                second_pass(0, q, 0, stop=True)
             fetch_scores(0, q)
-        outs.append(sb("out1", [P, T2], F32, WOVEN_TAGS[FINAL]))
-        nc.vector.memset(outs[1][:], 0.0)
+        for c0, bank in halves:
+            fold_passes(FINAL, c0, HALF)
+        for c0, bank in halves:
+            second_pass(0, FINAL, 0, stop=True, c0=c0, width=HALF)
+            fetch_scores(0, FINAL, c0, HALF)
         for s in range(QUADS):
             columns = slice(P * s, P * (s + 1))
             nc.sync.dma_start(pass1_codes[3 * QUAD : P, :, columns].bitcast(I32), fold_codes[QUAD * s : QUAD * (s + 1), :, :].bitcast(I32))

@@ -35,7 +35,15 @@ LIMIT_ROWS = 2 * R_TILES + N_TILES
 PLANE_ROW = (12, 0)
 ROWS_AT = 12
 
-FIRST_HALF_AT, SECOND_HALF_AT, H1_AT, H2_AT = 0, 2048, 4096, 8192
+LEAD = 512
+FIRST = 256
+LATE = S - 256
+
+WORDS0_AT, OUT_AT = 0, (0, 8192)
+ROWS_TILE_AT = PAGE1_AT = 16384
+FIRST_PART_AT, SECOND_PART_AT, H1_AT, H2_AT = 24576, 25600, 28672, 32768
+RAW_AT = {0: 36864, 1: 40960}
+ROUNDED0_AT = 45056
 H_AT = {1: H1_AT, 2: H2_AT}
 REACH = 16
 W1_CODES_BYTES = 4 * PASSES * P
@@ -44,7 +52,8 @@ PAIRS = (("work0", "work1"), ("work2", "work3"))
 BACK_BANKS = ("back0", "back1")
 SPARE_BANKS = ("spare0", "spare1")
 TURNED_EARLY = {4: (2, 3), 5: (2, 3, 0, 1), 6: (2, 3, 0, 1)}
-WOVEN_TAGS = ("rawA", "rawB", "rawC", "rawD", "h0", "plane", "woven6", "woven7")
+WOVEN_AT = {0: RAW_AT[0], 1: RAW_AT[1]}
+WOVEN_TAGS = {2: "rawC", 3: "rawD", 4: "h0", 5: "woven5", 6: "woven6", 7: "woven7"}
 
 
 def tile_list_eclipse_shed_planner_kernel(
@@ -65,7 +74,7 @@ def tile_list_eclipse_shed_planner_kernel(
         def bank_tile(name, shape, tag):
             return psum.tile(shape, F32, name=name, tag=tag)
 
-        tab_rows = sb("tab_rows", [P, T], U8, "plane")
+        tab_rows = link("tab_rows", [P, T], U8, ROWS_TILE_AT)
         nc.vector.memset(tab_rows[:].bitcast(I32), 0)
         distance = keep.tile([P, P], F32, name="distance")
         nc.gpsimd.iota(distance[:], [[1, P]], base=0, channel_multiplier=-1, allow_small_or_imprecise_dtypes=True)
@@ -79,10 +88,10 @@ def tile_list_eclipse_shed_planner_kernel(
             nc.sync.dma_start(tile[:], src)
             return tile
 
-        def load_table(a):
-            tile = sb(f"words{a}", [P, T], I32, f"wide{a}")
-            nc.sync.dma_start(tile[:], tab_words[a].rearrange("p t i -> p (t i)").bitcast(I32))
-            return tile
+        words = [link("words0", [P, T], I32, WORDS0_AT), sb("words1", [P, T], I32, "wide1")]
+
+        def load_table(a, c0, c1):
+            nc.sync.dma_start(words[a][:, c0:c1], tab_words[a].rearrange("p t i -> p (t i)").bitcast(I32)[:, c0:c1])
 
         w1_raw = {}
 
@@ -91,7 +100,9 @@ def tile_list_eclipse_shed_planner_kernel(
             if len(tags) == 1:
                 both = sb(f"w1raw{tiles[0]}", [P, PASSES, 4, width], F32, tags[0])
             for a in range(PASSES):
-                if len(tags) == 1:
+                if not tags:
+                    raw = link(f"w1raw{tiles[0]}_{a}", [P, 4, width], F32, RAW_AT[tiles[0]] + 16 * width * a)[:]
+                elif len(tags) == 1:
                     raw = both[:, a, :, :]
                 else:
                     raw = sb(f"w1raw{tiles[0]}_{a}", [P, 4, width], F32, tags[a])[:]
@@ -106,16 +117,16 @@ def tile_list_eclipse_shed_planner_kernel(
             nc.sync.dma_start(stored_sb[j][:], stored[P * j : P * (j + 1), :])
 
         idx = load_list(offs, "idx")
-        load_w1((0,), ("rawA",))
+        load_table(0, 0, LEAD)
         rows = slice(ROWS_AT, ROWS_AT + 16 * PASSES)
         nc.sync.dma_start(tab_rows[rows, :].bitcast(I32), tab_scales.rearrange("a q t -> (a q) t").bitcast(I32))
         limits = keep.tile([LIMIT_ROWS, P], F32, name="limits")
         nc.sync.dma_start(limits[0:R_TILES, :], lo.rearrange("(j p) -> j p", p=P))
         nc.sync.dma_start(limits[R_TILES : 2 * R_TILES, :], hi.rearrange("(j p) -> j p", p=P))
         nc.sync.dma_start(limits[2 * R_TILES : LIMIT_ROWS, :], gain.rearrange("(j p) -> j p", p=P))
-        words0 = load_table(0)
-        words1 = load_table(1)
         idx2 = load_list(offs2, "idx2")
+        load_table(0, LEAD, T)
+        load_table(1, 0, T // 2)
 
         v_rows = sb("v_rows", [P, S], U8)
         nc.vector.tensor_copy(v_rows[:], tab_rows[:].indirect(idx[:]))
@@ -125,15 +136,18 @@ def tile_list_eclipse_shed_planner_kernel(
             for quad in range(QUADS):
                 src, dst = ROWS_AT + 16 * a + 4 * quad, QUAD * quad + PLANE_ROW[a]
                 if src != dst:
-                    nc.scalar.dma_start(v_plane[dst : dst + 4, :].bitcast(I32), v_rows[src : src + 4, :].bitcast(I32))
+                    nc.sync.dma_start(v_plane[dst : dst + 4, :].bitcast(I32), v_rows[src : src + 4, :].bitcast(I32))
 
+        load_table(1, T // 2, T)
+        load_w1((0,), ())
         wgs_sb = sb("wgs_sb", [P, S], F32)
-        nc.sync.dma_start(wgs_sb[:], wgs)
-        load_w1((1,), ("rawB",))
+        nc.sync.dma_start(wgs_sb[:, 0:FIRST], wgs[:, 0:FIRST])
+        load_w1((1,), ())
+        nc.sync.dma_start(wgs_sb[:, FIRST:S], wgs[:, FIRST:S])
         load_w1((2, 3), ("rawC", "rawD"))
         load_stored(0)
 
-        pages = [sb(f"page{b}", [P, T2], F32) for b in range(PAGES)]
+        pages = [sb("page0", [P, T2], F32), link("page1", [P, T2], F32, PAGE1_AT)]
         for page in pages:
             nc.vector.memset(page[:], 0.0)
         w4_plane = sb("w4_plane", [P, PASSES, N], U8)
@@ -142,9 +156,6 @@ def tile_list_eclipse_shed_planner_kernel(
         nc.vector.memset(w4_masked[:].bitcast(I32), 0)
         w4_fold_plane = sb("w4_fold_plane", [P, P], U8)
         nc.vector.memset(w4_fold_plane[:].bitcast(I32), 0)
-        outs = [sb(f"out{b}", [P, T2], F32) for b in range(2)]
-        for page in outs:
-            nc.vector.memset(page[:], 0.0)
 
         nc.scalar.copy(limit_rows[0:LIMIT_ROWS, :], limits[:])
         turned = bank_tile("turned", [P, P], BACK_BANKS[0])
@@ -157,10 +168,12 @@ def tile_list_eclipse_shed_planner_kernel(
         w1_scales = {}
 
         def round_w1(j):
-            if j == 4:
-                rounded = link("w1r4", [P, PASSES * P * 4], BF16, H2_AT)
+            if j == 0:
+                rounded = link("w1r0", [P, PASSES * P * 4], BF16, ROUNDED0_AT)
+            elif j == 1:
+                rounded = sb("w1r1", [P, PASSES * P * 4], BF16)
             else:
-                rounded = sb(f"w1r{j}", [P, PASSES * P * 4], BF16, f"w1r{j % 2}")
+                rounded = link(f"w1r{j}", [P, PASSES * P * 4], BF16, H2_AT if j == 4 else RAW_AT[0] + 2048 * (j % 2))
             w1_rounded[j] = rounded
             for a in range(PASSES):
                 nc.scalar.copy(
@@ -168,37 +181,51 @@ def tile_list_eclipse_shed_planner_kernel(
                 )
 
         def quantise_w1(j):
-            if j == 0:
-                w1_codes[j] = sb("w1c0", [P, PASSES * P], U32)
+            if j <= 1:
+                w1_codes[j] = sb(f"w1c{j}", [P, PASSES * P], U32)
             else:
-                at = FIRST_HALF_AT if j == 1 else SECOND_HALF_AT + W1_CODES_BYTES * (j % 2)
-                w1_codes[j] = link(f"w1c{j}", [P, PASSES * P], U32, at)
+                w1_codes[j] = link(f"w1c{j}", [P, PASSES * P], U32, SECOND_PART_AT + W1_CODES_BYTES * (j % 2))
             w1_scales[j] = sb(f"w1s{j}", [P, PASSES * P], U8, f"w1s{j % 2}")
-            nc.vector.quantize_mx(out=w1_codes[j][:].bitcast(FP8X4), scales=w1_scales[j][:], in_=w1_rounded[j][:])
+            if j > 1:
+                nc.vector.quantize_mx(out=w1_codes[j][:].bitcast(FP8X4), scales=w1_scales[j][:], in_=w1_rounded[j][:])
 
-        v_codes = [sb(f"v_codes{a}", [P, S], U32) for a in range(PASSES)]
+        def quantise_pass(j, a):
+            span = slice(P * a, P * (a + 1))
+            nc.vector.quantize_mx(out=w1_codes[j][:, span].bitcast(FP8X4), scales=w1_scales[j][:, span], in_=w1_rounded[j][:, 4 * P * a : 4 * P * (a + 1)])
+
+        v_codes = [sb("v_codes0", [P, S], U32), sb("v_codes1", [P, LATE], U32)]
+        v_late = []
+
+        def table_words(a, c0, c1):
+            return v_late[0][:, c0 - LATE : c1 - LATE] if a == 1 and c0 >= LATE else v_codes[a][:, c0:c1]
+
         d_acc = {}
+
+        def product_part(j, c0, c1, bank, order=(0, 1)):
+            d_acc[j, c0] = bank_tile(f"dacc{j}_{c0}", [P, c1 - c0], bank)
+            steps = []
+            for a in order:
+                steps.extend([(a, c0, LATE), (a, LATE, c1)] if a == 1 and c0 < LATE < c1 else [(a, c0, c1)])
+            for step in steps:
+                a, lo_col, hi_col = step
+                nc.tensor.matmul_mx(
+                    out=d_acc[j, c0][:, lo_col - c0 : hi_col - c0],
+                    lhsT=w1_codes[j][:, P * a : P * (a + 1)].bitcast(FP8X4),
+                    lhsT_scale=w1_scales[j][:, P * a : P * (a + 1)],
+                    rhs=table_words(a, lo_col, hi_col).bitcast(FP8X4),
+                    rhs_scale=v_plane[PLANE_ROW[a] : P, lo_col:hi_col],
+                    start=(step == steps[0]),
+                    stop=(step == steps[-1]),
+                )
 
         def first_product(j):
             for half in range(2):
-                d_acc[j, half] = bank_tile(f"dacc{j}_{half}", [P, BANK], PAIRS[j % 2][half])
-            by_half = [(half, a) for half in range(2) for a in range(PASSES)]
-            for half, a in sorted(by_half, key=lambda step: step[1]) if j == 0 else by_half:
-                span = slice(BANK * half, BANK * (half + 1))
-                nc.tensor.matmul_mx(
-                    out=d_acc[j, half][:],
-                    lhsT=w1_codes[j][:, P * a : P * (a + 1)].bitcast(FP8X4),
-                    lhsT_scale=w1_scales[j][:, P * a : P * (a + 1)],
-                    rhs=v_codes[a][:, span].bitcast(FP8X4),
-                    rhs_scale=v_plane[PLANE_ROW[a] : P, span],
-                    start=(a == 0),
-                    stop=(a == PASSES - 1),
-                )
+                product_part(j, BANK * half, BANK * (half + 1), PAIRS[j % 2][half])
 
         def fetch_product(j, tag):
             d_sb = sb(f"d{j}", [P, S], F32, tag)
             for half in range(2):
-                nc.scalar.copy(d_sb[:, BANK * half : BANK * (half + 1)], d_acc[j, half][:])
+                nc.scalar.copy(d_sb[:, BANK * half : BANK * (half + 1)], d_acc[j, BANK * half][:])
             return d_sb
 
         def clamp(j, dst, src):
@@ -249,7 +276,11 @@ def tile_list_eclipse_shed_planner_kernel(
         def turn_back(a, q, banks):
             first = 3 * QUAD * (1 - a)
             pairs = z_turned[q][:].rearrange("t s u p e -> t (s u p e)").bitcast(F32).rearrange("t (s u p) -> t s u p", s=4, u=2)
-            woven = sb(f"zw{a}_{q}", [P, 4 * BANK], BF16, WOVEN_TAGS[QUARTERS * a + q])
+            place = QUARTERS * a + q
+            if place in WOVEN_AT:
+                woven = link(f"zw{a}_{q}", [P, 4 * BANK], BF16, WOVEN_AT[place])
+            else:
+                woven = sb(f"zw{a}_{q}", [P, 4 * BANK], BF16, WOVEN_TAGS[place])
             for half in range(2):
                 bank = bank_tile(f"back{a}_{q}_{half}", [P, 2, 2 * P], banks[half])
                 for s in range(2):
@@ -322,27 +353,38 @@ def tile_list_eclipse_shed_planner_kernel(
             else:
                 nc.scalar.activation(dst, y_acc[n, q, c0][:], COPY, scale=gain_col)
 
-        nc.vector.tensor_copy(v_codes[0][:], words0[:].bitcast(U32).indirect(idx[:]))
+        nc.vector.tensor_copy(v_codes[0][:], words[0][:].bitcast(U32).indirect(idx[:]))
+        outs = [link(f"out{b}", [P, T2], F32, OUT_AT[b]) for b in range(2)]
+        for page in outs:
+            nc.vector.memset(page[:], 0.0)
+        nc.vector.tensor_copy(v_codes[1][:], words[1][:].bitcast(U32).indirect(idx[:, 0 : LATE // 16]))
         round_w1(0)
         quantise_w1(0)
-        for half in range(2):
-            listed = idx[:, BANK // 16 * half : BANK // 16 * (half + 1)]
-            nc.vector.tensor_copy(v_codes[1][:, BANK * half : BANK * (half + 1)], words1[:].bitcast(U32).indirect(listed))
+        for a in range(PASSES):
+            quantise_pass(0, a)
+        v_late.append(link("v_late", [P, S - LATE], U32, ROUNDED0_AT))
+        nc.vector.tensor_copy(v_late[0][:], words[1][:].bitcast(U32).indirect(idx[:, LATE // 16 : S // 16]))
 
-        first_product(0)
-        h_first = link("h0a", [P, BANK + REACH], F32, FIRST_HALF_AT)
-        clamp(0, h_first[:, 0:BANK], d_acc[0, 0][:])
-        scatter_page(0, h_first[:, 0:BANK], 0, BANK)
+        product_part(0, 0, FIRST, PAIRS[0][0])
+        product_part(0, FIRST, LATE, PAIRS[0][1], (1, 0))
+        product_part(0, LATE, S, SPARE_BANKS[0], (1, 0))
+        h_first = link("h0a", [P, FIRST + REACH], F32, FIRST_PART_AT)
+        clamp(0, h_first[:, 0:FIRST], d_acc[0, 0][:])
+        d_second = link("d0b", [P, S - FIRST], F32, RAW_AT[0])
+        nc.scalar.copy(d_second[:, 0 : LATE - FIRST], d_acc[0, FIRST][:])
+        nc.scalar.copy(d_second[:, LATE - FIRST : S - FIRST], d_acc[0, LATE][:])
         round_w1(1)
-        d_second = sb("d0b", [P, BANK], F32, "rawB")
-        nc.scalar.copy(d_second[:], d_acc[0, 1][:])
-        h_second = link("h0b", [P, BANK + REACH], F32, SECOND_HALF_AT)
-        clamp(0, h_second[:, 0:BANK], d_second[:])
         quantise_w1(1)
-        scatter_page(0, h_second[:, 0:BANK], BANK, S)
+        quantise_pass(1, 0)
+        scatter_page(0, h_first[:, 0:FIRST], 0, FIRST)
+        quantise_pass(1, 1)
+        h_second = link("h0b", [P, S - FIRST + REACH], F32, SECOND_PART_AT)
+        clamp(0, h_second[:, 0 : S - FIRST], d_second[:])
+        scatter_page(0, h_second[:, 0 : S - FIRST], FIRST, S)
 
         load_w1((4, 5, 6, 7), ("wide1",))
         load_stored(1)
+        load_stored(2)
         for n in range(N_TILES):
             passes = 1 if n == 0 else PASSES
             tile = sb(f"w4_sb{n}", [P, passes, 2 * P], U8)
@@ -360,7 +402,6 @@ def tile_list_eclipse_shed_planner_kernel(
             nc.sync.dma_start(w4_masked[lanes, quad, :].bitcast(I32), w4_words[1, 3 * QUAD : P, 0 : 2 * P].bitcast(I32))
             nc.sync.dma_start(w4_fold_plane[live, :].bitcast(I32), w4_scales[1, 12:16, 0:P].bitcast(I32))
         nc.sync.dma_start(w4_masked[0 : 3 * QUAD, QUADS, :].bitcast(I32), w4_words[1, 0 : 3 * QUAD, 0 : 2 * P].bitcast(I32))
-        load_stored(2)
         idx3 = load_list(offs3, "idx3")
         idx4 = load_list(offs4, "idx4")
 
@@ -370,7 +411,7 @@ def tile_list_eclipse_shed_planner_kernel(
         clamp_product(1, fetch_product(1, "rawC"))
         quantise_w1(2)
         quantise_w1(3)
-        duty_sb = sb("duty_sb", [P, N_TILES, PICK], F32, "wide0")
+        duty_sb = sb("duty_sb", [P, N_TILES, PICK], F32)
         nc.sync.dma_start(duty_sb[:], duty.rearrange("(n p) m -> p n m", p=P))
         wgo_sb = sb("wgo_sb", [P, PICK], F32)
         nc.sync.dma_start(wgo_sb[:], wgo)

@@ -32,20 +32,18 @@ ROW_BUFS = 3
 H_BUFS = 3
 LIMIT_ROWS = 2 * R_TILES + N_TILES
 
-PLANE_ROW = (12, 0)
-ROWS_AT = 12
+PLANE_ROW = (0, 4)
+ROWS_AT = 3 * QUAD
+MOVES_AHEAD = 3
 
-LEAD = 512
 FIRST = 256
 LATE = S - 256
 
-WORDS0_AT, OUT_AT = 0, (0, 8192)
+WORDS0_AT = 0
 ROWS_TILE_AT = PAGE1_AT = 16384
-FIRST_PART_AT, SECOND_PART_AT, H1_AT, H2_AT = 24576, 25600, 28672, 32768
+SECOND_PART_AT, W1_CODES_AT, H2_AT = 25600, 28672, 32768
 RAW_AT = {0: 36864, 1: 40960}
 ROUNDED0_AT = 45056
-H_AT = {1: H1_AT, 2: H2_AT}
-REACH = 16
 W1_CODES_BYTES = 4 * PASSES * P
 
 PAIRS = (("work0", "work1"), ("work2", "work3"))
@@ -75,7 +73,7 @@ def tile_list_eclipse_shed_planner_kernel(
             return psum.tile(shape, F32, name=name, tag=tag)
 
         tab_rows = link("tab_rows", [P, T], U8, ROWS_TILE_AT)
-        nc.vector.memset(tab_rows[:].bitcast(I32), 0)
+        nc.vector.memset(tab_rows[0:ROWS_AT, :].bitcast(I32), 0)
         distance = keep.tile([P, P], F32, name="distance")
         nc.gpsimd.iota(distance[:], [[1, P]], base=0, channel_multiplier=-1, allow_small_or_imprecise_dtypes=True)
         ident = keep.tile([P, P], F32, name="ident")
@@ -100,9 +98,7 @@ def tile_list_eclipse_shed_planner_kernel(
             if len(tags) == 1:
                 both = sb(f"w1raw{tiles[0]}", [P, PASSES, 4, width], F32, tags[0])
             for a in range(PASSES):
-                if not tags:
-                    raw = link(f"w1raw{tiles[0]}_{a}", [P, 4, width], F32, RAW_AT[tiles[0]] + 16 * width * a)[:]
-                elif len(tags) == 1:
+                if len(tags) == 1:
                     raw = both[:, a, :, :]
                 else:
                     raw = sb(f"w1raw{tiles[0]}_{a}", [P, 4, width], F32, tags[a])[:]
@@ -110,39 +106,48 @@ def tile_list_eclipse_shed_planner_kernel(
                 for place, j in enumerate(tiles):
                     w1_raw[j, a] = raw[:, :, P * place : P * (place + 1)]
 
+        def load_w1_pass(j, a):
+            w1_raw[j, a] = link(f"w1raw{j}_{a}", [P, 4, P], F32, RAW_AT[j] + 16 * P * a)[:]
+            nc.sync.dma_start(w1_raw[j, a], w1[512 * a : 512 * (a + 1), P * j : P * (j + 1)].rearrange("(p i) c -> p i c", i=4))
+
         stored_sb = {}
 
         def load_stored(j):
             stored_sb[j] = sb(f"stored{j}", [P, T2], F32, f"rows{j % ROW_BUFS}")
             nc.sync.dma_start(stored_sb[j][:], stored[P * j : P * (j + 1), :])
 
+        nc.sync.dma_start(tab_rows[ROWS_AT:P, :].bitcast(I32), tab_scales.rearrange("a q t -> (a q) t").bitcast(I32))
         idx = load_list(offs, "idx")
-        load_table(0, 0, LEAD)
-        rows = slice(ROWS_AT, ROWS_AT + 16 * PASSES)
-        nc.sync.dma_start(tab_rows[rows, :].bitcast(I32), tab_scales.rearrange("a q t -> (a q) t").bitcast(I32))
         limits = keep.tile([LIMIT_ROWS, P], F32, name="limits")
         nc.sync.dma_start(limits[0:R_TILES, :], lo.rearrange("(j p) -> j p", p=P))
         nc.sync.dma_start(limits[R_TILES : 2 * R_TILES, :], hi.rearrange("(j p) -> j p", p=P))
+        load_table(0, 0, T)
         nc.sync.dma_start(limits[2 * R_TILES : LIMIT_ROWS, :], gain.rearrange("(j p) -> j p", p=P))
         idx2 = load_list(offs2, "idx2")
-        load_table(0, LEAD, T)
         load_table(1, 0, T // 2)
 
+        v_plane = sb("v_plane", [P, S], U8)
+        nc.vector.memset(v_plane[:].bitcast(I32), 0)
+        w4_plane = sb("w4_plane", [P, PASSES, N], U8)
+        nc.vector.memset(w4_plane[:].bitcast(I32), 0)
+        w4_masked = sb("w4_masked", [P, QUADS + 1, 2 * P], U8)
+        nc.vector.memset(w4_masked[:].bitcast(I32), 0)
+        w4_fold_plane = sb("w4_fold_plane", [P, P], U8)
+        nc.vector.memset(w4_fold_plane[:].bitcast(I32), 0)
         v_rows = sb("v_rows", [P, S], U8)
         nc.vector.tensor_copy(v_rows[:], tab_rows[:].indirect(idx[:]))
-        v_plane = sb("v_plane", [P, S], U8)
-        nc.vector.tensor_copy(v_plane[:].bitcast(I32), v_rows[:].bitcast(I32))
-        for a in range(PASSES):
-            for quad in range(QUADS):
-                src, dst = ROWS_AT + 16 * a + 4 * quad, QUAD * quad + PLANE_ROW[a]
-                if src != dst:
-                    nc.sync.dma_start(v_plane[dst : dst + 4, :].bitcast(I32), v_rows[src : src + 4, :].bitcast(I32))
+        for move in range(PASSES * QUADS):
+            if move == MOVES_AHEAD:
+                load_table(1, T // 2, T)
+            src, dst = ROWS_AT + 4 * move, QUAD * (move % QUADS) + PLANE_ROW[move // QUADS]
+            nc.sync.dma_start(v_plane[dst : dst + 4, :].bitcast(I32), v_rows[src : src + 4, :].bitcast(I32))
 
-        load_table(1, T // 2, T)
-        load_w1((0,), ())
+        for a in range(PASSES):
+            load_w1_pass(0, a)
         wgs_sb = sb("wgs_sb", [P, S], F32)
+        load_w1_pass(1, 0)
         nc.sync.dma_start(wgs_sb[:, 0:FIRST], wgs[:, 0:FIRST])
-        load_w1((1,), ())
+        load_w1_pass(1, 1)
         nc.sync.dma_start(wgs_sb[:, FIRST:S], wgs[:, FIRST:S])
         load_w1((2, 3), ("rawC", "rawD"))
         load_stored(0)
@@ -150,12 +155,9 @@ def tile_list_eclipse_shed_planner_kernel(
         pages = [sb("page0", [P, T2], F32), link("page1", [P, T2], F32, PAGE1_AT)]
         for page in pages:
             nc.vector.memset(page[:], 0.0)
-        w4_plane = sb("w4_plane", [P, PASSES, N], U8)
-        nc.vector.memset(w4_plane[:].bitcast(I32), 0)
-        w4_masked = sb("w4_masked", [P, QUADS + 1, 2 * P], U8)
-        nc.vector.memset(w4_masked[:].bitcast(I32), 0)
-        w4_fold_plane = sb("w4_fold_plane", [P, P], U8)
-        nc.vector.memset(w4_fold_plane[:].bitcast(I32), 0)
+        outs = [sb(f"out{b}", [P, T2], F32) for b in range(2)]
+        for page in outs:
+            nc.vector.memset(page[:], 0.0)
 
         nc.scalar.copy(limit_rows[0:LIMIT_ROWS, :], limits[:])
         turned = bank_tile("turned", [P, P], BACK_BANKS[0])
@@ -170,28 +172,28 @@ def tile_list_eclipse_shed_planner_kernel(
         def round_w1(j):
             if j == 0:
                 rounded = link("w1r0", [P, PASSES * P * 4], BF16, ROUNDED0_AT)
-            elif j == 1:
-                rounded = sb("w1r1", [P, PASSES * P * 4], BF16)
             else:
                 rounded = link(f"w1r{j}", [P, PASSES * P * 4], BF16, H2_AT if j == 4 else RAW_AT[0] + 2048 * (j % 2))
             w1_rounded[j] = rounded
             for a in range(PASSES):
-                nc.scalar.copy(
-                    rounded[:, 4 * P * a : 4 * P * (a + 1)].rearrange("p (c i) -> p c i", i=4), w1_raw[j, a].rearrange("p i c -> p c i")
-                )
+                round_pass(j, a, rounded[:, 4 * P * a : 4 * P * (a + 1)])
+
+        def round_pass(j, a, dst):
+            w1_rounded[j, a] = dst
+            nc.scalar.copy(dst.rearrange("p (c i) -> p c i", i=4), w1_raw[j, a].rearrange("p i c -> p c i"))
 
         def quantise_w1(j):
             if j <= 1:
                 w1_codes[j] = sb(f"w1c{j}", [P, PASSES * P], U32)
             else:
-                w1_codes[j] = link(f"w1c{j}", [P, PASSES * P], U32, SECOND_PART_AT + W1_CODES_BYTES * (j % 2))
+                w1_codes[j] = link(f"w1c{j}", [P, PASSES * P], U32, W1_CODES_AT + W1_CODES_BYTES * (j % 2))
             w1_scales[j] = sb(f"w1s{j}", [P, PASSES * P], U8, f"w1s{j % 2}")
             if j > 1:
                 nc.vector.quantize_mx(out=w1_codes[j][:].bitcast(FP8X4), scales=w1_scales[j][:], in_=w1_rounded[j][:])
 
         def quantise_pass(j, a):
             span = slice(P * a, P * (a + 1))
-            nc.vector.quantize_mx(out=w1_codes[j][:, span].bitcast(FP8X4), scales=w1_scales[j][:, span], in_=w1_rounded[j][:, 4 * P * a : 4 * P * (a + 1)])
+            nc.vector.quantize_mx(out=w1_codes[j][:, span].bitcast(FP8X4), scales=w1_scales[j][:, span], in_=w1_rounded[j, a])
 
         v_codes = [sb("v_codes0", [P, S], U32), sb("v_codes1", [P, LATE], U32)]
         v_late = []
@@ -234,7 +236,7 @@ def tile_list_eclipse_shed_planner_kernel(
         h_sb = {}
 
         def clamp_product(j, d_sb):
-            h_sb[j] = link(f"h{j}", [P, S], F32, H_AT[j])[:] if j in H_AT else d_sb[:]
+            h_sb[j] = link(f"h{j}", [P, S], F32, H2_AT)[:] if j == 2 else d_sb[:]
             clamp(j, h_sb[j], d_sb[:])
 
         def scatter_page(j, h, c0, c1):
@@ -354,9 +356,6 @@ def tile_list_eclipse_shed_planner_kernel(
                 nc.scalar.activation(dst, y_acc[n, q, c0][:], COPY, scale=gain_col)
 
         nc.vector.tensor_copy(v_codes[0][:], words[0][:].bitcast(U32).indirect(idx[:]))
-        outs = [link(f"out{b}", [P, T2], F32, OUT_AT[b]) for b in range(2)]
-        for page in outs:
-            nc.vector.memset(page[:], 0.0)
         nc.vector.tensor_copy(v_codes[1][:], words[1][:].bitcast(U32).indirect(idx[:, 0 : LATE // 16]))
         round_w1(0)
         quantise_w1(0)
@@ -368,19 +367,20 @@ def tile_list_eclipse_shed_planner_kernel(
         product_part(0, 0, FIRST, PAIRS[0][0])
         product_part(0, FIRST, LATE, PAIRS[0][1], (1, 0))
         product_part(0, LATE, S, SPARE_BANKS[0], (1, 0))
-        h_first = link("h0a", [P, FIRST + REACH], F32, FIRST_PART_AT)
-        clamp(0, h_first[:, 0:FIRST], d_acc[0, 0][:])
+        h_first = sb("h_first", [P, FIRST], F32)
+        clamp(0, h_first[:], d_acc[0, 0][:])
+        round_pass(1, 0, link("w1r1_0", [P, 4 * P], BF16, SECOND_PART_AT)[:])
         d_second = link("d0b", [P, S - FIRST], F32, RAW_AT[0])
         nc.scalar.copy(d_second[:, 0 : LATE - FIRST], d_acc[0, FIRST][:])
         nc.scalar.copy(d_second[:, LATE - FIRST : S - FIRST], d_acc[0, LATE][:])
-        round_w1(1)
+        round_pass(1, 1, sb("w1r1_1", [P, 4 * P], BF16)[:])
         quantise_w1(1)
         quantise_pass(1, 0)
-        scatter_page(0, h_first[:, 0:FIRST], 0, FIRST)
+        scatter_page(0, h_first[:], 0, FIRST)
+        h_second = link("h0b", [P, S - FIRST], F32, SECOND_PART_AT)
+        clamp(0, h_second[:], d_second[:])
         quantise_pass(1, 1)
-        h_second = link("h0b", [P, S - FIRST + REACH], F32, SECOND_PART_AT)
-        clamp(0, h_second[:, 0 : S - FIRST], d_second[:])
-        scatter_page(0, h_second[:, 0 : S - FIRST], FIRST, S)
+        scatter_page(0, h_second[:], FIRST, S)
 
         load_w1((4, 5, 6, 7), ("wide1",))
         load_stored(1)
@@ -411,7 +411,7 @@ def tile_list_eclipse_shed_planner_kernel(
         clamp_product(1, fetch_product(1, "rawC"))
         quantise_w1(2)
         quantise_w1(3)
-        duty_sb = sb("duty_sb", [P, N_TILES, PICK], F32)
+        duty_sb = link("duty_sb", [P, N_TILES, PICK], F32, WORDS0_AT)
         nc.sync.dma_start(duty_sb[:], duty.rearrange("(n p) m -> p n m", p=P))
         wgo_sb = sb("wgo_sb", [P, PICK], F32)
         nc.sync.dma_start(wgo_sb[:], wgo)

@@ -30,11 +30,11 @@ FINAL = QUARTERS - 1
 PAGES = 2
 ROW_BUFS = 3
 H_BUFS = 3
-LIMIT_ROWS = 2 * R_TILES + N_TILES
+LIMIT_ROWS = 2 * R_TILES
 
-PLANE_ROW = (0, 4)
+PLANE_ROW = (12, 0)
 ROWS_AT = 3 * QUAD
-MOVES_AHEAD = 3
+MOVES_AHEAD = 2
 
 FIRST = 256
 LATE = S - 256
@@ -120,14 +120,13 @@ def tile_list_eclipse_shed_planner_kernel(
         idx = load_list(offs, "idx")
         limits = keep.tile([LIMIT_ROWS, P], F32, name="limits")
         nc.sync.dma_start(limits[0:R_TILES, :], lo.rearrange("(j p) -> j p", p=P))
-        nc.sync.dma_start(limits[R_TILES : 2 * R_TILES, :], hi.rearrange("(j p) -> j p", p=P))
-        load_table(0, 0, T)
-        nc.sync.dma_start(limits[2 * R_TILES : LIMIT_ROWS, :], gain.rearrange("(j p) -> j p", p=P))
+        nc.sync.dma_start(limits[R_TILES:LIMIT_ROWS, :], hi.rearrange("(j p) -> j p", p=P))
         idx2 = load_list(offs2, "idx2")
+        load_table(0, 0, T)
         load_table(1, 0, T // 2)
 
         v_plane = sb("v_plane", [P, S], U8)
-        nc.vector.memset(v_plane[:].bitcast(I32), 0)
+        nc.vector.memset(v_plane[0:ROWS_AT, :].bitcast(I32), 0)
         w4_plane = sb("w4_plane", [P, PASSES, N], U8)
         nc.vector.memset(w4_plane[:].bitcast(I32), 0)
         w4_masked = sb("w4_masked", [P, QUADS + 1, 2 * P], U8)
@@ -136,18 +135,19 @@ def tile_list_eclipse_shed_planner_kernel(
         nc.vector.memset(w4_fold_plane[:].bitcast(I32), 0)
         v_rows = sb("v_rows", [P, S], U8)
         nc.vector.tensor_copy(v_rows[:], tab_rows[:].indirect(idx[:]))
-        for move in range(PASSES * QUADS):
-            if move == MOVES_AHEAD:
+        nc.vector.tensor_copy(v_plane[ROWS_AT:P, :].bitcast(I32), v_rows[ROWS_AT:P, :].bitcast(I32))
+        moves = [(ROWS_AT + 16 * a + 4 * quad, QUAD * quad + PLANE_ROW[a]) for a in range(PASSES) for quad in range(QUADS)]
+        for place, (src, dst) in enumerate([move for move in moves if move[0] != move[1]]):
+            if place == MOVES_AHEAD:
                 load_table(1, T // 2, T)
-            src, dst = ROWS_AT + 4 * move, QUAD * (move % QUADS) + PLANE_ROW[move // QUADS]
+                for a in range(PASSES):
+                    load_w1_pass(0, a)
             nc.sync.dma_start(v_plane[dst : dst + 4, :].bitcast(I32), v_rows[src : src + 4, :].bitcast(I32))
 
-        for a in range(PASSES):
-            load_w1_pass(0, a)
         wgs_sb = sb("wgs_sb", [P, S], F32)
-        load_w1_pass(1, 0)
         nc.sync.dma_start(wgs_sb[:, 0:FIRST], wgs[:, 0:FIRST])
-        load_w1_pass(1, 1)
+        for a in range(PASSES):
+            load_w1_pass(1, a)
         nc.sync.dma_start(wgs_sb[:, FIRST:S], wgs[:, FIRST:S])
         load_w1((2, 3), ("rawC", "rawD"))
         load_stored(0)
@@ -349,7 +349,7 @@ def tile_list_eclipse_shed_planner_kernel(
             if q == 0:
                 y_sb[n] = sb(f"y{n}", [P, T2], F32, f"rows{(R_TILES + n) % ROW_BUFS}")
             dst = y_sb[n][:, BANK * q + c0 : BANK * q + c0 + width]
-            gain_col = cols[:, 2 * R_TILES + n : 2 * R_TILES + n + 1]
+            gain_col = gain_sb[:, n : n + 1]
             if (n, q) == (0, 1):
                 nc.vector.tensor_scalar(dst, y_acc[n, q, c0][:], gain_col, None, ALU.mult)
             else:
@@ -369,14 +369,14 @@ def tile_list_eclipse_shed_planner_kernel(
         product_part(0, LATE, S, SPARE_BANKS[0], (1, 0))
         h_first = sb("h_first", [P, FIRST], F32)
         clamp(0, h_first[:], d_acc[0, 0][:])
-        round_pass(1, 0, link("w1r1_0", [P, 4 * P], BF16, SECOND_PART_AT)[:])
+        round_pass(1, 0, sb("w1r1_0", [P, 4 * P], BF16)[:])
         d_second = link("d0b", [P, S - FIRST], F32, RAW_AT[0])
         nc.scalar.copy(d_second[:, 0 : LATE - FIRST], d_acc[0, FIRST][:])
         nc.scalar.copy(d_second[:, LATE - FIRST : S - FIRST], d_acc[0, LATE][:])
         round_pass(1, 1, sb("w1r1_1", [P, 4 * P], BF16)[:])
         quantise_w1(1)
-        quantise_pass(1, 0)
         scatter_page(0, h_first[:], 0, FIRST)
+        quantise_pass(1, 0)
         h_second = link("h0b", [P, S - FIRST], F32, SECOND_PART_AT)
         clamp(0, h_second[:], d_second[:])
         quantise_pass(1, 1)
@@ -402,6 +402,9 @@ def tile_list_eclipse_shed_planner_kernel(
             nc.sync.dma_start(w4_masked[lanes, quad, :].bitcast(I32), w4_words[1, 3 * QUAD : P, 0 : 2 * P].bitcast(I32))
             nc.sync.dma_start(w4_fold_plane[live, :].bitcast(I32), w4_scales[1, 12:16, 0:P].bitcast(I32))
         nc.sync.dma_start(w4_masked[0 : 3 * QUAD, QUADS, :].bitcast(I32), w4_words[1, 0 : 3 * QUAD, 0 : 2 * P].bitcast(I32))
+        gain_sb = keep.tile([P, N_TILES], F32, name="gain_sb")
+        with nc.allow_non_contiguous_dma(reason="one value of gain for each partition and score tile"):
+            nc.sync.dma_start(gain_sb[:], gain.rearrange("(n p) -> p n", p=P))
         idx3 = load_list(offs3, "idx3")
         idx4 = load_list(offs4, "idx4")
 

@@ -145,9 +145,9 @@ def tile_list_eclipse_shed_planner_kernel(
             nc.sync.dma_start(v_plane[dst : dst + 4, :].bitcast(I32), v_rows[src : src + 4, :].bitcast(I32))
 
         wgs_sb = sb("wgs_sb", [P, S], F32)
+        load_w1_pass(1, 0)
         nc.sync.dma_start(wgs_sb[:, 0:FIRST], wgs[:, 0:FIRST])
-        for a in range(PASSES):
-            load_w1_pass(1, a)
+        load_w1_pass(1, 1)
         nc.sync.dma_start(wgs_sb[:, FIRST:S], wgs[:, FIRST:S])
         load_w1((2, 3), ("rawC", "rawD"))
         load_stored(0)
@@ -369,14 +369,14 @@ def tile_list_eclipse_shed_planner_kernel(
         product_part(0, LATE, S, SPARE_BANKS[0], (1, 0))
         h_first = sb("h_first", [P, FIRST], F32)
         clamp(0, h_first[:], d_acc[0, 0][:])
-        round_pass(1, 0, sb("w1r1_0", [P, 4 * P], BF16)[:])
+        round_pass(1, 0, link("w1r1_0", [P, 4 * P], BF16, SECOND_PART_AT)[:])
         d_second = link("d0b", [P, S - FIRST], F32, RAW_AT[0])
         nc.scalar.copy(d_second[:, 0 : LATE - FIRST], d_acc[0, FIRST][:])
         nc.scalar.copy(d_second[:, LATE - FIRST : S - FIRST], d_acc[0, LATE][:])
         round_pass(1, 1, sb("w1r1_1", [P, 4 * P], BF16)[:])
         quantise_w1(1)
-        scatter_page(0, h_first[:], 0, FIRST)
         quantise_pass(1, 0)
+        scatter_page(0, h_first[:], 0, FIRST)
         h_second = link("h0b", [P, S - FIRST], F32, SECOND_PART_AT)
         clamp(0, h_second[:], d_second[:])
         quantise_pass(1, 1)

@@ -34,7 +34,7 @@ LIMIT_ROWS = 2 * R_TILES
 
 PLANE_ROW = (12, 0)
 ROWS_AT = 3 * QUAD
-MOVES_AHEAD = 2
+MOVES_AHEAD = 3
 
 FIRST = 256
 LATE = S - 256

@@ -42,8 +42,12 @@ LATE = S - 256
 WORDS0_AT = 0
 ROWS_TILE_AT = PAGE1_AT = 16384
 SECOND_PART_AT, W1_CODES_AT, H2_AT = 25600, 28672, 32768
-RAW_AT = {0: 36864, 1: 40960}
-ROUNDED0_AT = 45056
+RAW_AT = {0: 38912, 1: 43008}
+ROUNDED0_AT = 47104
+W1_CODES3_AT = 36352
+ROUNDED_AT = {2: RAW_AT[0], 3: RAW_AT[0] + 2048, 4: 34816, 5: 36864, 6: RAW_AT[0], 7: 36864}
+TURNED_AT, TURNED_BYTES = 49152, 4 * 2 * LAST * QUAD * 2 * 2
+RAW45_AT = tuple(TURNED_AT + TURNED_BYTES * (2 * a + 1) - 2048 for a in range(PASSES))
 W1_CODES_BYTES = 4 * PASSES * P
 
 PAIRS = (("work0", "work1"), ("work2", "work3"))
@@ -93,18 +97,11 @@ def tile_list_eclipse_shed_planner_kernel(
 
         w1_raw = {}
 
-        def load_w1(tiles, tags):
-            c0, width = P * tiles[0], P * len(tiles)
-            if len(tags) == 1:
-                both = sb(f"w1raw{tiles[0]}", [P, PASSES, 4, width], F32, tags[0])
+        def load_w1(first, raws):
             for a in range(PASSES):
-                if len(tags) == 1:
-                    raw = both[:, a, :, :]
-                else:
-                    raw = sb(f"w1raw{tiles[0]}_{a}", [P, 4, width], F32, tags[a])[:]
-                nc.sync.dma_start(raw, w1[512 * a : 512 * (a + 1), c0 : c0 + width].rearrange("(p i) c -> p i c", i=4))
-                for place, j in enumerate(tiles):
-                    w1_raw[j, a] = raw[:, :, P * place : P * (place + 1)]
+                nc.sync.dma_start(raws[a], w1[512 * a : 512 * (a + 1), P * first : P * (first + 2)].rearrange("(p i) c -> p i c", i=4))
+                for place in range(2):
+                    w1_raw[first + place, a] = raws[a][:, :, P * place : P * (place + 1)]
 
         def load_w1_pass(j, a):
             w1_raw[j, a] = link(f"w1raw{j}_{a}", [P, 4, P], F32, RAW_AT[j] + 16 * P * a)[:]
@@ -149,7 +146,7 @@ def tile_list_eclipse_shed_planner_kernel(
         nc.sync.dma_start(wgs_sb[:, 0:FIRST], wgs[:, 0:FIRST])
         load_w1_pass(1, 1)
         nc.sync.dma_start(wgs_sb[:, FIRST:S], wgs[:, FIRST:S])
-        load_w1((2, 3), ("rawC", "rawD"))
+        load_w1(2, [sb(f"w1raw2_{a}", [P, 4, 2 * P], F32, ("rawC", "rawD")[a])[:] for a in range(PASSES)])
         load_stored(0)
 
         pages = [sb("page0", [P, T2], F32), link("page1", [P, T2], F32, PAGE1_AT)]
@@ -173,7 +170,7 @@ def tile_list_eclipse_shed_planner_kernel(
             if j == 0:
                 rounded = link("w1r0", [P, PASSES * P * 4], BF16, ROUNDED0_AT)
             else:
-                rounded = link(f"w1r{j}", [P, PASSES * P * 4], BF16, H2_AT if j == 4 else RAW_AT[0] + 2048 * (j % 2))
+                rounded = link(f"w1r{j}", [P, PASSES * P * 4], BF16, ROUNDED_AT[j])
             w1_rounded[j] = rounded
             for a in range(PASSES):
                 round_pass(j, a, rounded[:, 4 * P * a : 4 * P * (a + 1)])
@@ -185,6 +182,8 @@ def tile_list_eclipse_shed_planner_kernel(
         def quantise_w1(j):
             if j <= 1:
                 w1_codes[j] = sb(f"w1c{j}", [P, PASSES * P], U32)
+            elif j == 3:
+                w1_codes[j] = link(f"w1c{j}", [P, PASSES * P], U32, W1_CODES3_AT)
             else:
                 w1_codes[j] = link(f"w1c{j}", [P, PASSES * P], U32, W1_CODES_AT + W1_CODES_BYTES * (j % 2))
             w1_scales[j] = sb(f"w1s{j}", [P, PASSES * P], U8, f"w1s{j % 2}")
@@ -254,7 +253,7 @@ def tile_list_eclipse_shed_planner_kernel(
                 t0 = BANK * q + P * s
                 nc.tensor.matmul(sums[j, q][:, s, :], stored_sb[j][:, t0 : t0 + P], ident[:], start=(s == 0), stop=False, is_transpose=True)
 
-        z_turned = [sb(f"zt{q}", [P, 4, 2, LAST * QUAD, 2], BF16) for q in range(QUARTERS)]
+        z_turned = [link(f"zt{q}", [P, 4, 2, LAST * QUAD, 2], BF16, TURNED_AT + TURNED_BYTES * q) for q in range(QUARTERS)]
         z_folded = {}
 
         def add_page(j, q):
@@ -382,7 +381,9 @@ def tile_list_eclipse_shed_planner_kernel(
         quantise_pass(1, 1)
         scatter_page(0, h_second[:], FIRST, S)
 
-        load_w1((4, 5, 6, 7), ("wide1",))
+        load_w1(4, [link(f"w1raw4_{a}", [P, 4, 2 * P], F32, RAW45_AT[a])[:] for a in range(PASSES)])
+        last_pair = sb("w1raw6", [P, PASSES, 4, 2 * P], F32, "wide1")
+        load_w1(6, [last_pair[:, a, :, :] for a in range(PASSES)])
         load_stored(1)
         load_stored(2)
         for n in range(N_TILES):
@@ -422,12 +423,12 @@ def tile_list_eclipse_shed_planner_kernel(
         for j in range(1, LAST):
             scatter_page(j, h_sb[j], 0, S)
             if j == 1:
-                round_w1(4)
-                round_w1(5)
                 fetched = []
                 for ahead in (2, 3):
                     first_product(ahead)
                     fetched.append(fetch_product(ahead, f"h{ahead % H_BUFS}"))
+                round_w1(4)
+                round_w1(5)
                 quantise_w1(4)
                 quantise_w1(5)
                 clamp_product(2, fetched[0])

from contextlib import ExitStack

import concourse.mybir as mybir

K, H, N, T, S, T2, PICK = 1024, 1024, 512, 4096, 1024, 2048, 1024
FLOPS = 2 * K * H * S + 2 * H * N * T2

F32 = mybir.dt.float32
BF16 = mybir.dt.bfloat16
I32 = mybir.dt.int32
U32 = mybir.dt.uint32
U16 = mybir.dt.uint16
U8 = mybir.dt.uint8
FP8X4 = mybir.dt.float8_e4m3fn_x4
FP4X4 = mybir.dt.float4_e2m1fn_x4
ALU = mybir.AluOpType
COPY = mybir.ActivationFunctionType.Copy

P = 128
QUAD = 32
QUADS = P // QUAD
PASSES = 2
BANK = 512
HALF = BANK // 2
R_TILES = H // P
N_TILES = N // P
QUARTERS = T2 // BANK
LAST = R_TILES - 1
FINAL = QUARTERS - 1
PAGES = 2
ROW_BUFS = 3
H_BUFS = 3
LIMIT_ROWS = 2 * R_TILES

PLANE_ROW = (12, 0)
ROWS_AT = 3 * QUAD
MOVES_AHEAD = 3

FIRST = 256
LATE = S - 256

WORDS0_AT = 0
ROWS_TILE_AT = PAGE1_AT = 16384
SECOND_PART_AT, W1_CODES_AT, H2_AT = 25600, 28672, 32768
RAW_AT = {0: 38912, 1: 43008}
ROUNDED0_AT = 47104
W1_CODES3_AT = 36352
ROUNDED_AT = {2: RAW_AT[0], 3: RAW_AT[0] + 2048, 4: 34816, 5: 36864, 6: RAW_AT[0], 7: 36864}
TURNED_AT, TURNED_BYTES = 49152, 4 * 2 * LAST * QUAD * 2 * 2
RAW45_AT = tuple(TURNED_AT + TURNED_BYTES * (2 * a + 1) - 2048 for a in range(PASSES))
W1_CODES_BYTES = 4 * PASSES * P

PAIRS = (("work0", "work1"), ("work2", "work3"))
BACK_BANKS = ("back0", "back1")
SPARE_BANKS = ("spare0", "spare1")
TURNED_EARLY = {4: (2, 3), 5: (2, 3, 0, 1), 6: (2, 3, 0, 1)}
WOVEN_AT = {0: RAW_AT[0], 1: RAW_AT[1]}
WOVEN_TAGS = {2: "rawC", 3: "rawD", 4: "h0", 5: "woven5", 6: "woven6", 7: "woven7"}


def tile_list_eclipse_shed_planner_kernel(
    tc, tab_words, tab_scales, offs, w1, lo, hi, offs2, wgs, stored, w4_words, w4_scales, offs3, gain, duty, offs4, wgo, out
):
    nc = tc.nc
    with ExitStack() as ctx:
        keep = ctx.enter_context(tc.tile_pool(name="keep", bufs=1))
        chain = ctx.enter_context(tc.tile_pool(name="chain", bufs=1))
        psum = ctx.enter_context(tc.psum_pool(name="psum", bufs=1))

        def sb(name, shape, dtype, tag=None):
            return keep.tile(shape, dtype, name=name, tag=tag or name, align_bytes=64)

        def link(name, shape, dtype, offset):
            return chain.tile(shape, dtype, name=name, align_bytes=64, offset=offset)

        def bank_tile(name, shape, tag):
            return psum.tile(shape, F32, name=name, tag=tag)

        tab_rows = link("tab_rows", [P, T], U8, ROWS_TILE_AT)
        nc.vector.memset(tab_rows[0:ROWS_AT, :].bitcast(I32), 0)
        distance = keep.tile([P, P], F32, name="distance")
        nc.gpsimd.iota(distance[:], [[1, P]], base=0, channel_multiplier=-1, allow_small_or_imprecise_dtypes=True)
        ident = keep.tile([P, P], F32, name="ident")
        nc.vector.tensor_scalar(ident[:], distance[:], 0.0, None, ALU.is_equal)
        limit_rows = keep.tile([P, P], F32, name="limit_rows")
        nc.scalar.copy(limit_rows[:], distance[:])

        def load_list(src, name):
            tile = keep.tile([P, S // 16], U16, name=name)
            nc.sync.dma_start(tile[:], src)
            return tile

        words = [link("words0", [P, T], I32, WORDS0_AT), sb("words1", [P, T], I32, "wide1")]

        def load_table(a, c0, c1):
            nc.sync.dma_start(words[a][:, c0:c1], tab_words[a].rearrange("p t i -> p (t i)").bitcast(I32)[:, c0:c1])

        w1_raw = {}

        def load_w1(first, raws):
            for a in range(PASSES):
                nc.sync.dma_start(raws[a], w1[512 * a : 512 * (a + 1), P * first : P * (first + 2)].rearrange("(p i) c -> p i c", i=4))
                for place in range(2):
                    w1_raw[first + place, a] = raws[a][:, :, P * place : P * (place + 1)]

        def load_w1_pass(j, a):
            w1_raw[j, a] = link(f"w1raw{j}_{a}", [P, 4, P], F32, RAW_AT[j] + 16 * P * a)[:]
            nc.sync.dma_start(w1_raw[j, a], w1[512 * a : 512 * (a + 1), P * j : P * (j + 1)].rearrange("(p i) c -> p i c", i=4))

        stored_sb = {}

        def load_stored(j):
            stored_sb[j] = sb(f"stored{j}", [P, T2], F32, f"rows{j % ROW_BUFS}")
            nc.sync.dma_start(stored_sb[j][:], stored[P * j : P * (j + 1), :])

        nc.sync.dma_start(tab_rows[ROWS_AT:P, :].bitcast(I32), tab_scales.rearrange("a q t -> (a q) t").bitcast(I32))
        idx = load_list(offs, "idx")
        limits = keep.tile([LIMIT_ROWS, P], F32, name="limits")
        nc.sync.dma_start(limits[0:R_TILES, :], lo.rearrange("(j p) -> j p", p=P))
        nc.sync.dma_start(limits[R_TILES:LIMIT_ROWS, :], hi.rearrange("(j p) -> j p", p=P))
        idx2 = load_list(offs2, "idx2")
        load_table(0, 0, T)
        load_table(1, 0, T // 2)

        v_plane = sb("v_plane", [P, S], U8)
        nc.vector.memset(v_plane[0:ROWS_AT, :].bitcast(I32), 0)
        w4_plane = sb("w4_plane", [P, PASSES, N], U8)
        nc.vector.memset(w4_plane[:].bitcast(I32), 0)
        w4_masked = sb("w4_masked", [P, QUADS + 1, 2 * P], U8)
        nc.vector.memset(w4_masked[:].bitcast(I32), 0)
        w4_fold_plane = sb("w4_fold_plane", [P, P], U8)
        nc.vector.memset(w4_fold_plane[:].bitcast(I32), 0)
        v_rows = sb("v_rows", [P, S], U8)
        nc.vector.tensor_copy(v_rows[:], tab_rows[:].indirect(idx[:]))
        nc.vector.tensor_copy(v_plane[ROWS_AT:P, :].bitcast(I32), v_rows[ROWS_AT:P, :].bitcast(I32))
        moves = [(ROWS_AT + 16 * a + 4 * quad, QUAD * quad + PLANE_ROW[a]) for a in range(PASSES) for quad in range(QUADS)]
        for place, (src, dst) in enumerate([move for move in moves if move[0] != move[1]]):
            if place == MOVES_AHEAD:
                load_table(1, T // 2, T)
                for a in range(PASSES):
                    load_w1_pass(0, a)
            nc.sync.dma_start(v_plane[dst : dst + 4, :].bitcast(I32), v_rows[src : src + 4, :].bitcast(I32))

        wgs_sb = sb("wgs_sb", [P, S], F32)
        load_w1_pass(1, 0)
        nc.sync.dma_start(wgs_sb[:, 0:FIRST], wgs[:, 0:FIRST])
        load_w1_pass(1, 1)
        nc.sync.dma_start(wgs_sb[:, FIRST:S], wgs[:, FIRST:S])
        load_w1(2, [sb(f"w1raw2_{a}", [P, 4, 2 * P], F32, ("rawC", "rawD")[a])[:] for a in range(PASSES)])
        load_stored(0)

        pages = [sb("page0", [P, T2], F32), link("page1", [P, T2], F32, PAGE1_AT)]
        for page in pages:
            nc.vector.memset(page[:], 0.0)
        outs = [sb(f"out{b}", [P, T2], F32) for b in range(2)]
        for page in outs:
            nc.vector.memset(page[:], 0.0)

        nc.scalar.copy(limit_rows[0:LIMIT_ROWS, :], limits[:])
        turned = bank_tile("turned", [P, P], BACK_BANKS[0])
        nc.tensor.transpose(turned[:], limit_rows[:], ident[:])
        cols = keep.tile([P, LIMIT_ROWS], F32, name="cols")
        nc.scalar.copy(cols[:], turned[:, 0:LIMIT_ROWS])

        w1_rounded = {}
        w1_codes = {}
        w1_scales = {}

        def round_w1(j):
            if j == 0:
                rounded = link("w1r0", [P, PASSES * P * 4], BF16, ROUNDED0_AT)
            else:
                rounded = link(f"w1r{j}", [P, PASSES * P * 4], BF16, ROUNDED_AT[j])
            w1_rounded[j] = rounded
            for a in range(PASSES):
                round_pass(j, a, rounded[:, 4 * P * a : 4 * P * (a + 1)])

        def round_pass(j, a, dst):
            w1_rounded[j, a] = dst
            nc.scalar.copy(dst.rearrange("p (c i) -> p c i", i=4), w1_raw[j, a].rearrange("p i c -> p c i"))

        def quantise_w1(j):
            if j <= 1:
                w1_codes[j] = sb(f"w1c{j}", [P, PASSES * P], U32)
            elif j == 3:
                w1_codes[j] = link(f"w1c{j}", [P, PASSES * P], U32, W1_CODES3_AT)
            else:
                w1_codes[j] = link(f"w1c{j}", [P, PASSES * P], U32, W1_CODES_AT + W1_CODES_BYTES * (j % 2))
            w1_scales[j] = sb(f"w1s{j}", [P, PASSES * P], U8, f"w1s{j % 2}")
            if j > 1:
                nc.vector.quantize_mx(out=w1_codes[j][:].bitcast(FP8X4), scales=w1_scales[j][:], in_=w1_rounded[j][:])

        def quantise_pass(j, a):
            span = slice(P * a, P * (a + 1))
            nc.vector.quantize_mx(out=w1_codes[j][:, span].bitcast(FP8X4), scales=w1_scales[j][:, span], in_=w1_rounded[j, a])

        v_codes = [sb("v_codes0", [P, S], U32), sb("v_codes1", [P, LATE], U32)]
        v_late = []

        def table_words(a, c0, c1):
            return v_late[0][:, c0 - LATE : c1 - LATE] if a == 1 and c0 >= LATE else v_codes[a][:, c0:c1]

        d_acc = {}

        def product_part(j, c0, c1, bank, order=(0, 1)):
            d_acc[j, c0] = bank_tile(f"dacc{j}_{c0}", [P, c1 - c0], bank)
            steps = []
            for a in order:
                steps.extend([(a, c0, LATE), (a, LATE, c1)] if a == 1 and c0 < LATE < c1 else [(a, c0, c1)])
            for step in steps:
                a, lo_col, hi_col = step
                nc.tensor.matmul_mx(
                    out=d_acc[j, c0][:, lo_col - c0 : hi_col - c0],
                    lhsT=w1_codes[j][:, P * a : P * (a + 1)].bitcast(FP8X4),
                    lhsT_scale=w1_scales[j][:, P * a : P * (a + 1)],
                    rhs=table_words(a, lo_col, hi_col).bitcast(FP8X4),
                    rhs_scale=v_plane[PLANE_ROW[a] : P, lo_col:hi_col],
                    start=(step == steps[0]),
                    stop=(step == steps[-1]),
                )

        def first_product(j):
            for half in range(2):
                product_part(j, BANK * half, BANK * (half + 1), PAIRS[j % 2][half])

        def fetch_product(j, tag):
            d_sb = sb(f"d{j}", [P, S], F32, tag)
            for half in range(2):
                nc.scalar.copy(d_sb[:, BANK * half : BANK * (half + 1)], d_acc[j, BANK * half][:])
            return d_sb

        def clamp(j, dst, src):
            nc.vector.tensor_scalar(dst, src, cols[:, j : j + 1], cols[:, R_TILES + j : R_TILES + j + 1], ALU.max, ALU.min)

        h_sb = {}

        def clamp_product(j, d_sb):
            h_sb[j] = link(f"h{j}", [P, S], F32, H2_AT)[:] if j == 2 else d_sb[:]
            clamp(j, h_sb[j], d_sb[:])

        def scatter_page(j, h, c0, c1):
            window = pages[j % PAGES][:].indirect(idx2[:, c0 // 16 : c1 // 16])
            nc.vector.tensor_tensor(window, h, wgs_sb[:, c0:c1], ALU.mult)

        sums = {}

        def sum_bank(j, q):
            return PAIRS[(j + 1 + q // 2) % 2][q % 2]

        def turn_stored(j, q):
            sums[j, q] = bank_tile(f"sum{j}_{q}", [P, 4, P], sum_bank(j, q))
            for s in range(4):
                t0 = BANK * q + P * s
                nc.tensor.matmul(sums[j, q][:, s, :], stored_sb[j][:, t0 : t0 + P], ident[:], start=(s == 0), stop=False, is_transpose=True)

        z_turned = [link(f"zt{q}", [P, 4, 2, LAST * QUAD, 2], BF16, TURNED_AT + TURNED_BYTES * q) for q in range(QUARTERS)]
        z_folded = {}

        def add_page(j, q):
            bank = sums[j, q]
            for s in range(4):
                t0 = BANK * q + P * s
                nc.tensor.matmul(bank[:, s, :], pages[j % PAGES][:, t0 : t0 + P], ident[:], start=False, stop=(s == 3), is_transpose=True)
            if j < LAST:
                place = (j + 3) % LAST
                dst = z_turned[q][:, :, :, QUAD * place : QUAD * (place + 1), :]
                nc.scalar.copy(dst, bank[:].rearrange("t s (p u e) -> t s u p e", u=2, e=2))
            else:
                z_folded[q] = sb(f"zfold{q}", [P, 2, 4, QUAD, 2], BF16)
                nc.scalar.copy(z_folded[q][:], bank[:].rearrange("t s (p u e) -> t u s p e", u=2, e=2))

        pass1_codes = sb("pass1_codes", [P, QUARTERS, BANK], U32)
        z_codes = {(1, q): pass1_codes[:, q, :] for q in range(QUARTERS)}
        z_scales = [sb(f"z_scales{a}", [P, QUARTERS, BANK], U8) for a in range(PASSES)]
        z_woven = {}

        def turn_back(a, q, banks):
            first = 3 * QUAD * (1 - a)
            pairs = z_turned[q][:].rearrange("t s u p e -> t (s u p e)").bitcast(F32).rearrange("t (s u p) -> t s u p", s=4, u=2)
            place = QUARTERS * a + q
            if place in WOVEN_AT:
                woven = link(f"zw{a}_{q}", [P, 4 * BANK], BF16, WOVEN_AT[place])
            else:
                woven = sb(f"zw{a}_{q}", [P, 4 * BANK], BF16, WOVEN_TAGS[place])
            for half in range(2):
                bank = bank_tile(f"back{a}_{q}_{half}", [P, 2, 2 * P], banks[half])
                for s in range(2):
                    for u in range(2):
                        nc.tensor.transpose(bank[:, u, P * s : P * (s + 1)], pairs[:, 2 * half + s, u, first : first + P], ident[:])
                words = woven[:, 2 * BANK * half : 2 * BANK * (half + 1)].bitcast(F32)
                nc.scalar.copy(words.rearrange("p (t u) -> p t u", u=2), bank[:].rearrange("p u t -> p t u"))
            z_woven[a, q] = woven

        def quantise_z(a, q):
            if (a, q) == (0, FINAL):
                z_codes[a, q] = sb("pass0_final", [P, BANK], U32, f"zwfold{q}")[:]
            width = HALF if (a, q) == (0, FINAL) else BANK
            for c0 in range(0, BANK, width):
                nc.vector.quantize_mx(
                    out=z_codes[a, q][:, c0 : c0 + width].bitcast(FP8X4),
                    scales=z_scales[a][:, q, c0 : c0 + width],
                    in_=z_woven[a, q][:, 4 * c0 : 4 * (c0 + width)],
                )

        fold_codes = sb("fold_codes", [P, QUARTERS, P], U32)
        fold_scales = sb("fold_scales", [P, QUARTERS, P], U8)

        def finish_fold(q):
            pairs = z_folded[q][:].rearrange("t u s p e -> t (u s p e)").bitcast(F32).rearrange("t (u c) -> t u c", u=2)
            bank = bank_tile(f"backfold{q}", [P, 2, P], sum_bank(LAST, q))
            for u in range(2):
                nc.tensor.transpose(bank[:, u, :], pairs[:, u, :], ident[:])
            woven = sb(f"zwfold{q}", [P, 4 * P], BF16)
            nc.scalar.copy(woven[:].bitcast(F32).rearrange("p (t u) -> p t u", u=2), bank[:].rearrange("p u t -> p t u"))
            nc.vector.quantize_mx(out=fold_codes[:, q, :].bitcast(FP8X4), scales=fold_scales[:, q, :], in_=woven[:])

        w4_sb = {}
        y_sb = {}
        y_acc = {}

        def second_pass(n, q, a, bank=None, stop=False, c0=0, width=BANK):
            if bank:
                y_acc[n, q, c0] = bank_tile(f"yacc{n}_{q}_{c0}", [P, width], bank)
            nc.tensor.matmul_mx(
                out=y_acc[n, q, c0][:],
                lhsT=w4_sb[n, a].bitcast(FP4X4),
                lhsT_scale=w4_plane[:, a, P * n : P * (n + 1)],
                rhs=z_codes[a, q][:, c0 : c0 + width].bitcast(FP8X4),
                rhs_scale=z_scales[a][:, q, c0 : c0 + width],
                start=bool(bank),
                stop=stop,
            )

        def fold_passes(q, c0=0, width=BANK):
            groups = range(c0 // P, (c0 + width) // P)
            for s in groups:
                nc.tensor.matmul_mx(
                    out=y_acc[0, q, c0][:, P * s - c0 : P * (s + 1) - c0],
                    lhsT=w4_masked[:, s, :].bitcast(FP4X4),
                    lhsT_scale=w4_fold_plane[:],
                    rhs=fold_codes[:, q, :].bitcast(FP8X4),
                    rhs_scale=fold_scales[:, q, :],
                    start=False,
                    stop=(s == groups[-1] and q < FINAL),
                )

        def fetch_scores(n, q, c0=0, width=BANK):
            if q == 0:
                y_sb[n] = sb(f"y{n}", [P, T2], F32, f"rows{(R_TILES + n) % ROW_BUFS}")
            dst = y_sb[n][:, BANK * q + c0 : BANK * q + c0 + width]
            gain_col = gain_sb[:, n : n + 1]
            if (n, q) == (0, 1):
                nc.vector.tensor_scalar(dst, y_acc[n, q, c0][:], gain_col, None, ALU.mult)
            else:
                nc.scalar.activation(dst, y_acc[n, q, c0][:], COPY, scale=gain_col)

        nc.vector.tensor_copy(v_codes[0][:], words[0][:].bitcast(U32).indirect(idx[:]))
        nc.vector.tensor_copy(v_codes[1][:], words[1][:].bitcast(U32).indirect(idx[:, 0 : LATE // 16]))
        round_w1(0)
        quantise_w1(0)
        for a in range(PASSES):
            quantise_pass(0, a)
        v_late.append(link("v_late", [P, S - LATE], U32, ROUNDED0_AT))
        nc.vector.tensor_copy(v_late[0][:], words[1][:].bitcast(U32).indirect(idx[:, LATE // 16 : S // 16]))

        product_part(0, 0, FIRST, PAIRS[0][0])
        product_part(0, FIRST, LATE, PAIRS[0][1], (1, 0))
        product_part(0, LATE, S, SPARE_BANKS[0], (1, 0))
        h_first = sb("h_first", [P, FIRST], F32)
        clamp(0, h_first[:], d_acc[0, 0][:])
        round_pass(1, 0, link("w1r1_0", [P, 4 * P], BF16, SECOND_PART_AT)[:])
        d_second = link("d0b", [P, S - FIRST], F32, RAW_AT[0])
        nc.scalar.copy(d_second[:, 0 : LATE - FIRST], d_acc[0, FIRST][:])
        nc.scalar.copy(d_second[:, LATE - FIRST : S - FIRST], d_acc[0, LATE][:])
        round_pass(1, 1, sb("w1r1_1", [P, 4 * P], BF16)[:])
        quantise_w1(1)
        quantise_pass(1, 0)
        scatter_page(0, h_first[:], 0, FIRST)
        h_second = link("h0b", [P, S - FIRST], F32, SECOND_PART_AT)
        clamp(0, h_second[:], d_second[:])
        quantise_pass(1, 1)
        scatter_page(0, h_second[:], FIRST, S)

        load_w1(4, [link(f"w1raw4_{a}", [P, 4, 2 * P], F32, RAW45_AT[a])[:] for a in range(PASSES)])
        last_pair = sb("w1raw6", [P, PASSES, 4, 2 * P], F32, "wide1")
        load_w1(6, [last_pair[:, a, :, :] for a in range(PASSES)])
        load_stored(1)
        load_stored(2)
        for n in range(N_TILES):
            passes = 1 if n == 0 else PASSES
            tile = sb(f"w4_sb{n}", [P, passes, 2 * P], U8)
            columns = w4_words[0:passes, :, 2 * P * n : 2 * P * (n + 1)]
            nc.sync.dma_start(tile[:].bitcast(I32), columns.rearrange("a p c -> p a c").bitcast(I32))
            for a in range(passes):
                w4_sb[n, a] = tile[:, a, :]
        w4_sb[0, 1] = w4_masked[:, QUADS, :]
        for quad in range(QUADS):
            lanes = slice(QUAD * quad, QUAD * (quad + 1))
            live = slice(QUAD * quad, QUAD * quad + 4)
            nc.sync.dma_start(
                w4_plane[live, :, :].bitcast(I32), w4_scales[:, 4 * quad : 4 * quad + 4, :].rearrange("a r c -> r a c").bitcast(I32)
            )
            nc.sync.dma_start(w4_masked[lanes, quad, :].bitcast(I32), w4_words[1, 3 * QUAD : P, 0 : 2 * P].bitcast(I32))
            nc.sync.dma_start(w4_fold_plane[live, :].bitcast(I32), w4_scales[1, 12:16, 0:P].bitcast(I32))
        nc.sync.dma_start(w4_masked[0 : 3 * QUAD, QUADS, :].bitcast(I32), w4_words[1, 0 : 3 * QUAD, 0 : 2 * P].bitcast(I32))
        gain_sb = keep.tile([P, N_TILES], F32, name="gain_sb")
        with nc.allow_non_contiguous_dma(reason="one value of gain for each partition and score tile"):
            nc.sync.dma_start(gain_sb[:], gain.rearrange("(n p) -> p n", p=P))
        idx3 = load_list(offs3, "idx3")
        idx4 = load_list(offs4, "idx4")

        first_product(1)
        round_w1(2)
        round_w1(3)
        clamp_product(1, fetch_product(1, "rawC"))
        quantise_w1(2)
        quantise_w1(3)
        duty_sb = link("duty_sb", [P, N_TILES, PICK], F32, WORDS0_AT)
        nc.sync.dma_start(duty_sb[:], duty.rearrange("(n p) m -> p n m", p=P))
        wgo_sb = sb("wgo_sb", [P, PICK], F32)
        nc.sync.dma_start(wgo_sb[:], wgo)

        for j in range(1, LAST):
            scatter_page(j, h_sb[j], 0, S)
            if j == 1:
                fetched = []
                for ahead in (2, 3):
                    first_product(ahead)
                    fetched.append(fetch_product(ahead, f"h{ahead % H_BUFS}"))
                round_w1(4)
                round_w1(5)
                quantise_w1(4)
                quantise_w1(5)
                clamp_product(2, fetched[0])
                clamp_product(3, fetched[1])
            elif j + 2 <= LAST:
                if j + 4 <= LAST:
                    round_w1(j + 4)
                first_product(j + 2)
                clamp_product(j + 2, fetch_product(j + 2, f"h{(j + 2) % H_BUFS}"))
                if j + 4 <= LAST:
                    quantise_w1(j + 4)
            if j >= 5:
                turn_back(0, 2 * (j - 5), BACK_BANKS)
                turn_back(0, 2 * (j - 5) + 1, SPARE_BANKS)
            for q in range(QUARTERS):
                if (j - 1, q) not in sums:
                    turn_stored(j - 1, q)
                add_page(j - 1, q)
            if j + 2 <= LAST:
                load_stored(j + 2)
            for q in TURNED_EARLY.get(j, ()):
                turn_stored(j, q)

        scatter_page(LAST, h_sb[LAST], 0, S)
        for q in range(QUARTERS):
            add_page(LAST - 1, q)
        pass0_codes = sb("pass0_codes", [P, FINAL, BANK], U32, f"page{(LAST - 1) % PAGES}")
        for q in range(FINAL):
            z_codes[0, q] = pass0_codes[:, q, :]
            quantise_z(0, q)
        for q in range(QUARTERS):
            turn_back(1, q, (BACK_BANKS, SPARE_BANKS)[q % 2])
            quantise_z(1, q)
            turn_stored(LAST, (q + 2) % QUARTERS)

        even_banks = BACK_BANKS + SPARE_BANKS
        for q in range(QUARTERS):
            add_page(LAST, q)
        for q in range(FINAL):
            second_pass(0, q, 0, even_banks[q])
        second_pass(0, 0, 1)
        for q in range(QUARTERS):
            finish_fold(q)
        quantise_z(0, FINAL)
        for q in range(1, FINAL):
            second_pass(0, q, 1)
        halves = ((0, even_banks[FINAL]), (HALF, sum_bank(LAST, 0)))
        for c0, bank in halves:
            second_pass(0, FINAL, 1, bank, c0=c0, width=HALF)
        for q in range(FINAL):
            fold_passes(q)
            fetch_scores(0, q)
        for c0, bank in halves:
            fold_passes(FINAL, c0, HALF)
        for c0, bank in halves:
            second_pass(0, FINAL, 0, stop=True, c0=c0, width=HALF)
            fetch_scores(0, FINAL, c0, HALF)
        for s in range(QUADS):
            columns = slice(P * s, P * (s + 1))
            nc.sync.dma_start(pass1_codes[3 * QUAD : P, :, columns].bitcast(I32), fold_codes[QUAD * s : QUAD * (s + 1), :, :].bitcast(I32))
            nc.sync.dma_start(
                z_scales[1][3 * QUAD : 3 * QUAD + 4, :, columns].bitcast(I32), fold_scales[QUAD * s : QUAD * s + 4, :, :].bitcast(I32)
            )

        x_sb = {}

        def pick(n, tag):
            x_sb[n] = sb(f"x{n}", [P, PICK], F32, tag)
            nc.vector.tensor_tensor(x_sb[n][:], y_sb[n][:].indirect(idx3[:]), duty_sb[:, n, :], ALU.add)

        pick(0, "h0")
        for n in range(1, N_TILES):
            banks = PAIRS[0] + PAIRS[1] if n % 2 == 1 else even_banks
            for q in range(QUARTERS):
                second_pass(n, q, 1, banks[q])
                second_pass(n, q, 0, stop=True)
                fetch_scores(n, q)
        for n in range(N_TILES):
            if n == 1:
                pick(1, "w4_sb2")
            if 1 <= n < N_TILES - 1:
                pick(n + 1, f"h{n}")
            page = outs[n % 2]
            nc.vector.tensor_tensor(page[:].indirect(idx4[:]), x_sb[n][:], wgo_sb[:], ALU.mult)
            nc.sync.dma_start(out[P * n : P * (n + 1), :], page[:])
